import numpy as np
import ml_dtypes


def mxq(x, axis, fmt="e4m3"):
    dtype, down = {"e4m3": (ml_dtypes.float8_e4m3fn, 7), "e5m2": (ml_dtypes.float8_e5m2, 14)}[fmt]
    v = np.moveaxis(np.asarray(x, np.float32).astype(ml_dtypes.bfloat16).astype(np.float64), axis, -1)
    blocks = v.reshape(v.shape[:-1] + (-1, 32))
    amax = np.abs(blocks).max(-1, keepdims=True)
    byte = np.maximum(np.where(amax > 0, np.frexp(amax)[1] - 1 + 127, 0) - down, 1)
    scale = np.exp2(byte - 127.0)
    codes = (blocks / scale).astype(np.float32).astype(dtype).astype(np.float64)
    return np.moveaxis((codes * scale).reshape(v.shape), -1, axis)


WIDE = False


def mx_kscale(k):
    if not WIDE:
        return np.ones(k)
    levels = np.array([10, -10, 5, -5, 0])
    if k % 512:
        return np.exp2(np.random.permutation(np.resize(levels, k // 32))).repeat(32)
    a = np.empty((k // 512, 16))
    for p in range(k // 512):
        a[p, :8] = np.random.permutation(np.resize(levels, 8))
        for g in range(8):
            far = levels[np.abs(levels - a[p, g]) >= 10]
            a[p, g + 8] = far[np.random.randint(len(far))]
    return np.exp2(a.ravel()).repeat(32)


BF16 = ml_dtypes.bfloat16


def bf(x):
    return np.asarray(x, np.float32).astype(BF16)


def f64(x):
    return np.asarray(x).astype(np.float64)


E2M1 = np.array([0.0, 0.5, 1.0, 1.5, 2.0, 3.0, 4.0, 6.0, -0.0, -0.5, -1.0, -1.5, -2.0, -3.0, -4.0, -6.0])


def pack_weight(w, fmt):
    k, n = w.shape
    w = f64(bf(w)).reshape(k // 32, 32, n)
    amax = np.abs(w).max(1)
    if fmt == "e4m3":
        byte = np.frexp(amax)[1] - 1 + 127 - 7
    else:
        mant, ex = np.frexp(amax / 6.0)
        byte = np.where(mant > 0.5, ex, ex - 1) + 127
    byte = np.clip(np.where(amax > 0, byte, 1), 1, 254)
    scaled = (w * np.exp2(127.0 - byte)[:, None, :]).reshape(k, n).astype(np.float32)
    by_word = np.ascontiguousarray(scaled.reshape(k // 512, 128, 4, n).transpose(0, 1, 3, 2))
    if fmt == "e4m3":
        words = by_word.astype(ml_dtypes.float8_e4m3fn).view(np.uint8)
    else:
        c = by_word.astype(ml_dtypes.float4_e2m1fn).view(np.uint8) & 0xF
        words = c[..., 0::2] | (c[..., 1::2] << 4)
    return np.ascontiguousarray(words), np.ascontiguousarray(byte.astype(np.uint8).reshape(k // 512, 16, n))


def unpack_weight(words, scales, fmt):
    g, p, n, _ = words.shape
    if fmt == "e4m3":
        vals = np.ascontiguousarray(words).view(ml_dtypes.float8_e4m3fn).astype(np.float64)
    else:
        nib = np.empty((g, p, n, 4), np.uint8)
        nib[..., 0::2] = words & 0xF
        nib[..., 1::2] = words >> 4
        vals = E2M1[nib]
    vals = vals * np.repeat(np.exp2(scales.astype(np.float64) - 127.0), 8, axis=1)[..., None]
    return vals.transpose(0, 1, 3, 2).reshape(g * 512, n)
def pack4(w):
    words, scales = pack_weight(w, "e2m1")
    return words.reshape(words.shape[0], 128, -1), scales


def unpack4(words, scales):
    return unpack_weight(words.reshape(words.shape[0], 128, -1, 2), scales, "e2m1")


M, T, S, K, N, R, L = 2048, 8, 256, 1536, 1024, 512, 256


def draw0():
    s = mx_kscale(K)
    c = mx_kscale(N)
    u = mx_kscale(M)
    proj = np.random.standard_normal((N, R)) / np.sqrt(N) / c[:, None]
    proj_words, proj_scales = pack4(proj)
    return {"x": bf(np.random.standard_normal((M, K)) * s),
            "w": bf(np.random.standard_normal((K, N)) / np.sqrt(K) / s[:, None] * c),
            "time_pos": bf(0.5 * np.random.standard_normal((T, N)) * c),
            "space_pos": bf(0.5 * np.random.standard_normal((S, N)) * c),
            "gain": bf((1 + 0.1 * np.random.standard_normal(M)) * u),
            "proj_words": proj_words,
            "proj_scales": proj_scales,
            "pool": bf(np.random.standard_normal((L, M)) / np.sqrt(M) / u)}


def core(x, w, time_pos, space_pos, gain, proj_words, proj_scales, pool):
    e = mxq(f64(x), 1, "e4m3") @ mxq(f64(w), 0, "e4m3")
    z = e.reshape(T, S, N) + f64(time_pos)[:, None, :] + f64(space_pos)[None, :, :]
    h = z.reshape(M, N) * f64(gain)[:, None]
    feats = mxq(h, 1, "e4m3") @ unpack4(proj_words, proj_scales)
    latents = mxq(f64(pool), 1, "e4m3") @ mxq(h, 0, "e4m3")
    return feats, latents


def e4m3fn_bytes(y):
    return np.clip(np.asarray(y, np.float64), -448.0, 448.0).astype(np.float32).astype(ml_dtypes.float8_e4m3fn).view(np.uint8)


def e4m3fn_values(b):
    return np.asarray(b, np.uint8).view(ml_dtypes.float8_e4m3fn).astype(np.float64)


def setup_inputs():
    d = draw0()
    x0 = np.asarray(d['x']).astype(np.float64)
    s = (np.max(np.abs(x0), axis=(0,), keepdims=True) / 448.0).astype(np.float32)
    out = {}
    for k, v in d.items():
        if k == 'x':
            out['x_bytes'] = e4m3fn_bytes(x0 / s.astype(np.float64))
            out['x_scale'] = s
        else:
            out[k] = v
    return out


def reference(x_bytes, x_scale, w, time_pos, space_pos, gain, proj_words, proj_scales, pool):
    return core(e4m3fn_values(x_bytes) * x_scale.astype(np.float64), w, time_pos, space_pos, gain, proj_words, proj_scales, pool)

@@ -1,0 +1,435 @@
+from contextlib import ExitStack
+
+import concourse.mybir as mybir
+from concourse.masks import make_identity
+
+M, T, K, N, R, L = 2048, 8, 1536, 1024, 512, 256
+FLOPS = 2 * (M * K * N + M * N * R + L * M * N)
+
+F32 = mybir.dt.float32
+BF16 = mybir.dt.bfloat16
+I32 = mybir.dt.int32
+U32 = mybir.dt.uint32
+U8 = mybir.dt.uint8
+F8 = mybir.dt.float8_e4m3fn
+F8X4 = mybir.dt.float8_e4m3fn_x4
+F4X4 = mybir.dt.float4_e2m1fn_x4
+COPY = mybir.ActivationFunctionType.Copy
+ADD = mybir.AluOpType.add
+MULT = mybir.AluOpType.mult
+
+P = 128
+PASSES = K // 512
+GROUPS = M // 512
+TILES = M // P
+HALF = 512
+QUARTER = 256
+SPLIT_TILES = 2
+BIG = 11
+ALIGN = 64
+
+
+def tile_tubelet_embed_pool_s8_kernel(
+    tc, x_bytes, x_scale, w, time_pos, space_pos, gain, proj_words, proj_scales, pool, out_0, out_1
+):
+    nc = tc.nc
+    with ExitStack() as ctx:
+        keep = ctx.enter_context(tc.tile_pool(name="keep", bufs=1))
+        work = ctx.enter_context(tc.tile_pool(name="work", bufs=2))
+        psum = ctx.enter_context(tc.psum_pool(name="psum", bufs=1))
+        ctx.enter_context(tc.manual_schedule())
+
+        ident = keep.tile([P, P], F32, align_bytes=ALIGN)
+        make_identity(nc, ident[:])
+        pos = keep.tile([P, 4, N], BF16, align_bytes=ALIGN)
+        nc.gpsimd.memset(pos[64:128].rearrange("p t d -> p (t d)").bitcast(F32), 0.0)
+        proj_s = keep.tile([P, 2, R], U8, align_bytes=ALIGN)
+        nc.gpsimd.memset(proj_s[:].rearrange("p b n -> p (b n)").bitcast(I32), 0)
+
+        select = keep.tile([P, GROUPS, 2, 64], BF16, align_bytes=ALIGN)
+        for g in range(GROUPS):
+            nc.vector.tensor_tensor(
+                out=select[:, g],
+                in0=ident[:, 0:64].unsqueeze(1).to_broadcast([P, 2, 64]),
+                in1=ident[:, 64 + 2 * g : 66 + 2 * g].unsqueeze(2).to_broadcast([P, 2, 64]),
+                op=ADD,
+            )
+
+        x_raw = []
+        for s in range(TILES // 2):
+            x_raw.append(keep.tile([P, 2, K], U8, name="x_raw%d" % s, align_bytes=ALIGN))
+        scale_rows = keep.tile([P, K], F32, align_bytes=ALIGN)
+        scale_k = keep.tile([P, PASSES, 4], F32)
+        gain_raw = keep.tile([P, GROUPS, 4], BF16)
+        gain_col = keep.tile([P, TILES], F32, align_bytes=ALIGN)
+        pool_raw = keep.tile([P, 2, M], BF16, align_bytes=ALIGN)
+        proj_w = keep.tile([P, 2, 2 * R], U8, align_bytes=ALIGN)
+        w_raw = {}
+        for h in range(2):
+            for c in range(PASSES):
+                w_raw[c, h] = work.tile(
+                    [P, 4, HALF], BF16, name="w_raw%d%d" % (c, h), tag="big", bufs=BIG, align_bytes=ALIGN
+                )
+
+        w_codes = {}
+        w_scales = {}
+        for h in range(2):
+            for c in range(PASSES):
+                w_codes[c, h] = keep.tile([P, HALF], U32, name="w_codes%d%d" % (c, h), align_bytes=ALIGN)
+                w_scales[c, h] = keep.tile([P, HALF], U8, name="w_scales%d%d" % (c, h), align_bytes=ALIGN)
+        h_codes = []
+        h_scales = []
+        for g in range(GROUPS):
+            h_codes.append(keep.tile([P, N], U32, name="h_codes%d" % g, align_bytes=ALIGN))
+            h_scales.append(keep.tile([P, N], U8, name="h_scales%d" % g, align_bytes=ALIGN))
+        p_codes = keep.tile([P, GROUPS, L], U32, align_bytes=ALIGN)
+        p_scales = keep.tile([P, GROUPS, L], U8, align_bytes=ALIGN)
+
+        def load_w(c, h):
+            rows = w.rearrange("(c p j) n -> c p j n", p=P, j=4)[c]
+            nc.sync.dma_start(out=w_raw[c, h][:], in_=rows[:, :, h * HALF : (h + 1) * HALF])
+
+        def load_x(first, count):
+            g, t = first // 4, first % 4
+            rows = x_bytes.rearrange("(g p t) k -> g p t k", p=P, t=4)[g]
+            slot = first % 2
+            nc.sync.dma_start(out=x_raw[first // 2][:, slot : slot + count, :], in_=rows[:, t : t + count, :])
+
+        nc.scalar.dma_start(out=scale_k[:], in_=x_scale.rearrange("o (c p t) -> p (o c) t", p=P, t=4))
+        load_w(2, 1)
+        load_w(1, 0)
+        load_w(2, 0)
+        load_w(1, 1)
+        nc.sync.dma_start(out=pool_raw[:], in_=pool.rearrange("(a p) m -> p a m", p=P))
+        load_w(0, 1)
+        nc.sync.dma_start(out=gain_raw[:], in_=gain.rearrange("(g p t) -> p g t", p=P, t=4))
+        load_x(0, 1)
+        load_w(0, 0)
+        load_x(1, 1)
+        nc.sync.dma_start(out=pos[0:64], in_=space_pos.rearrange("(k t) d -> k t d", t=4))
+        nc.sync.dma_start(out=pos[64:72], in_=time_pos.unsqueeze(1).to_broadcast([T, 4, N]))
+        nc.sync.dma_start(out=scale_rows[:], in_=x_scale.rearrange("o k -> (o k)").partition_broadcast(P))
+        for i in range(2, TILES, 2):
+            load_x(i, 2)
+        for q in range(4):
+            nc.sync.dma_start(
+                out=proj_s[32 * q : 32 * q + 4].bitcast(I32),
+                in_=proj_scales[:, 4 * q : 4 * q + 4, :].rearrange("b r n -> r b n").bitcast(I32),
+            )
+        nc.sync.dma_start(out=proj_w[:].bitcast(I32), in_=proj_words.rearrange("b p n -> p b n").bitcast(I32))
+
+        w_inter = {}
+        pool_ps = {}
+        pool_inter = {}
+        x_wide = {}
+        x_ps = {}
+        x_inter = {}
+        x_codes = {}
+        x_scales = {}
+        term_ps = {}
+        term = {}
+        e_ps = {}
+        h_rows = {}
+        h_ps = {}
+        hf_inter = {}
+        hf_codes = {}
+        hf_scales = {}
+        feats_ps = {}
+        ht_inter = {}
+        latents_ps = {}
+
+        def interleave_w(c, h, copy):
+            w_i = work.tile([P, HALF, 4], BF16, bufs=3, align_bytes=ALIGN)
+            w_inter[c, h] = w_i
+            copy(
+                out=w_i[:].rearrange("p (u q e) j -> p q j u e", u=2, e=2),
+                in_=w_raw[c, h][:].rearrange("p j (q u e) -> p q j u e", u=2, e=2),
+            )
+
+        def quantize_w(c, h):
+            nc.vector.quantize_mx(
+                out=w_codes[c, h][:].bitcast(F8X4),
+                scales=w_scales[c, h][:],
+                in_=w_inter[c, h][:].rearrange("p n j -> p (n j)"),
+            )
+
+        def turn_pool(g):
+            words = pool_raw[:].rearrange("p a m -> p (a m)").bitcast(F32)
+            turned = psum.tile([P, 2, 2, P], F32, bufs=2)
+            pool_ps[g] = turned
+            for a in range(2):
+                for u in range(2):
+                    m0 = a * (M // 2) + 256 * g
+                    nc.tensor.transpose(turned[:, a, u, :], words[:, m0 + u : m0 + 256 : 2], ident[:])
+
+        def empty_pool(g):
+            pool_i = work.tile([P, 2, P, 2], F32, bufs=4, align_bytes=ALIGN)
+            pool_inter[g] = pool_i
+            nc.scalar.copy(out=pool_i[:], in_=pool_ps[g][:].rearrange("p a u l -> p a l u"))
+
+        def quantize_pool(g):
+            nc.vector.quantize_mx(
+                out=p_codes[:, g].bitcast(F8X4),
+                scales=p_scales[:, g],
+                in_=pool_inter[g][:].rearrange("p a l u -> p (a l u)").bitcast(BF16),
+            )
+
+        x_banks = ((0, 2), (2, 1))
+
+        def widen_x(i):
+            wide = work.tile([P, K], BF16, bufs=3, align_bytes=ALIGN)
+            x_wide[i] = wide
+            values = x_raw[i // 2][:, i % 2, :].bitcast(F8)
+            if i < SPLIT_TILES:
+                nc.scalar.copy(out=wide[:], in_=values)
+            else:
+                nc.vector.tensor_tensor(out=wide[:], in0=values, in1=scale_rows[:], op=MULT)
+
+        def turn_x(i, b):
+            first, count = x_banks[b]
+            words = x_wide[i][:].bitcast(F32)
+            x_turned = psum.tile([P, count, 2, P], F32, bufs=2)
+            x_ps[i, b] = x_turned
+            for c in range(count):
+                for u in range(2):
+                    k0 = 256 * (first + c)
+                    nc.tensor.transpose(x_turned[:, c, u, :], words[:, k0 + u : k0 + 256 : 2], ident[:])
+
+        def empty_x(i, b):
+            first, count = x_banks[b]
+            if b == 0:
+                x_i = work.tile([P, PASSES, P, 2], F32, bufs=3, align_bytes=ALIGN)
+                x_inter[i] = x_i
+            if i >= SPLIT_TILES:
+                nc.scalar.copy(
+                    out=x_inter[i][:, first : first + count], in_=x_ps[i, b][:].rearrange("p c u m -> p c m u")
+                )
+                return
+            raw = x_ps[i, b][:].rearrange("p c u m -> p (c u m)").bitcast(BF16)
+            raw = raw.rearrange("p (c u m e) -> p c m u e", c=count, u=2, e=2)
+            dst = x_inter[i][:].rearrange("p c m u -> p (c m u)").bitcast(BF16)
+            dst = dst.rearrange("p (c m u e) -> p c m u e", c=PASSES, u=2, e=2)
+            for c in range(count):
+                scale = scale_k[:, first + c].rearrange("p (u e) -> p u e", u=2)
+                scale = scale.unsqueeze(1).to_broadcast([P, P, 2, 2])
+                nc.vector.tensor_tensor(out=dst[:, first + c], in0=raw[:, c], in1=scale, op=MULT)
+
+        def quantize_x(i, b):
+            first, count = x_banks[b]
+            if b == 0:
+                codes = work.tile([P, PASSES, P], U32, bufs=3, align_bytes=ALIGN)
+                scales = work.tile([P, PASSES, P], U8, bufs=3, align_bytes=ALIGN)
+                x_codes[i] = codes
+                x_scales[i] = scales
+            cs = slice(first, first + count)
+            nc.vector.quantize_mx(
+                out=x_codes[i][:, cs].rearrange("p c m -> p (c m)").bitcast(F8X4),
+                scales=x_scales[i][:, cs].rearrange("p c m -> p (c m)"),
+                in_=x_inter[i][:, cs].rearrange("p c m u -> p (c m u)").bitcast(BF16),
+            )
+
+        def place(i, h):
+            placed = psum.tile([P, HALF], F32, bufs=1)
+            term_ps[i, h] = placed
+            nc.tensor.matmul(
+                out=placed[:],
+                lhsT=select[:, i // 4].rearrange("p a b -> p (a b)"),
+                rhs=pos[:, i % 4, h * HALF : (h + 1) * HALF],
+                start=True,
+                stop=True,
+            )
+
+        def scale_term(i, h):
+            if h == 0:
+                term_i = work.tile([P, 2, HALF], F32, tag="big", bufs=BIG, align_bytes=ALIGN)
+                term[i] = term_i
+            nc.scalar.activation(
+                out=term[i][:, h].rearrange("p (u q e) -> p u q e", u=2, e=2),
+                in_=term_ps[i, h][:].rearrange("p (q u e) -> p u q e", u=2, e=2),
+                func=COPY,
+                scale=gain_col[:, i : i + 1],
+            )
+
+        def embed(i, h):
+            acc = psum.tile([P, HALF], F32, bufs=2)
+            e_ps[i, h] = acc
+            for c in range(PASSES):
+                nc.tensor.matmul_mx(
+                    out=acc[:],
+                    lhsT=x_codes[i][:, c].bitcast(F8X4),
+                    lhsT_scale=x_scales[i][:, c],
+                    rhs=w_codes[c, h][:].bitcast(F8X4),
+                    rhs_scale=w_scales[c, h][:],
+                    start=(c == 0),
+                    stop=(c == PASSES - 1),
+                )
+
+        def finish_h(i, h):
+            g, t = i // 4, i % 4
+            if t == 0 and h == 0:
+                rows = work.tile([P, 4, N], BF16, bufs=2, align_bytes=ALIGN)
+                h_rows[g] = rows
+            nc.vector.scalar_tensor_tensor(
+                out=h_rows[g][:, t, h * HALF : (h + 1) * HALF],
+                in0=e_ps[i, h][:],
+                scalar=gain_col[:, i : i + 1],
+                in1=term[i][:, h],
+                op0=MULT,
+                op1=ADD,
+            )
+
+        def turn_h(i):
+            g, t = i // 4, i % 4
+            words = h_rows[g][:].rearrange("p t d -> p (t d)").bitcast(F32)
+            turned = psum.tile([P, 2, 2, P], F32, bufs=2)
+            h_ps[i] = turned
+            for b in range(2):
+                for u in range(2):
+                    d0 = t * HALF + 256 * b + 128 * u
+                    nc.tensor.transpose(turned[:, b, u, :], words[:, d0 : d0 + 128], ident[:])
+
+        def empty_h(i):
+            hf_i = work.tile([P, 2, P, 2], F32, bufs=3, align_bytes=ALIGN)
+            hf_inter[i] = hf_i
+            nc.scalar.copy(out=hf_i[:], in_=h_ps[i][:].rearrange("p b u m -> p b m u"))
+
+        def quantize_features(i):
+            codes_f = work.tile([P, 2, P], U32, bufs=2, align_bytes=ALIGN)
+            scales_f = work.tile([P, 2, P], U8, bufs=2, align_bytes=ALIGN)
+            hf_codes[i] = codes_f
+            hf_scales[i] = scales_f
+            nc.vector.quantize_mx(
+                out=codes_f[:].rearrange("p b m -> p (b m)").bitcast(F8X4),
+                scales=scales_f[:].rearrange("p b m -> p (b m)"),
+                in_=hf_inter[i][:].rearrange("p b m u -> p (b m u)").bitcast(BF16),
+            )
+
+        def project(i):
+            projected = psum.tile([P, R], F32, bufs=1)
+            feats_ps[i] = projected
+            for b in range(2):
+                nc.tensor.matmul_mx(
+                    out=projected[:],
+                    lhsT=hf_codes[i][:, b].bitcast(F8X4),
+                    lhsT_scale=hf_scales[i][:, b],
+                    rhs=proj_w[:, b].bitcast(F4X4),
+                    rhs_scale=proj_s[:, b],
+                    start=(b == 0),
+                    stop=(b == 1),
+                )
+
+        def store_features(i):
+            feats = work.tile([P, R], F32, bufs=3, align_bytes=ALIGN)
+            nc.scalar.copy(out=feats[:], in_=feats_ps[i][:])
+            nc.sync.dma_start(out=out_0.rearrange("(g p t) r -> g t p r", p=P, t=4)[i // 4, i % 4], in_=feats[:])
+
+        def interleave_h(n):
+            g, d0 = n // 4, QUARTER * (n % 4)
+            ht_i = work.tile([P, QUARTER, 4], BF16, bufs=3, align_bytes=ALIGN)
+            ht_inter[n] = ht_i
+            on_scalar = n % 3 != 1 and g < GROUPS - 1
+            copy = nc.scalar.copy if on_scalar else nc.vector.tensor_copy
+            copy(
+                out=ht_i[:].rearrange("p (n i) t -> p n t i", i=4),
+                in_=h_rows[g][:, :, d0 : d0 + QUARTER].rearrange("p t (n i) -> p n t i", i=4),
+            )
+
+        def quantize_tokens(n):
+            g, d0 = n // 4, QUARTER * (n % 4)
+            nc.vector.quantize_mx(
+                out=h_codes[g][:, d0 : d0 + QUARTER].bitcast(F8X4),
+                scales=h_scales[g][:, d0 : d0 + QUARTER],
+                in_=ht_inter[n][:].rearrange("p d t -> p (d t)"),
+            )
+
+        def pool_pass(g, h):
+            for a in range(2):
+                nc.tensor.matmul_mx(
+                    out=latents_ps[a, h][:],
+                    lhsT=p_codes[:, g, a * P : (a + 1) * P].bitcast(F8X4),
+                    lhsT_scale=p_scales[:, g, a * P : (a + 1) * P],
+                    rhs=h_codes[g][:, h * HALF : (h + 1) * HALF].bitcast(F8X4),
+                    rhs_scale=h_scales[g][:, h * HALF : (h + 1) * HALF],
+                    start=(g == 0),
+                    stop=(g == GROUPS - 1),
+                )
+
+        def store_latents(a, h):
+            lat = work.tile([P, HALF], F32, bufs=4, align_bytes=ALIGN)
+            copy = nc.vector.tensor_copy if a == 0 else nc.scalar.copy
+            copy(
+                out=lat[:].rearrange("p (q u e) -> p q u e", u=2, e=2),
+                in_=latents_ps[a, h][:].rearrange("p (u q e) -> p q u e", u=2, e=2),
+            )
+            nc.sync.dma_start(out=out_1[a * P : (a + 1) * P, h * HALF : (h + 1) * HALF], in_=lat[:])
+
+        scalar, vector = nc.scalar.copy, nc.vector.tensor_copy
+        interleave_w(1, 0, vector)
+        interleave_w(2, 1, scalar)
+        quantize_w(1, 0)
+        interleave_w(2, 0, scalar)
+        interleave_w(1, 1, vector)
+        quantize_w(1, 1)
+        turn_pool(0)
+        quantize_w(2, 1)
+        empty_pool(0)
+        quantize_w(2, 0)
+        turn_pool(1)
+        interleave_w(0, 1, vector)
+        quantize_pool(0)
+        nc.vector.tensor_copy(out=gain_col[:], in_=gain_raw[:].rearrange("p g t -> p (g t)"))
+        empty_pool(1)
+        interleave_w(0, 0, vector)
+        turn_pool(2)
+        turn_pool(3)
+        empty_pool(2)
+        quantize_pool(1)
+        quantize_w(0, 1)
+        quantize_w(0, 0)
+        widen_x(0)
+        empty_pool(3)
+
+        steps = (
+            (turn_x, 1, (0,)),
+            (widen_x, 2, ()),
+            (store_features, -3, ()),
+            (empty_x, 1, (0,)),
+            (turn_x, 1, (1,)),
+            (turn_h, -1, ()),
+            (place, 1, (0,)),
+            (embed, 0, (0,)),
+            (scale_term, 1, (0,)),
+            (embed, 0, (1,)),
+            (empty_x, 1, (1,)),
+            (interleave_h, -4, ()),
+            (quantize_features, -2, ()),
+            (place, 1, (1,)),
+            (scale_term, 1, (1,)),
+            (quantize_tokens, -5, ()),
+            (empty_h, -1, ()),
+            (finish_h, 0, (0,)),
+            (project, -2, ()),
+            (finish_h, 0, (1,)),
+            (quantize_x, 1, (0,)),
+            (quantize_x, 1, (1,)),
+        )
+        for i in range(-1, TILES + 5):
+            if i in (2, 3):
+                quantize_pool(i)
+            if i == TILES:
+                banks = (("x_turned", 2), ("x_turned", 2), ("placed", 1), ("acc", 2))
+                for n, (tag, bufs) in enumerate(banks):
+                    bank = psum.tile([P, HALF], F32, tag=tag, bufs=bufs)
+                    latents_ps[n // 2, n % 2] = bank
+            if TILES <= i < TILES + 3:
+                for h in range(2):
+                    pool_pass(i - TILES, h)
+            for stage, ahead, part in steps:
+                if 0 <= i + ahead < TILES:
+                    stage(i + ahead, *part)
+            if i == TILES + 2:
+                pool_pass(3, 0)
+        pool_pass(3, 1)
+        for h in range(2):
+            for a in range(2):
+                store_latents(a, h)

@@ -22,10 +22,11 @@ P = 128
 PASSES = K // 512
 GROUPS = M // 512
 TILES = M // P
+PAIRS = TILES // 2
 HALF = 512
 QUARTER = 256
-SPLIT_TILES = 2
-BIG = 11
+SHARE = 64
+POOL_STEP = 5
 ALIGN = 64
 
 
@@ -36,16 +37,23 @@ def tile_tubelet_embed_pool_s8_kernel(
     with ExitStack() as ctx:
         keep = ctx.enter_context(tc.tile_pool(name="keep", bufs=1))
         work = ctx.enter_context(tc.tile_pool(name="work", bufs=2))
-        psum = ctx.enter_context(tc.psum_pool(name="psum", bufs=1))
+        psum = ctx.enter_context(tc.psum_pool(name="psum", bufs=4))
         ctx.enter_context(tc.manual_schedule())
+
+        def bank_in(shape, dtype):
+            return psum.tile(shape, dtype, name="bank_in")
+
+        def bank_out(shape, dtype):
+            return psum.tile(shape, dtype, name="bank_out")
 
         ident = keep.tile([P, P], F32, align_bytes=ALIGN)
         make_identity(nc, ident[:])
         pos = keep.tile([P, 4, N], BF16, align_bytes=ALIGN)
-        nc.gpsimd.memset(pos[64:128].rearrange("p t d -> p (t d)").bitcast(F32), 0.0)
+        nc.vector.memset(pos[64:128].rearrange("p t d -> p (t d)").bitcast(F32), 0.0)
+        ident_b = keep.tile([P, P], BF16, align_bytes=ALIGN)
+        nc.vector.tensor_copy(out=ident_b[:], in_=ident[:])
         proj_s = keep.tile([P, 2, R], U8, align_bytes=ALIGN)
-        nc.gpsimd.memset(proj_s[:].rearrange("p b n -> p (b n)").bitcast(I32), 0)
-
+        nc.vector.memset(proj_s[:].rearrange("p b n -> p (b n)").bitcast(I32), 0)
         select = keep.tile([P, GROUPS, 2, 64], BF16, align_bytes=ALIGN)
         for g in range(GROUPS):
             nc.vector.tensor_tensor(
@@ -56,25 +64,20 @@ def tile_tubelet_embed_pool_s8_kernel(
             )
 
         x_raw = []
-        for s in range(TILES // 2):
+        for s in range(PAIRS):
             x_raw.append(keep.tile([P, 2, K], U8, name="x_raw%d" % s, align_bytes=ALIGN))
-        scale_rows = keep.tile([P, K], F32, align_bytes=ALIGN)
+        scale_all = keep.tile([P, K], F32, align_bytes=ALIGN)
         scale_k = keep.tile([P, PASSES, 4], F32)
         gain_raw = keep.tile([P, GROUPS, 4], BF16)
         gain_col = keep.tile([P, TILES], F32, align_bytes=ALIGN)
         pool_raw = keep.tile([P, 2, M], BF16, align_bytes=ALIGN)
         proj_w = keep.tile([P, 2, 2 * R], U8, align_bytes=ALIGN)
         w_raw = {}
-        for h in range(2):
-            for c in range(PASSES):
-                w_raw[c, h] = work.tile(
-                    [P, 4, HALF], BF16, name="w_raw%d%d" % (c, h), tag="big", bufs=BIG, align_bytes=ALIGN
-                )
-
         w_codes = {}
         w_scales = {}
         for h in range(2):
             for c in range(PASSES):
+                w_raw[c, h] = keep.tile([P, 4, HALF], BF16, name="w_raw%d%d" % (c, h), align_bytes=ALIGN)
                 w_codes[c, h] = keep.tile([P, HALF], U32, name="w_codes%d%d" % (c, h), align_bytes=ALIGN)
                 w_scales[c, h] = keep.tile([P, HALF], U8, name="w_scales%d%d" % (c, h), align_bytes=ALIGN)
         h_codes = []
@@ -82,8 +85,6 @@ def tile_tubelet_embed_pool_s8_kernel(
         for g in range(GROUPS):
             h_codes.append(keep.tile([P, N], U32, name="h_codes%d" % g, align_bytes=ALIGN))
             h_scales.append(keep.tile([P, N], U8, name="h_scales%d" % g, align_bytes=ALIGN))
-        p_codes = keep.tile([P, GROUPS, L], U32, align_bytes=ALIGN)
-        p_scales = keep.tile([P, GROUPS, L], U8, align_bytes=ALIGN)
 
         def load_w(c, h):
             rows = w.rearrange("(c p j) n -> c p j n", p=P, j=4)[c]
@@ -95,32 +96,37 @@ def tile_tubelet_embed_pool_s8_kernel(
             slot = first % 2
             nc.sync.dma_start(out=x_raw[first // 2][:, slot : slot + count, :], in_=rows[:, t : t + count, :])
 
+        def load_sites(t):
+            nc.sync.dma_start(out=pos[0:64, t : t + 2], in_=space_pos.rearrange("(k t) d -> k t d", t=4)[:, t : t + 2])
+
         nc.scalar.dma_start(out=scale_k[:], in_=x_scale.rearrange("o (c p t) -> p (o c) t", p=P, t=4))
-        load_w(2, 1)
-        load_w(1, 0)
-        load_w(2, 0)
-        load_w(1, 1)
-        nc.sync.dma_start(out=pool_raw[:], in_=pool.rearrange("(a p) m -> p a m", p=P))
-        load_w(0, 1)
-        nc.sync.dma_start(out=gain_raw[:], in_=gain.rearrange("(g p t) -> p g t", p=P, t=4))
         load_x(0, 1)
         load_w(0, 0)
         load_x(1, 1)
-        nc.sync.dma_start(out=pos[0:64], in_=space_pos.rearrange("(k t) d -> k t d", t=4))
+        load_w(1, 0)
+        load_w(2, 0)
+        nc.scalar.dma_start(out=gain_raw[:], in_=gain.rearrange("(g p t) -> p g t", p=P, t=4))
+        load_x(2, 2)
+        load_w(0, 1)
+        load_w(1, 1)
+        load_w(2, 1)
+        load_sites(0)
         nc.sync.dma_start(out=pos[64:72], in_=time_pos.unsqueeze(1).to_broadcast([T, 4, N]))
-        nc.sync.dma_start(out=scale_rows[:], in_=x_scale.rearrange("o k -> (o k)").partition_broadcast(P))
-        for i in range(2, TILES, 2):
-            load_x(i, 2)
+        load_sites(2)
+        load_x(4, 2)
         for q in range(4):
             nc.sync.dma_start(
                 out=proj_s[32 * q : 32 * q + 4].bitcast(I32),
                 in_=proj_scales[:, 4 * q : 4 * q + 4, :].rearrange("b r n -> r b n").bitcast(I32),
             )
         nc.sync.dma_start(out=proj_w[:].bitcast(I32), in_=proj_words.rearrange("b p n -> p b n").bitcast(I32))
+        nc.sync.dma_start(out=pool_raw[:], in_=pool.rearrange("(a p) m -> p a m", p=P))
+        for i in range(6, TILES, 2):
+            load_x(i, 2)
 
+        scale_ps = {}
+        w_ps = {}
         w_inter = {}
-        pool_ps = {}
-        pool_inter = {}
         x_wide = {}
         x_ps = {}
         x_inter = {}
@@ -138,11 +144,36 @@ def tile_tubelet_embed_pool_s8_kernel(
         ht_inter = {}
         latents_ps = {}
 
-        def interleave_w(c, h, copy):
-            w_i = work.tile([P, HALF, 4], BF16, bufs=3, align_bytes=ALIGN)
+        def spread_scale(c):
+            spread = bank_in([P, 4, P], F32)
+            scale_ps[c] = spread
+            for t in range(4):
+                nc.tensor.transpose(spread[:, t, :], scale_k[:, c, t : t + 1].to_broadcast([P, P]), ident[:])
+
+        def empty_scale(c, copy):
+            copy(
+                out=scale_all[:, c * 512 : (c + 1) * 512].rearrange("p (n t) -> p n t", t=4),
+                in_=scale_ps[c][:].rearrange("p t n -> p n t"),
+            )
+
+        def interleave_w(c, h, u, bank):
+            laid = bank([P, 2, 64, 2, 4], BF16)
+            w_ps[c, h, u] = laid
+            rows = w_raw[c, h][:].rearrange("p j (s q u e) -> p u s q e j", s=2, u=2, e=2)
+            for s in range(2):
+                nc.tensor.matmul(out=laid[:, s], lhsT=ident_b[:], rhs=rows[:, u, s], start=True, stop=True)
+
+        def empty_w(c, h, u):
+            if u == 0:
+                w_i = work.tile([P, 2, 2 * HALF], BF16, bufs=3, align_bytes=ALIGN)
+                w_inter[c, h] = w_i
+            nc.scalar.copy(out=w_inter[c, h][:, u], in_=w_ps[c, h, u][:].rearrange("p s q e j -> p (s q e j)"))
+
+        def copy_w(c, h, copy):
+            w_i = work.tile([P, 2, 2 * HALF], BF16, bufs=3, align_bytes=ALIGN)
             w_inter[c, h] = w_i
             copy(
-                out=w_i[:].rearrange("p (u q e) j -> p q j u e", u=2, e=2),
+                out=w_i[:].rearrange("p u (q e j) -> p q j u e", e=2, j=4),
                 in_=w_raw[c, h][:].rearrange("p j (q u e) -> p q j u e", u=2, e=2),
             )
 
@@ -150,78 +181,54 @@ def tile_tubelet_embed_pool_s8_kernel(
             nc.vector.quantize_mx(
                 out=w_codes[c, h][:].bitcast(F8X4),
                 scales=w_scales[c, h][:],
-                in_=w_inter[c, h][:].rearrange("p n j -> p (n j)"),
+                in_=w_inter[c, h][:].rearrange("p u n -> p (u n)"),
             )
 
-        def turn_pool(g):
-            words = pool_raw[:].rearrange("p a m -> p (a m)").bitcast(F32)
-            turned = psum.tile([P, 2, 2, P], F32, bufs=2)
-            pool_ps[g] = turned
-            for a in range(2):
-                for u in range(2):
-                    m0 = a * (M // 2) + 256 * g
-                    nc.tensor.transpose(turned[:, a, u, :], words[:, m0 + u : m0 + 256 : 2], ident[:])
+        def rides(i):
+            return POOL_STEP <= i < POOL_STEP + 2 * GROUPS
 
-        def empty_pool(g):
-            pool_i = work.tile([P, 2, P, 2], F32, bufs=4, align_bytes=ALIGN)
-            pool_inter[g] = pool_i
-            nc.scalar.copy(out=pool_i[:], in_=pool_ps[g][:].rearrange("p a u l -> p a l u"))
+        def blocks(i, b):
+            return slice(0, 2) if b == 0 else slice(2, 4 if rides(i) else 3)
 
-        def quantize_pool(g):
-            nc.vector.quantize_mx(
-                out=p_codes[:, g].bitcast(F8X4),
-                scales=p_scales[:, g],
-                in_=pool_inter[g][:].rearrange("p a l u -> p (a l u)").bitcast(BF16),
+        def widen_x(i, first=0, count=PASSES):
+            if first == 0:
+                wide = work.tile([P, K], BF16, bufs=3, align_bytes=ALIGN)
+                x_wide[i] = wide
+            ks = slice(512 * first, 512 * (first + count))
+            nc.vector.tensor_tensor(
+                out=x_wide[i][:, ks], in0=x_raw[i // 2][:, i % 2, ks].bitcast(F8), in1=scale_all[:, ks], op=MULT
             )
-
-        x_banks = ((0, 2), (2, 1))
-
-        def widen_x(i):
-            wide = work.tile([P, K], BF16, bufs=3, align_bytes=ALIGN)
-            x_wide[i] = wide
-            values = x_raw[i // 2][:, i % 2, :].bitcast(F8)
-            if i < SPLIT_TILES:
-                nc.scalar.copy(out=wide[:], in_=values)
-            else:
-                nc.vector.tensor_tensor(out=wide[:], in0=values, in1=scale_rows[:], op=MULT)
 
         def turn_x(i, b):
-            first, count = x_banks[b]
-            words = x_wide[i][:].bitcast(F32)
-            x_turned = psum.tile([P, count, 2, P], F32, bufs=2)
+            cs = blocks(i, b)
+            x_turned = bank_in([P, cs.stop - cs.start, 2, P], F32)
             x_ps[i, b] = x_turned
-            for c in range(count):
+            for c in range(cs.start, cs.stop):
+                if c < PASSES:
+                    words = x_wide[i][:].bitcast(F32)[:, 256 * c : 256 * (c + 1)]
+                else:
+                    g, a = divmod(i - POOL_STEP, 2)
+                    words = pool_raw[:, a].bitcast(F32)[:, 256 * g : 256 * (g + 1)]
                 for u in range(2):
-                    k0 = 256 * (first + c)
-                    nc.tensor.transpose(x_turned[:, c, u, :], words[:, k0 + u : k0 + 256 : 2], ident[:])
+                    nc.tensor.transpose(x_turned[:, c - cs.start, u, :], words[:, u:256:2], ident[:])
 
         def empty_x(i, b):
-            first, count = x_banks[b]
             if b == 0:
-                x_i = work.tile([P, PASSES, P, 2], F32, bufs=3, align_bytes=ALIGN)
+                x_i = work.tile([P, PASSES + 1, P, 2], F32, bufs=3, align_bytes=ALIGN)
                 x_inter[i] = x_i
-            if i >= SPLIT_TILES:
-                nc.scalar.copy(
-                    out=x_inter[i][:, first : first + count], in_=x_ps[i, b][:].rearrange("p c u m -> p c m u")
-                )
-                return
-            raw = x_ps[i, b][:].rearrange("p c u m -> p (c u m)").bitcast(BF16)
-            raw = raw.rearrange("p (c u m e) -> p c m u e", c=count, u=2, e=2)
-            dst = x_inter[i][:].rearrange("p c m u -> p (c m u)").bitcast(BF16)
-            dst = dst.rearrange("p (c m u e) -> p c m u e", c=PASSES, u=2, e=2)
-            for c in range(count):
-                scale = scale_k[:, first + c].rearrange("p (u e) -> p u e", u=2)
-                scale = scale.unsqueeze(1).to_broadcast([P, P, 2, 2])
-                nc.vector.tensor_tensor(out=dst[:, first + c], in0=raw[:, c], in1=scale, op=MULT)
+            nc.scalar.copy(out=x_inter[i][:, blocks(i, b)], in_=x_ps[i, b][:].rearrange("p c u m -> p c m u"))
 
         def quantize_x(i, b):
-            first, count = x_banks[b]
             if b == 0:
-                codes = work.tile([P, PASSES, P], U32, bufs=3, align_bytes=ALIGN)
-                scales = work.tile([P, PASSES, P], U8, bufs=3, align_bytes=ALIGN)
+                if rides(i):
+                    codes = keep.tile([P, PASSES + 1, P], U32, name="x_codes%d" % i, align_bytes=ALIGN)
+                    scales = keep.tile([P, PASSES + 1, P], U8, name="x_scales%d" % i, align_bytes=ALIGN)
+                else:
+                    codes = work.tile([P, PASSES, P], U32, bufs=3, align_bytes=ALIGN)
+                    scales = work.tile([P, PASSES, P], U8, bufs=3, align_bytes=ALIGN)
                 x_codes[i] = codes
                 x_scales[i] = scales
-            cs = slice(first, first + count)
+            cs = blocks(i, b)
             nc.vector.quantize_mx(
                 out=x_codes[i][:, cs].rearrange("p c m -> p (c m)").bitcast(F8X4),
                 scales=x_scales[i][:, cs].rearrange("p c m -> p (c m)"),
@@ -229,7 +236,7 @@ def tile_tubelet_embed_pool_s8_kernel(
             )
 
         def place(i, h):
-            placed = psum.tile([P, HALF], F32, bufs=1)
+            placed = bank_in([P, HALF], F32)
             term_ps[i, h] = placed
             nc.tensor.matmul(
                 out=placed[:],
@@ -240,18 +247,17 @@ def tile_tubelet_embed_pool_s8_kernel(
             )
 
         def scale_term(i, h):
-            if h == 0:
-                term_i = work.tile([P, 2, HALF], F32, tag="big", bufs=BIG, align_bytes=ALIGN)
-                term[i] = term_i
+            term_i = work.tile([P, HALF], F32, bufs=6, align_bytes=ALIGN)
+            term[i, h] = term_i
             nc.scalar.activation(
-                out=term[i][:, h].rearrange("p (u q e) -> p u q e", u=2, e=2),
+                out=term_i[:].rearrange("p (u q e) -> p u q e", u=2, e=2),
                 in_=term_ps[i, h][:].rearrange("p (q u e) -> p u q e", u=2, e=2),
                 func=COPY,
                 scale=gain_col[:, i : i + 1],
             )
 
         def embed(i, h):
-            acc = psum.tile([P, HALF], F32, bufs=2)
+            acc = bank_out([P, HALF], F32)
             e_ps[i, h] = acc
             for c in range(PASSES):
                 nc.tensor.matmul_mx(
@@ -273,7 +279,7 @@ def tile_tubelet_embed_pool_s8_kernel(
                 out=h_rows[g][:, t, h * HALF : (h + 1) * HALF],
                 in0=e_ps[i, h][:],
                 scalar=gain_col[:, i : i + 1],
-                in1=term[i][:, h],
+                in1=term[i, h][:],
                 op0=MULT,
                 op1=ADD,
             )
@@ -281,7 +287,7 @@ def tile_tubelet_embed_pool_s8_kernel(
         def turn_h(i):
             g, t = i // 4, i % 4
             words = h_rows[g][:].rearrange("p t d -> p (t d)").bitcast(F32)
-            turned = psum.tile([P, 2, 2, P], F32, bufs=2)
+            turned = bank_out([P, 2, 2, P], F32)
             h_ps[i] = turned
             for b in range(2):
                 for u in range(2):
@@ -305,7 +311,7 @@ def tile_tubelet_embed_pool_s8_kernel(
             )
 
         def project(i):
-            projected = psum.tile([P, R], F32, bufs=1)
+            projected = bank_out([P, R], F32)
             feats_ps[i] = projected
             for b in range(2):
                 nc.tensor.matmul_mx(
@@ -323,15 +329,14 @@ def tile_tubelet_embed_pool_s8_kernel(
             nc.scalar.copy(out=feats[:], in_=feats_ps[i][:])
             nc.sync.dma_start(out=out_0.rearrange("(g p t) r -> g t p r", p=P, t=4)[i // 4, i % 4], in_=feats[:])
 
-        def interleave_h(n):
-            g, d0 = n // 4, QUARTER * (n % 4)
-            ht_i = work.tile([P, QUARTER, 4], BF16, bufs=3, align_bytes=ALIGN)
-            ht_inter[n] = ht_i
-            on_scalar = n % 3 != 1 and g < GROUPS - 1
-            copy = nc.scalar.copy if on_scalar else nc.vector.tensor_copy
+        def interleave_h(n, copy, first, count):
+            g, d0 = n // 4, QUARTER * (n % 4) + first
+            if n not in ht_inter:
+                ht_i = work.tile([P, QUARTER, 4], BF16, bufs=3, align_bytes=ALIGN)
+                ht_inter[n] = ht_i
             copy(
-                out=ht_i[:].rearrange("p (n i) t -> p n t i", i=4),
-                in_=h_rows[g][:, :, d0 : d0 + QUARTER].rearrange("p t (n i) -> p n t i", i=4),
+                out=ht_inter[n][:, first : first + count].rearrange("p (n i) t -> p n t i", i=4),
+                in_=h_rows[g][:, :, d0 : d0 + count].rearrange("p t (n i) -> p n t i", i=4),
             )
 
         def quantize_tokens(n):
@@ -342,17 +347,18 @@ def tile_tubelet_embed_pool_s8_kernel(
                 in_=ht_inter[n][:].rearrange("p d t -> p (d t)"),
             )
 
-        def pool_pass(g, h):
-            for a in range(2):
-                nc.tensor.matmul_mx(
-                    out=latents_ps[a, h][:],
-                    lhsT=p_codes[:, g, a * P : (a + 1) * P].bitcast(F8X4),
-                    lhsT_scale=p_scales[:, g, a * P : (a + 1) * P],
-                    rhs=h_codes[g][:, h * HALF : (h + 1) * HALF].bitcast(F8X4),
-                    rhs_scale=h_scales[g][:, h * HALF : (h + 1) * HALF],
-                    start=(g == 0),
-                    stop=(g == GROUPS - 1),
-                )
+        def pool_pass(g, a, h):
+            if g == 0:
+                latents_ps[a, h] = bank_in([P, HALF], F32)
+            nc.tensor.matmul_mx(
+                out=latents_ps[a, h][:],
+                lhsT=x_codes[POOL_STEP + 2 * g + a][:, PASSES].bitcast(F8X4),
+                lhsT_scale=x_scales[POOL_STEP + 2 * g + a][:, PASSES],
+                rhs=h_codes[g][:, h * HALF : (h + 1) * HALF].bitcast(F8X4),
+                rhs_scale=h_scales[g][:, h * HALF : (h + 1) * HALF],
+                start=(g == 0),
+                stop=(g == GROUPS - 1),
+            )
 
         def store_latents(a, h):
             lat = work.tile([P, HALF], F32, bufs=4, align_bytes=ALIGN)
@@ -364,72 +370,144 @@ def tile_tubelet_embed_pool_s8_kernel(
             nc.sync.dma_start(out=out_1[a * P : (a + 1) * P, h * HALF : (h + 1) * HALF], in_=lat[:])
 
         scalar, vector = nc.scalar.copy, nc.vector.tensor_copy
-        interleave_w(1, 0, vector)
-        interleave_w(2, 1, scalar)
-        quantize_w(1, 0)
-        interleave_w(2, 0, scalar)
-        interleave_w(1, 1, vector)
-        quantize_w(1, 1)
-        turn_pool(0)
-        quantize_w(2, 1)
-        empty_pool(0)
-        quantize_w(2, 0)
-        turn_pool(1)
-        interleave_w(0, 1, vector)
-        quantize_pool(0)
-        nc.vector.tensor_copy(out=gain_col[:], in_=gain_raw[:].rearrange("p g t -> p (g t)"))
-        empty_pool(1)
-        interleave_w(0, 0, vector)
-        turn_pool(2)
-        turn_pool(3)
-        empty_pool(2)
-        quantize_pool(1)
-        quantize_w(0, 1)
-        quantize_w(0, 0)
-        widen_x(0)
-        empty_pool(3)
 
-        steps = (
-            (turn_x, 1, (0,)),
-            (widen_x, 2, ()),
-            (store_features, -3, ()),
-            (empty_x, 1, (0,)),
-            (turn_x, 1, (1,)),
-            (turn_h, -1, ()),
-            (place, 1, (0,)),
-            (embed, 0, (0,)),
-            (scale_term, 1, (0,)),
-            (embed, 0, (1,)),
-            (empty_x, 1, (1,)),
-            (interleave_h, -4, ()),
-            (quantize_features, -2, ()),
-            (place, 1, (1,)),
-            (scale_term, 1, (1,)),
-            (quantize_tokens, -5, ()),
-            (empty_h, -1, ()),
-            (finish_h, 0, (0,)),
-            (project, -2, ()),
-            (finish_h, 0, (1,)),
-            (quantize_x, 1, (0,)),
-            (quantize_x, 1, (1,)),
-        )
-        for i in range(-1, TILES + 5):
-            if i in (2, 3):
-                quantize_pool(i)
-            if i == TILES:
-                banks = (("x_turned", 2), ("x_turned", 2), ("placed", 1), ("acc", 2))
-                for n, (tag, bufs) in enumerate(banks):
-                    bank = psum.tile([P, HALF], F32, tag=tag, bufs=bufs)
-                    latents_ps[n // 2, n % 2] = bank
-            if TILES <= i < TILES + 3:
-                for h in range(2):
-                    pool_pass(i - TILES, h)
-            for stage, ahead, part in steps:
-                if 0 <= i + ahead < TILES:
-                    stage(i + ahead, *part)
-            if i == TILES + 2:
-                pool_pass(3, 0)
-        pool_pass(3, 1)
-        for h in range(2):
-            for a in range(2):
-                store_latents(a, h)
+        def prepare_w(c, h, bank):
+            for u in range(2):
+                interleave_w(c, h, u, bank)
+                empty_w(c, h, u)
+
+        for c in range(PASSES):
+            spread_scale(c)
+            empty_scale(c, vector if c == 0 else scalar)
+            widen_x(0, c, 1)
+        prepare_w(0, 0, bank_out)
+        widen_x(1)
+        prepare_w(1, 0, bank_out)
+        turn_x(0, 0)
+        turn_x(0, 1)
+        empty_x(0, 0)
+        empty_x(0, 1)
+        quantize_w(0, 0)
+        widen_x(2)
+        prepare_w(2, 0, bank_out)
+        quantize_w(1, 0)
+        quantize_x(0, 0)
+        quantize_x(0, 1)
+        quantize_w(2, 0)
+        turn_x(1, 0)
+        turn_x(1, 1)
+        empty_x(1, 0)
+        empty_x(1, 1)
+        embed(0, 0)
+        quantize_x(1, 0)
+        quantize_x(1, 1)
+        copy_w(0, 1, vector)
+        copy_w(1, 1, scalar)
+        turn_x(2, 0)
+        turn_x(2, 1)
+        empty_x(2, 0)
+        empty_x(2, 1)
+        embed(1, 0)
+        prepare_w(2, 1, bank_in)
+        quantize_w(0, 1)
+        quantize_w(1, 1)
+        quantize_x(2, 0)
+        quantize_x(2, 1)
+        nc.vector.tensor_copy(out=gain_col[:], in_=gain_raw[:].rearrange("p g t -> p (g t)"))
+        place(0, 0)
+        place(1, 0)
+        embed(2, 0)
+        quantize_w(2, 1)
+        scale_term(0, 0)
+        scale_term(1, 0)
+        finish_h(0, 0)
+        widen_x(3)
+        place(0, 1)
+        place(2, 0)
+        scale_term(0, 1)
+        scale_term(2, 0)
+        embed(0, 1)
+        place(1, 1)
+        scale_term(1, 1)
+        embed(1, 1)
+        finish_h(1, 0)
+        finish_h(0, 1)
+        finish_h(2, 0)
+        finish_h(1, 1)
+
+        for i in range(3, TILES + 1):
+            last = i == TILES
+            n = i - 4
+            if not last:
+                turn_x(i, 0)
+                turn_x(i, 1)
+            if i == 3:
+                turn_h(0)
+            turn_h(i - 2)
+            if i >= 4:
+                store_features(i - 3)
+            if i + 1 < TILES:
+                widen_x(i + 1)
+            if last:
+                interleave_h(12, vector, 0, QUARTER)
+            if not last:
+                empty_x(i, 0)
+                empty_x(i, 1)
+            if i == 3:
+                empty_h(0)
+            empty_h(i - 2)
+            place(i - 1, 1)
+            scale_term(i - 1, 1)
+            if not last:
+                place(i, 0)
+                scale_term(i, 0)
+                quantize_x(i, 0)
+                quantize_x(i, 1)
+            if i == 3:
+                quantize_features(0)
+            quantize_features(i - 2)
+            if n >= 1:
+                quantize_tokens(n - 1)
+            embed(i - 1, 1)
+            if last:
+                break
+            finish_h(i - 1, 1)
+            embed(i, 0)
+            if i == 3:
+                project(0)
+                store_features(0)
+            project(i - 2)
+            if n >= 0:
+                interleave_h(n, vector if n % 3 == 2 else scalar, 0, QUARTER)
+            finish_h(i, 0)
+
+        interleave_h(13, scalar, 0, QUARTER)
+        finish_h(15, 1)
+        for g in range(GROUPS - 1):
+            pool_pass(g, 0, 0)
+            if g == 0:
+                project(14)
+                store_features(14)
+            pool_pass(g, 1, 0)
+        turn_h(15)
+        interleave_h(14, vector, 0, QUARTER)
+        quantize_tokens(12)
+        quantize_tokens(13)
+        empty_h(15)
+        interleave_h(15, vector, 0, QUARTER)
+        pool_pass(3, 0, 0)
+        pool_pass(3, 1, 0)
+        store_latents(1, 0)
+        quantize_tokens(14)
+        quantize_features(15)
+        quantize_tokens(15)
+        store_latents(0, 0)
+        for g in range(GROUPS - 1):
+            pool_pass(g, 0, 1)
+        project(15)
+        pool_pass(3, 0, 1)
+        store_features(15)
+        store_latents(0, 1)
+        for g in range(GROUPS):
+            pool_pass(g, 1, 1)
+        store_latents(1, 1)

@@ -50,8 +50,6 @@ def tile_tubelet_embed_pool_s8_kernel(
         make_identity(nc, ident[:])
         pos = keep.tile([P, 4, N], BF16, align_bytes=ALIGN)
         nc.vector.memset(pos[64:128].rearrange("p t d -> p (t d)").bitcast(F32), 0.0)
-        ident_b = keep.tile([P, P], BF16, align_bytes=ALIGN)
-        nc.vector.tensor_copy(out=ident_b[:], in_=ident[:])
         proj_s = keep.tile([P, 2, R], U8, align_bytes=ALIGN)
         nc.vector.memset(proj_s[:].rearrange("p b n -> p (b n)").bitcast(I32), 0)
         select = keep.tile([P, GROUPS, 2, 64], BF16, align_bytes=ALIGN)
@@ -100,18 +98,18 @@ def tile_tubelet_embed_pool_s8_kernel(
             nc.sync.dma_start(out=pos[0:64, t : t + 2], in_=space_pos.rearrange("(k t) d -> k t d", t=4)[:, t : t + 2])
 
         nc.scalar.dma_start(out=scale_k[:], in_=x_scale.rearrange("o (c p t) -> p (o c) t", p=P, t=4))
-        load_x(0, 1)
         load_w(0, 0)
-        load_x(1, 1)
         load_w(1, 0)
+        load_x(0, 1)
         load_w(2, 0)
+        load_x(1, 1)
         nc.scalar.dma_start(out=gain_raw[:], in_=gain.rearrange("(g p t) -> p g t", p=P, t=4))
-        load_x(2, 2)
         load_w(0, 1)
+        load_x(2, 2)
         load_w(1, 1)
-        load_w(2, 1)
         load_sites(0)
         nc.sync.dma_start(out=pos[64:72], in_=time_pos.unsqueeze(1).to_broadcast([T, 4, N]))
+        load_w(2, 1)
         load_sites(2)
         load_x(4, 2)
         for q in range(4):
@@ -125,7 +123,6 @@ def tile_tubelet_embed_pool_s8_kernel(
             load_x(i, 2)
 
         scale_ps = {}
-        w_ps = {}
         w_inter = {}
         x_wide = {}
         x_ps = {}
@@ -155,19 +152,6 @@ def tile_tubelet_embed_pool_s8_kernel(
                 out=scale_all[:, c * 512 : (c + 1) * 512].rearrange("p (n t) -> p n t", t=4),
                 in_=scale_ps[c][:].rearrange("p t n -> p n t"),
             )
-
-        def interleave_w(c, h, u, bank):
-            laid = bank([P, 2, 64, 2, 4], BF16)
-            w_ps[c, h, u] = laid
-            rows = w_raw[c, h][:].rearrange("p j (s q u e) -> p u s q e j", s=2, u=2, e=2)
-            for s in range(2):
-                nc.tensor.matmul(out=laid[:, s], lhsT=ident_b[:], rhs=rows[:, u, s], start=True, stop=True)
-
-        def empty_w(c, h, u):
-            if u == 0:
-                w_i = work.tile([P, 2, 2 * HALF], BF16, bufs=3, align_bytes=ALIGN)
-                w_inter[c, h] = w_i
-            nc.scalar.copy(out=w_inter[c, h][:, u], in_=w_ps[c, h, u][:].rearrange("p s q e j -> p (s q e j)"))
 
         def copy_w(c, h, copy):
             w_i = work.tile([P, 2, 2 * HALF], BF16, bufs=3, align_bytes=ALIGN)
@@ -219,7 +203,9 @@ def tile_tubelet_embed_pool_s8_kernel(
             nc.scalar.copy(out=x_inter[i][:, blocks(i, b)], in_=x_ps[i, b][:].rearrange("p c u m -> p c m u"))
 
         def quantize_x(i, b):
-            if b == 0:
+            if rides(i) and b == 0:
+                return
+            if rides(i) or b == 0:
                 if rides(i):
                     codes = keep.tile([P, PASSES + 1, P], U32, name="x_codes%d" % i, align_bytes=ALIGN)
                     scales = keep.tile([P, PASSES + 1, P], U8, name="x_scales%d" % i, align_bytes=ALIGN)
@@ -228,7 +214,7 @@ def tile_tubelet_embed_pool_s8_kernel(
                     scales = work.tile([P, PASSES, P], U8, bufs=3, align_bytes=ALIGN)
                 x_codes[i] = codes
                 x_scales[i] = scales
-            cs = blocks(i, b)
+            cs = slice(0, 4) if rides(i) else blocks(i, b)
             nc.vector.quantize_mx(
                 out=x_codes[i][:, cs].rearrange("p c m -> p (c m)").bitcast(F8X4),
                 scales=x_scales[i][:, cs].rearrange("p c m -> p (c m)"),
@@ -325,26 +311,26 @@ def tile_tubelet_embed_pool_s8_kernel(
                 )
 
         def store_features(i):
-            feats = work.tile([P, R], F32, bufs=3, align_bytes=ALIGN)
+            feats = work.tile([P, R], F32, bufs=6, align_bytes=ALIGN)
             nc.scalar.copy(out=feats[:], in_=feats_ps[i][:])
             nc.sync.dma_start(out=out_0.rearrange("(g p t) r -> g t p r", p=P, t=4)[i // 4, i % 4], in_=feats[:])
 
-        def interleave_h(n, copy, first, count):
-            g, d0 = n // 4, QUARTER * (n % 4) + first
-            if n not in ht_inter:
-                ht_i = work.tile([P, QUARTER, 4], BF16, bufs=3, align_bytes=ALIGN)
-                ht_inter[n] = ht_i
+        def interleave_h(n, copy):
+            g, d0 = n // 4, QUARTER * (n % 4)
+            if n % 2 == 0:
+                ht_i = work.tile([P, 2, QUARTER, 4], BF16, bufs=2, align_bytes=ALIGN)
+                ht_inter[n // 2] = ht_i
             copy(
-                out=ht_inter[n][:, first : first + count].rearrange("p (n i) t -> p n t i", i=4),
-                in_=h_rows[g][:, :, d0 : d0 + count].rearrange("p t (n i) -> p n t i", i=4),
+                out=ht_inter[n // 2][:, n % 2].rearrange("p (n i) t -> p n t i", i=4),
+                in_=h_rows[g][:, :, d0 : d0 + QUARTER].rearrange("p t (n i) -> p n t i", i=4),
             )
 
-        def quantize_tokens(n):
-            g, d0 = n // 4, QUARTER * (n % 4)
+        def quantize_tokens(m):
+            g, h = divmod(m, 2)
             nc.vector.quantize_mx(
-                out=h_codes[g][:, d0 : d0 + QUARTER].bitcast(F8X4),
-                scales=h_scales[g][:, d0 : d0 + QUARTER],
-                in_=ht_inter[n][:].rearrange("p d t -> p (d t)"),
+                out=h_codes[g][:, h * HALF : (h + 1) * HALF].bitcast(F8X4),
+                scales=h_scales[g][:, h * HALF : (h + 1) * HALF],
+                in_=ht_inter[m][:].rearrange("p n d t -> p (n d t)"),
             )
 
         def pool_pass(g, a, h):
@@ -361,7 +347,7 @@ def tile_tubelet_embed_pool_s8_kernel(
             )
 
         def store_latents(a, h):
-            lat = work.tile([P, HALF], F32, bufs=4, align_bytes=ALIGN)
+            lat = work.tile([P, HALF], F32, tag="feats", bufs=6, align_bytes=ALIGN)
             copy = nc.vector.tensor_copy if a == 0 else nc.scalar.copy
             copy(
                 out=lat[:].rearrange("p (q u e) -> p q u e", u=2, e=2),
@@ -371,64 +357,63 @@ def tile_tubelet_embed_pool_s8_kernel(
 
         scalar, vector = nc.scalar.copy, nc.vector.tensor_copy
 
-        def prepare_w(c, h, bank):
-            for u in range(2):
-                interleave_w(c, h, u, bank)
-                empty_w(c, h, u)
-
         for c in range(PASSES):
             spread_scale(c)
-            empty_scale(c, vector if c == 0 else scalar)
-            widen_x(0, c, 1)
-        prepare_w(0, 0, bank_out)
-        widen_x(1)
-        prepare_w(1, 0, bank_out)
+            empty_scale(c, scalar)
+        copy_w(0, 0, vector)
+        copy_w(1, 0, vector)
+        widen_x(0)
+        copy_w(2, 0, scalar)
+        quantize_w(0, 0)
         turn_x(0, 0)
         turn_x(0, 1)
+        quantize_w(1, 0)
         empty_x(0, 0)
         empty_x(0, 1)
-        quantize_w(0, 0)
-        widen_x(2)
-        prepare_w(2, 0, bank_out)
-        quantize_w(1, 0)
+        widen_x(1)
         quantize_x(0, 0)
         quantize_x(0, 1)
         quantize_w(2, 0)
+        copy_w(0, 1, scalar)
+        embed(0, 0)
+        nc.vector.tensor_copy(out=gain_col[:], in_=gain_raw[:].rearrange("p g t -> p (g t)"))
+        copy_w(1, 1, scalar)
         turn_x(1, 0)
         turn_x(1, 1)
-        empty_x(1, 0)
-        empty_x(1, 1)
-        embed(0, 0)
-        quantize_x(1, 0)
-        quantize_x(1, 1)
-        copy_w(0, 1, vector)
-        copy_w(1, 1, scalar)
+        widen_x(2)
         turn_x(2, 0)
         turn_x(2, 1)
+        quantize_w(0, 1)
+        empty_x(1, 0)
+        empty_x(1, 1)
+        place(0, 0)
+        place(1, 0)
         empty_x(2, 0)
         empty_x(2, 1)
-        embed(1, 0)
-        prepare_w(2, 1, bank_in)
-        quantize_w(0, 1)
+        copy_w(2, 1, vector)
+        quantize_x(1, 0)
+        quantize_x(1, 1)
         quantize_w(1, 1)
         quantize_x(2, 0)
         quantize_x(2, 1)
-        nc.vector.tensor_copy(out=gain_col[:], in_=gain_raw[:].rearrange("p g t -> p (g t)"))
-        place(0, 0)
-        place(1, 0)
-        embed(2, 0)
         quantize_w(2, 1)
-        scale_term(0, 0)
-        scale_term(1, 0)
-        finish_h(0, 0)
-        widen_x(3)
+        embed(1, 0)
         place(0, 1)
         place(2, 0)
+        scale_term(0, 0)
+        scale_term(1, 0)
+        embed(2, 0)
         scale_term(0, 1)
         scale_term(2, 0)
+        finish_h(0, 0)
+        widen_x(3)
         embed(0, 1)
         place(1, 1)
+        place(2, 1)
+        place(3, 0)
         scale_term(1, 1)
+        scale_term(2, 1)
+        scale_term(3, 0)
         embed(1, 1)
         finish_h(1, 0)
         finish_h(0, 1)
@@ -441,66 +426,72 @@ def tile_tubelet_embed_pool_s8_kernel(
             if not last:
                 turn_x(i, 0)
                 turn_x(i, 1)
-            if i == 3:
-                turn_h(0)
-            turn_h(i - 2)
-            if i >= 4:
-                store_features(i - 3)
+            turn_h(0 if i == 3 else i - 2)
+            if i > 3:
+                finish_h(i - 1, 0)
             if i + 1 < TILES:
                 widen_x(i + 1)
+            if i == TILES - 1:
+                interleave_h(n, vector)
             if last:
-                interleave_h(12, vector, 0, QUARTER)
+                quantize_tokens(5)
+                interleave_h(12, vector)
             if not last:
                 empty_x(i, 0)
                 empty_x(i, 1)
-            if i == 3:
-                empty_h(0)
-            empty_h(i - 2)
-            place(i - 1, 1)
-            scale_term(i - 1, 1)
-            if not last:
-                place(i, 0)
-                scale_term(i, 0)
                 quantize_x(i, 0)
                 quantize_x(i, 1)
-            if i == 3:
-                quantize_features(0)
-            quantize_features(i - 2)
-            if n >= 1:
-                quantize_tokens(n - 1)
+            empty_h(0 if i == 3 else i - 2)
+            if not last:
+                place(i, 1)
+                scale_term(i, 1)
+            if i + 1 < TILES:
+                place(i + 1, 0)
+                scale_term(i + 1, 0)
+            if i == 4:
+                project(0)
+                store_features(0)
+            if i >= 4:
+                project(i - 3)
+                store_features(i - 3)
+            if last:
+                interleave_h(13, scalar)
+            elif n >= 0 and n % 4 != 3:
+                interleave_h(n, scalar)
             embed(i - 1, 1)
             if last:
                 break
+            if i == 3:
+                turn_h(1)
+                empty_h(1)
+                quantize_features(0)
+            quantize_features(i - 2)
+            if n >= 2 and n % 2 == 0:
+                quantize_tokens(n // 2 - 1)
+            if n % 4 == 3 and 0 <= n < 11:
+                interleave_h(n, vector)
             finish_h(i - 1, 1)
             embed(i, 0)
-            if i == 3:
-                project(0)
-                store_features(0)
-            project(i - 2)
-            if n >= 0:
-                interleave_h(n, vector if n % 3 == 2 else scalar, 0, QUARTER)
-            finish_h(i, 0)
 
-        interleave_h(13, scalar, 0, QUARTER)
+        quantize_features(14)
         finish_h(15, 1)
-        for g in range(GROUPS - 1):
-            pool_pass(g, 0, 0)
-            if g == 0:
-                project(14)
-                store_features(14)
-            pool_pass(g, 1, 0)
+        pool_pass(0, 0, 0)
+        pool_pass(0, 1, 0)
+        project(14)
+        pool_pass(1, 0, 0)
+        pool_pass(1, 1, 0)
         turn_h(15)
-        interleave_h(14, vector, 0, QUARTER)
-        quantize_tokens(12)
-        quantize_tokens(13)
+        interleave_h(14, vector)
+        quantize_tokens(6)
+        store_features(14)
         empty_h(15)
-        interleave_h(15, vector, 0, QUARTER)
-        pool_pass(3, 0, 0)
-        pool_pass(3, 1, 0)
-        store_latents(1, 0)
-        quantize_tokens(14)
+        interleave_h(15, vector)
+        for g in range(2, GROUPS):
+            pool_pass(g, 0, 0)
+            pool_pass(g, 1, 0)
         quantize_features(15)
-        quantize_tokens(15)
+        quantize_tokens(7)
+        store_latents(1, 0)
         store_latents(0, 0)
         for g in range(GROUPS - 1):
             pool_pass(g, 0, 1)

@@ -25,8 +25,8 @@ TILES = M // P
 PAIRS = TILES // 2
 HALF = 512
 QUARTER = 256
-SHARE = 64
-POOL_STEP = 5
+SHARE = 80
+POOL_STEP = 3
 ALIGN = 64
 
 
@@ -98,9 +98,9 @@ def tile_tubelet_embed_pool_s8_kernel(
             nc.sync.dma_start(out=pos[0:64, t : t + 2], in_=space_pos.rearrange("(k t) d -> k t d", t=4)[:, t : t + 2])
 
         nc.scalar.dma_start(out=scale_k[:], in_=x_scale.rearrange("o (c p t) -> p (o c) t", p=P, t=4))
+        load_x(0, 1)
         load_w(0, 0)
         load_w(1, 0)
-        load_x(0, 1)
         load_w(2, 0)
         load_x(1, 1)
         nc.scalar.dma_start(out=gain_raw[:], in_=gain.rearrange("(g p t) -> p g t", p=P, t=4))
@@ -153,12 +153,13 @@ def tile_tubelet_embed_pool_s8_kernel(
                 in_=scale_ps[c][:].rearrange("p t n -> p n t"),
             )
 
-        def copy_w(c, h, copy):
-            w_i = work.tile([P, 2, 2 * HALF], BF16, bufs=3, align_bytes=ALIGN)
-            w_inter[c, h] = w_i
+        def copy_w(c, h, copy, qs=slice(0, P)):
+            if qs.start == 0:
+                w_i = work.tile([P, 2, 2 * HALF], BF16, bufs=4, align_bytes=ALIGN)
+                w_inter[c, h] = w_i
             copy(
-                out=w_i[:].rearrange("p u (q e j) -> p q j u e", e=2, j=4),
-                in_=w_raw[c, h][:].rearrange("p j (q u e) -> p q j u e", u=2, e=2),
+                out=w_inter[c, h][:].rearrange("p u (q e j) -> p q j u e", e=2, j=4)[:, qs],
+                in_=w_raw[c, h][:].rearrange("p j (q u e) -> p q j u e", u=2, e=2)[:, qs],
             )
 
         def quantize_w(c, h):
@@ -221,8 +222,8 @@ def tile_tubelet_embed_pool_s8_kernel(
                 in_=x_inter[i][:, cs].rearrange("p c m u -> p (c m u)").bitcast(BF16),
             )
 
-        def place(i, h):
-            placed = bank_in([P, HALF], F32)
+        def place(i, h, bank=bank_in):
+            placed = bank([P, HALF], F32)
             term_ps[i, h] = placed
             nc.tensor.matmul(
                 out=placed[:],
@@ -315,14 +316,14 @@ def tile_tubelet_embed_pool_s8_kernel(
             nc.scalar.copy(out=feats[:], in_=feats_ps[i][:])
             nc.sync.dma_start(out=out_0.rearrange("(g p t) r -> g t p r", p=P, t=4)[i // 4, i % 4], in_=feats[:])
 
-        def interleave_h(n, copy):
-            g, d0 = n // 4, QUARTER * (n % 4)
-            if n % 2 == 0:
+        def interleave_h(n, copy, first=0, count=QUARTER):
+            g, d0 = n // 4, QUARTER * (n % 4) + first
+            if n // 2 not in ht_inter:
                 ht_i = work.tile([P, 2, QUARTER, 4], BF16, bufs=2, align_bytes=ALIGN)
                 ht_inter[n // 2] = ht_i
             copy(
-                out=ht_inter[n // 2][:, n % 2].rearrange("p (n i) t -> p n t i", i=4),
-                in_=h_rows[g][:, :, d0 : d0 + QUARTER].rearrange("p t (n i) -> p n t i", i=4),
+                out=ht_inter[n // 2][:, n % 2, first : first + count].rearrange("p (n i) t -> p n t i", i=4),
+                in_=h_rows[g][:, :, d0 : d0 + count].rearrange("p t (n i) -> p n t i", i=4),
             )
 
         def quantize_tokens(m):
@@ -360,58 +361,59 @@ def tile_tubelet_embed_pool_s8_kernel(
         for c in range(PASSES):
             spread_scale(c)
             empty_scale(c, scalar)
-        copy_w(0, 0, vector)
-        copy_w(1, 0, vector)
-        widen_x(0)
-        copy_w(2, 0, scalar)
-        quantize_w(0, 0)
+            widen_x(0, c, 1)
+        copy_w(0, 0, scalar)
         turn_x(0, 0)
         turn_x(0, 1)
-        quantize_w(1, 0)
+        copy_w(1, 0, vector)
+        copy_w(2, 0, vector)
         empty_x(0, 0)
         empty_x(0, 1)
-        widen_x(1)
+        quantize_w(1, 0)
+        quantize_w(0, 0)
+        copy_w(0, 1, scalar)
         quantize_x(0, 0)
         quantize_x(0, 1)
         quantize_w(2, 0)
-        copy_w(0, 1, scalar)
-        embed(0, 0)
-        nc.vector.tensor_copy(out=gain_col[:], in_=gain_raw[:].rearrange("p g t -> p (g t)"))
+        widen_x(1)
         copy_w(1, 1, scalar)
+        embed(0, 0)
         turn_x(1, 0)
         turn_x(1, 1)
-        widen_x(2)
-        turn_x(2, 0)
-        turn_x(2, 1)
-        quantize_w(0, 1)
         empty_x(1, 0)
         empty_x(1, 1)
+        nc.vector.tensor_copy(out=gain_col[:], in_=gain_raw[:].rearrange("p g t -> p (g t)"))
+        widen_x(2)
         place(0, 0)
         place(1, 0)
-        empty_x(2, 0)
-        empty_x(2, 1)
-        copy_w(2, 1, vector)
+        place(0, 1, bank_out)
+        quantize_w(0, 1)
         quantize_x(1, 0)
         quantize_x(1, 1)
+        turn_x(2, 0)
+        turn_x(2, 1)
+        embed(1, 0)
+        copy_w(2, 1, scalar, slice(0, 64))
+        empty_x(2, 0)
+        empty_x(2, 1)
+        scale_term(0, 0)
+        scale_term(1, 0)
+        scale_term(0, 1)
+        copy_w(2, 1, vector, slice(64, 128))
         quantize_w(1, 1)
         quantize_x(2, 0)
         quantize_x(2, 1)
         quantize_w(2, 1)
-        embed(1, 0)
-        place(0, 1)
-        place(2, 0)
-        scale_term(0, 0)
-        scale_term(1, 0)
-        embed(2, 0)
-        scale_term(0, 1)
-        scale_term(2, 0)
         finish_h(0, 0)
-        widen_x(3)
-        embed(0, 1)
+        place(2, 0)
         place(1, 1)
+        embed(2, 0)
+        scale_term(2, 0)
+        scale_term(1, 1)
+        widen_x(3)
         place(2, 1)
         place(3, 0)
-        scale_term(1, 1)
+        embed(0, 1)
         scale_term(2, 1)
         scale_term(3, 0)
         embed(1, 1)
@@ -424,6 +426,7 @@ def tile_tubelet_embed_pool_s8_kernel(
             last = i == TILES
             n = i - 4
             if not last:
+                place(i, 1)
                 turn_x(i, 0)
                 turn_x(i, 1)
             turn_h(0 if i == 3 else i - 2)
@@ -443,11 +446,13 @@ def tile_tubelet_embed_pool_s8_kernel(
                 quantize_x(i, 1)
             empty_h(0 if i == 3 else i - 2)
             if not last:
-                place(i, 1)
                 scale_term(i, 1)
             if i + 1 < TILES:
                 place(i + 1, 0)
                 scale_term(i + 1, 0)
+            if i == 3:
+                turn_h(1)
+                empty_h(1)
             if i == 4:
                 project(0)
                 store_features(0)
@@ -456,20 +461,18 @@ def tile_tubelet_embed_pool_s8_kernel(
                 store_features(i - 3)
             if last:
                 interleave_h(13, scalar)
-            elif n >= 0 and n % 4 != 3:
-                interleave_h(n, scalar)
+            elif 0 <= n < 11:
+                interleave_h(n, scalar, SHARE, QUARTER - SHARE)
             embed(i - 1, 1)
             if last:
                 break
             if i == 3:
-                turn_h(1)
-                empty_h(1)
                 quantize_features(0)
             quantize_features(i - 2)
             if n >= 2 and n % 2 == 0:
                 quantize_tokens(n // 2 - 1)
-            if n % 4 == 3 and 0 <= n < 11:
-                interleave_h(n, vector)
+            if 0 <= n < 11:
+                interleave_h(n, vector, 0, SHARE)
             finish_h(i - 1, 1)
             embed(i, 0)
 

@@ -27,6 +27,7 @@ HALF = 512
 QUARTER = 256
 SHARE = 80
 POOL_STEP = 3
+RING = 6
 ALIGN = 64
 
 
@@ -37,14 +38,14 @@ def tile_tubelet_embed_pool_s8_kernel(
     with ExitStack() as ctx:
         keep = ctx.enter_context(tc.tile_pool(name="keep", bufs=1))
         work = ctx.enter_context(tc.tile_pool(name="work", bufs=2))
-        psum = ctx.enter_context(tc.psum_pool(name="psum", bufs=4))
+        psum = ctx.enter_context(tc.psum_pool(name="psum", bufs=RING))
         ctx.enter_context(tc.manual_schedule())
 
-        def bank_in(shape, dtype):
-            return psum.tile(shape, dtype, name="bank_in")
+        def next_bank(shape, dtype):
+            return psum.tile(shape, dtype, name="ring")
 
-        def bank_out(shape, dtype):
-            return psum.tile(shape, dtype, name="bank_out")
+        def held_bank():
+            return psum.tile([P, HALF], F32, name="held", bufs=2)
 
         ident = keep.tile([P, P], F32, align_bytes=ALIGN)
         make_identity(nc, ident[:])
@@ -142,7 +143,7 @@ def tile_tubelet_embed_pool_s8_kernel(
         latents_ps = {}
 
         def spread_scale(c):
-            spread = bank_in([P, 4, P], F32)
+            spread = next_bank([P, 4, P], F32)
             scale_ps[c] = spread
             for t in range(4):
                 nc.tensor.transpose(spread[:, t, :], scale_k[:, c, t : t + 1].to_broadcast([P, P]), ident[:])
@@ -186,7 +187,7 @@ def tile_tubelet_embed_pool_s8_kernel(
 
         def turn_x(i, b):
             cs = blocks(i, b)
-            x_turned = bank_in([P, cs.stop - cs.start, 2, P], F32)
+            x_turned = next_bank([P, cs.stop - cs.start, 2, P], F32)
             x_ps[i, b] = x_turned
             for c in range(cs.start, cs.stop):
                 if c < PASSES:
@@ -222,8 +223,8 @@ def tile_tubelet_embed_pool_s8_kernel(
                 in_=x_inter[i][:, cs].rearrange("p c m u -> p (c m u)").bitcast(BF16),
             )
 
-        def place(i, h, bank=bank_in):
-            placed = bank([P, HALF], F32)
+        def place(i, h):
+            placed = next_bank([P, HALF], F32)
             term_ps[i, h] = placed
             nc.tensor.matmul(
                 out=placed[:],
@@ -244,7 +245,7 @@ def tile_tubelet_embed_pool_s8_kernel(
             )
 
         def embed(i, h):
-            acc = bank_out([P, HALF], F32)
+            acc = held_bank() if i < 2 and h == 0 else next_bank([P, HALF], F32)
             e_ps[i, h] = acc
             for c in range(PASSES):
                 nc.tensor.matmul_mx(
@@ -274,7 +275,7 @@ def tile_tubelet_embed_pool_s8_kernel(
         def turn_h(i):
             g, t = i // 4, i % 4
             words = h_rows[g][:].rearrange("p t d -> p (t d)").bitcast(F32)
-            turned = bank_out([P, 2, 2, P], F32)
+            turned = next_bank([P, 2, 2, P], F32)
             h_ps[i] = turned
             for b in range(2):
                 for u in range(2):
@@ -282,29 +283,33 @@ def tile_tubelet_embed_pool_s8_kernel(
                     nc.tensor.transpose(turned[:, b, u, :], words[:, d0 : d0 + 128], ident[:])
 
         def empty_h(i):
-            hf_i = work.tile([P, 2, P, 2], F32, bufs=3, align_bytes=ALIGN)
-            hf_inter[i] = hf_i
-            nc.scalar.copy(out=hf_i[:], in_=h_ps[i][:].rearrange("p b u m -> p b m u"))
+            if i % 2 == 0:
+                hf_i = work.tile([P, 2, 2, P, 2], F32, bufs=2, align_bytes=ALIGN)
+                hf_inter[i // 2] = hf_i
+            nc.scalar.copy(out=hf_inter[i // 2][:, i % 2], in_=h_ps[i][:].rearrange("p b u m -> p b m u"))
 
-        def quantize_features(i):
-            codes_f = work.tile([P, 2, P], U32, bufs=2, align_bytes=ALIGN)
-            scales_f = work.tile([P, 2, P], U8, bufs=2, align_bytes=ALIGN)
-            hf_codes[i] = codes_f
-            hf_scales[i] = scales_f
+        def quantize_features(first, count):
+            j = first // 2
+            if first % 2 == 0:
+                codes_f = work.tile([P, 2, 2, P], U32, bufs=2, align_bytes=ALIGN)
+                scales_f = work.tile([P, 2, 2, P], U8, bufs=2, align_bytes=ALIGN)
+                hf_codes[j] = codes_f
+                hf_scales[j] = scales_f
+            ss = slice(first % 2, first % 2 + count)
             nc.vector.quantize_mx(
-                out=codes_f[:].rearrange("p b m -> p (b m)").bitcast(F8X4),
-                scales=scales_f[:].rearrange("p b m -> p (b m)"),
-                in_=hf_inter[i][:].rearrange("p b m u -> p (b m u)").bitcast(BF16),
+                out=hf_codes[j][:, ss].rearrange("p s b m -> p (s b m)").bitcast(F8X4),
+                scales=hf_scales[j][:, ss].rearrange("p s b m -> p (s b m)"),
+                in_=hf_inter[j][:, ss].rearrange("p s b m u -> p (s b m u)").bitcast(BF16),
             )
 
         def project(i):
-            projected = bank_out([P, R], F32)
+            projected = next_bank([P, R], F32)
             feats_ps[i] = projected
             for b in range(2):
                 nc.tensor.matmul_mx(
                     out=projected[:],
-                    lhsT=hf_codes[i][:, b].bitcast(F8X4),
-                    lhsT_scale=hf_scales[i][:, b],
+                    lhsT=hf_codes[i // 2][:, i % 2, b].bitcast(F8X4),
+                    lhsT_scale=hf_scales[i // 2][:, i % 2, b],
                     rhs=proj_w[:, b].bitcast(F4X4),
                     rhs_scale=proj_s[:, b],
                     start=(b == 0),
@@ -319,7 +324,7 @@ def tile_tubelet_embed_pool_s8_kernel(
         def interleave_h(n, copy, first=0, count=QUARTER):
             g, d0 = n // 4, QUARTER * (n % 4) + first
             if n // 2 not in ht_inter:
-                ht_i = work.tile([P, 2, QUARTER, 4], BF16, bufs=2, align_bytes=ALIGN)
+                ht_i = work.tile([P, 2, QUARTER, 4], BF16, tag="w_i", bufs=4, align_bytes=ALIGN)
                 ht_inter[n // 2] = ht_i
             copy(
                 out=ht_inter[n // 2][:, n % 2, first : first + count].rearrange("p (n i) t -> p n t i", i=4),
@@ -335,8 +340,10 @@ def tile_tubelet_embed_pool_s8_kernel(
             )
 
         def pool_pass(g, a, h):
-            if g == 0:
-                latents_ps[a, h] = bank_in([P, HALF], F32)
+            if g == 0 and h == 0:
+                latents_ps[a, h] = held_bank()
+            elif g == 0:
+                latents_ps[a, h] = next_bank([P, HALF], F32)
             nc.tensor.matmul_mx(
                 out=latents_ps[a, h][:],
                 lhsT=x_codes[POOL_STEP + 2 * g + a][:, PASSES].bitcast(F8X4),
@@ -349,7 +356,7 @@ def tile_tubelet_embed_pool_s8_kernel(
 
         def store_latents(a, h):
             lat = work.tile([P, HALF], F32, tag="feats", bufs=6, align_bytes=ALIGN)
-            copy = nc.vector.tensor_copy if a == 0 else nc.scalar.copy
+            copy = nc.vector.tensor_copy if (a, h) == (0, 1) else nc.scalar.copy
             copy(
                 out=lat[:].rearrange("p (q u e) -> p q u e", u=2, e=2),
                 in_=latents_ps[a, h][:].rearrange("p (u q e) -> p q u e", u=2, e=2),
@@ -386,7 +393,7 @@ def tile_tubelet_embed_pool_s8_kernel(
         widen_x(2)
         place(0, 0)
         place(1, 0)
-        place(0, 1, bank_out)
+        place(0, 1)
         quantize_w(0, 1)
         quantize_x(1, 0)
         quantize_x(1, 1)
@@ -417,12 +424,12 @@ def tile_tubelet_embed_pool_s8_kernel(
         scale_term(2, 1)
         scale_term(3, 0)
         embed(1, 1)
-        finish_h(1, 0)
-        finish_h(0, 1)
         finish_h(2, 0)
+        finish_h(0, 1)
+        finish_h(1, 0)
         finish_h(1, 1)
 
-        for i in range(3, TILES + 1):
+        for i in range(3, TILES - 1):
             last = i == TILES
             n = i - 4
             if not last:
@@ -434,74 +441,104 @@ def tile_tubelet_embed_pool_s8_kernel(
                 finish_h(i - 1, 0)
             if i + 1 < TILES:
                 widen_x(i + 1)
-            if i == TILES - 1:
-                interleave_h(n, vector)
             if last:
                 quantize_tokens(5)
                 interleave_h(12, vector)
             if not last:
+                scale_term(i, 1)
                 empty_x(i, 0)
                 empty_x(i, 1)
                 quantize_x(i, 0)
                 quantize_x(i, 1)
             empty_h(0 if i == 3 else i - 2)
-            if not last:
-                scale_term(i, 1)
             if i + 1 < TILES:
                 place(i + 1, 0)
                 scale_term(i + 1, 0)
             if i == 3:
                 turn_h(1)
                 empty_h(1)
-            if i == 4:
-                project(0)
-                store_features(0)
             if i >= 4:
-                project(i - 3)
-                store_features(i - 3)
+                project(i - 4)
+                store_features(i - 4)
             if last:
                 interleave_h(13, scalar)
+            elif n == 11:
+                interleave_h(n, scalar)
             elif 0 <= n < 11:
                 interleave_h(n, scalar, SHARE, QUARTER - SHARE)
+            if i % 4 == 3 and i > 3:
+                pool_pass(i // 4 - 1, 0, 0)
+                pool_pass(i // 4 - 1, 1, 0)
             embed(i - 1, 1)
             if last:
                 break
-            if i == 3:
-                quantize_features(0)
-            quantize_features(i - 2)
-            if n >= 2 and n % 2 == 0:
+            if i > 3 and i % 2 == 1:
+                quantize_features(i - 3, 2)
+            if 2 <= n < 8 and n % 2 == 0:
                 quantize_tokens(n // 2 - 1)
             if 0 <= n < 11:
                 interleave_h(n, vector, 0, SHARE)
             finish_h(i - 1, 1)
+            if i == 3:
+                quantize_features(0, 2)
             embed(i, 0)
 
-        quantize_features(14)
+        place(15, 1)
+        turn_x(15, 0)
+        turn_x(15, 1)
+        turn_h(13)
+        finish_h(14, 0)
+        quantize_tokens(3)
+        empty_x(15, 0)
+        empty_x(15, 1)
+        quantize_x(15, 0)
+        quantize_x(15, 1)
+        scale_term(15, 1)
+        empty_h(13)
+        project(11)
+        embed(14, 1)
+        quantize_tokens(4)
+        finish_h(14, 1)
+        embed(15, 0)
+        store_features(11)
+        interleave_h(11, scalar)
+        quantize_features(12, 2)
+        embed(15, 1)
+        finish_h(15, 0)
         finish_h(15, 1)
-        pool_pass(0, 0, 0)
-        pool_pass(0, 1, 0)
-        project(14)
-        pool_pass(1, 0, 0)
-        pool_pass(1, 1, 0)
+        project(12)
+        turn_h(14)
         turn_h(15)
-        interleave_h(14, vector)
-        quantize_tokens(6)
-        store_features(14)
+        interleave_h(12, vector)
+        interleave_h(13, scalar)
+        project(13)
+        pool_pass(2, 0, 0)
+        pool_pass(2, 1, 0)
+        store_features(12)
+        empty_h(14)
         empty_h(15)
-        interleave_h(15, vector)
-        for g in range(2, GROUPS):
-            pool_pass(g, 0, 0)
-            pool_pass(g, 1, 0)
-        quantize_features(15)
-        quantize_tokens(7)
-        store_latents(1, 0)
-        store_latents(0, 0)
-        for g in range(GROUPS - 1):
+        quantize_tokens(5)
+        quantize_tokens(6)
+        interleave_h(14, vector)
+        for g in range(2):
             pool_pass(g, 0, 1)
+            pool_pass(g, 1, 1)
+        pool_pass(3, 0, 0)
+        pool_pass(3, 1, 0)
+        store_features(13)
+        quantize_features(14, 1)
+        interleave_h(15, vector)
+        store_latents(0, 0)
+        store_latents(1, 0)
+        project(14)
+        quantize_features(15, 1)
+        quantize_tokens(7)
+        pool_pass(2, 0, 1)
+        pool_pass(2, 1, 1)
         project(15)
+        store_features(14)
         pool_pass(3, 0, 1)
+        pool_pass(3, 1, 1)
         store_features(15)
         store_latents(0, 1)
-        for g in range(GROUPS):
-            pool_pass(g, 1, 1)
         store_latents(1, 1)

@@ -25,9 +25,9 @@ TILES = M // P
 PAIRS = TILES // 2
 HALF = 512
 QUARTER = 256
-SHARE = 80
-POOL_STEP = 3
-RING = 6
+XB = 4
+TB = 8
+BANKS = 8
 ALIGN = 64
 
 
@@ -38,14 +38,19 @@ def tile_tubelet_embed_pool_s8_kernel(
     with ExitStack() as ctx:
         keep = ctx.enter_context(tc.tile_pool(name="keep", bufs=1))
         work = ctx.enter_context(tc.tile_pool(name="work", bufs=2))
-        psum = ctx.enter_context(tc.psum_pool(name="psum", bufs=RING))
+        psum = ctx.enter_context(tc.psum_pool(name="psum", bufs=1))
         ctx.enter_context(tc.manual_schedule())
 
-        def next_bank(shape, dtype):
-            return psum.tile(shape, dtype, name="ring")
+        free_banks = list(range(BANKS))
+        bank_of = {}
 
-        def held_bank():
-            return psum.tile([P, HALF], F32, name="held", bufs=2)
+        def next_bank(key, shape):
+            bank_of[key] = free_banks[0]
+            free_banks.remove(bank_of[key])
+            return psum.tile(shape, F32, name="bank%d" % bank_of[key])
+
+        def release(key):
+            free_banks.append(bank_of[key])
 
         ident = keep.tile([P, P], F32, align_bytes=ALIGN)
         make_identity(nc, ident[:])
@@ -65,8 +70,7 @@ def tile_tubelet_embed_pool_s8_kernel(
         x_raw = []
         for s in range(PAIRS):
             x_raw.append(keep.tile([P, 2, K], U8, name="x_raw%d" % s, align_bytes=ALIGN))
-        scale_all = keep.tile([P, K], F32, align_bytes=ALIGN)
-        scale_k = keep.tile([P, PASSES, 4], F32)
+        scale_k = keep.tile([P, PASSES, 4], F32, align_bytes=ALIGN)
         gain_raw = keep.tile([P, GROUPS, 4], BF16)
         gain_col = keep.tile([P, TILES], F32, align_bytes=ALIGN)
         pool_raw = keep.tile([P, 2, M], BF16, align_bytes=ALIGN)
@@ -79,6 +83,8 @@ def tile_tubelet_embed_pool_s8_kernel(
                 w_raw[c, h] = keep.tile([P, 4, HALF], BF16, name="w_raw%d%d" % (c, h), align_bytes=ALIGN)
                 w_codes[c, h] = keep.tile([P, HALF], U32, name="w_codes%d%d" % (c, h), align_bytes=ALIGN)
                 w_scales[c, h] = keep.tile([P, HALF], U8, name="w_scales%d%d" % (c, h), align_bytes=ALIGN)
+        pool_codes = keep.tile([P, GROUPS, 2, P], U32, align_bytes=ALIGN)
+        pool_scales = keep.tile([P, GROUPS, 2, P], U8, align_bytes=ALIGN)
         h_codes = []
         h_scales = []
         for g in range(GROUPS):
@@ -99,18 +105,18 @@ def tile_tubelet_embed_pool_s8_kernel(
             nc.sync.dma_start(out=pos[0:64, t : t + 2], in_=space_pos.rearrange("(k t) d -> k t d", t=4)[:, t : t + 2])
 
         nc.scalar.dma_start(out=scale_k[:], in_=x_scale.rearrange("o (c p t) -> p (o c) t", p=P, t=4))
-        load_x(0, 1)
         load_w(0, 0)
+        load_x(0, 1)
         load_w(1, 0)
         load_w(2, 0)
         load_x(1, 1)
         nc.scalar.dma_start(out=gain_raw[:], in_=gain.rearrange("(g p t) -> p g t", p=P, t=4))
         load_w(0, 1)
-        load_x(2, 2)
         load_w(1, 1)
+        load_x(2, 2)
+        load_w(2, 1)
         load_sites(0)
         nc.sync.dma_start(out=pos[64:72], in_=time_pos.unsqueeze(1).to_broadcast([T, 4, N]))
-        load_w(2, 1)
         load_sites(2)
         load_x(4, 2)
         for q in range(4):
@@ -123,7 +129,8 @@ def tile_tubelet_embed_pool_s8_kernel(
         for i in range(6, TILES, 2):
             load_x(i, 2)
 
-        scale_ps = {}
+        pool_ps = {}
+        pool_inter = {}
         w_inter = {}
         x_wide = {}
         x_ps = {}
@@ -142,89 +149,94 @@ def tile_tubelet_embed_pool_s8_kernel(
         ht_inter = {}
         latents_ps = {}
 
-        def spread_scale(c):
-            spread = next_bank([P, 4, P], F32)
-            scale_ps[c] = spread
-            for t in range(4):
-                nc.tensor.transpose(spread[:, t, :], scale_k[:, c, t : t + 1].to_broadcast([P, P]), ident[:])
+        def gpsimd_copy(out, in_):
+            nc.gpsimd.tensor_scalar(out=out, in0=in_, scalar1=1.0, scalar2=0.0, op0=MULT, op1=ADD)
 
-        def empty_scale(c, copy):
-            copy(
-                out=scale_all[:, c * 512 : (c + 1) * 512].rearrange("p (n t) -> p n t", t=4),
-                in_=scale_ps[c][:].rearrange("p t n -> p n t"),
-            )
+        def copy_w(c, h, u, copy):
+            if copy is gpsimd_copy or (c, h, u) == (0, 0, 0):
+                plane = work.tile([P, P, 2, 4], BF16, tag="gated", bufs=1, align_bytes=ALIGN)
+            else:
+                plane = work.tile([P, P, 2, 4], BF16, tag="plane", bufs=5, align_bytes=ALIGN)
+            w_inter[c, h, u] = plane
+            rows = w_raw[c, h][:].rearrange("p j (q u e) -> p u q e j", u=2, e=2)[:, u]
+            if copy is gpsimd_copy:
+                copy(out=plane[:], in_=rows)
+            else:
+                copy(out=plane[:].rearrange("p q e j -> p q j e"), in_=rows.rearrange("p q e j -> p q j e"))
 
-        def copy_w(c, h, copy, qs=slice(0, P)):
-            if qs.start == 0:
-                w_i = work.tile([P, 2, 2 * HALF], BF16, bufs=4, align_bytes=ALIGN)
-                w_inter[c, h] = w_i
-            copy(
-                out=w_inter[c, h][:].rearrange("p u (q e j) -> p q j u e", e=2, j=4)[:, qs],
-                in_=w_raw[c, h][:].rearrange("p j (q u e) -> p q j u e", u=2, e=2)[:, qs],
-            )
-
-        def quantize_w(c, h):
+        def quantize_w(c, h, u):
+            ns = slice(u * QUARTER, (u + 1) * QUARTER)
             nc.vector.quantize_mx(
-                out=w_codes[c, h][:].bitcast(F8X4),
-                scales=w_scales[c, h][:],
-                in_=w_inter[c, h][:].rearrange("p u n -> p (u n)"),
+                out=w_codes[c, h][:, ns].bitcast(F8X4),
+                scales=w_scales[c, h][:, ns],
+                in_=w_inter[c, h, u][:].rearrange("p q e j -> p (q e j)"),
             )
-
-        def rides(i):
-            return POOL_STEP <= i < POOL_STEP + 2 * GROUPS
-
-        def blocks(i, b):
-            return slice(0, 2) if b == 0 else slice(2, 4 if rides(i) else 3)
 
         def widen_x(i, first=0, count=PASSES):
             if first == 0:
                 wide = work.tile([P, K], BF16, bufs=3, align_bytes=ALIGN)
                 x_wide[i] = wide
             ks = slice(512 * first, 512 * (first + count))
-            nc.vector.tensor_tensor(
-                out=x_wide[i][:, ks], in0=x_raw[i // 2][:, i % 2, ks].bitcast(F8), in1=scale_all[:, ks], op=MULT
-            )
+            nc.scalar.copy(out=x_wide[i][:, ks], in_=x_raw[i // 2][:, i % 2, ks].bitcast(F8))
+
+        def turn_words(bank, words):
+            for u in range(2):
+                nc.tensor.transpose(bank[:, u, :], words[:, u:256:2], ident[:])
 
         def turn_x(i, b):
-            cs = blocks(i, b)
-            x_turned = next_bank([P, cs.stop - cs.start, 2, P], F32)
-            x_ps[i, b] = x_turned
-            for c in range(cs.start, cs.stop):
-                if c < PASSES:
-                    words = x_wide[i][:].bitcast(F32)[:, 256 * c : 256 * (c + 1)]
-                else:
-                    g, a = divmod(i - POOL_STEP, 2)
-                    words = pool_raw[:, a].bitcast(F32)[:, 256 * g : 256 * (g + 1)]
-                for u in range(2):
-                    nc.tensor.transpose(x_turned[:, c - cs.start, u, :], words[:, u:256:2], ident[:])
+            cs = range(0, 2) if b == 0 else range(2, 3)
+            x_turned = next_bank(("x", i, b), [P, len(cs), 2, P])
+            for c in cs:
+                x_ps[i, c] = x_turned[:, c - cs.start]
+                turn_words(x_ps[i, c], x_wide[i][:].bitcast(F32)[:, 256 * c : 256 * (c + 1)])
 
-        def empty_x(i, b):
-            if b == 0:
-                x_i = work.tile([P, PASSES + 1, P, 2], F32, bufs=3, align_bytes=ALIGN)
+        def scale_x(i, c):
+            if c == 0:
+                x_i = work.tile([P, PASSES, P, 4], BF16, bufs=3, align_bytes=ALIGN)
                 x_inter[i] = x_i
-            nc.scalar.copy(out=x_inter[i][:, blocks(i, b)], in_=x_ps[i, b][:].rearrange("p c u m -> p c m u"))
+            nc.vector.tensor_tensor(
+                out=x_inter[i][:, c].rearrange("p m (u e) -> p m u e", e=2),
+                in0=x_ps[i, c].bitcast(BF16).rearrange("p u (m e) -> p m u e", e=2),
+                in1=scale_k[:, c].rearrange("p (u e) -> p u e", e=2).unsqueeze(1).to_broadcast([P, P, 2, 2]),
+                op=MULT,
+            )
+            if c > 0:
+                release(("x", i, c - 1))
 
-        def quantize_x(i, b):
-            if rides(i) and b == 0:
-                return
-            if rides(i) or b == 0:
-                if rides(i):
-                    codes = keep.tile([P, PASSES + 1, P], U32, name="x_codes%d" % i, align_bytes=ALIGN)
-                    scales = keep.tile([P, PASSES + 1, P], U8, name="x_scales%d" % i, align_bytes=ALIGN)
-                else:
-                    codes = work.tile([P, PASSES, P], U32, bufs=3, align_bytes=ALIGN)
-                    scales = work.tile([P, PASSES, P], U8, bufs=3, align_bytes=ALIGN)
+        def quantize_x(i, first, count):
+            if first == 0:
+                codes = work.tile([P, PASSES, P], U32, bufs=XB, align_bytes=ALIGN)
+                scales = work.tile([P, PASSES, P], U8, bufs=XB, align_bytes=ALIGN)
                 x_codes[i] = codes
                 x_scales[i] = scales
-            cs = slice(0, 4) if rides(i) else blocks(i, b)
+            cs = slice(first, first + count)
             nc.vector.quantize_mx(
                 out=x_codes[i][:, cs].rearrange("p c m -> p (c m)").bitcast(F8X4),
                 scales=x_scales[i][:, cs].rearrange("p c m -> p (c m)"),
-                in_=x_inter[i][:, cs].rearrange("p c m u -> p (c m u)").bitcast(BF16),
+                in_=x_inter[i][:, cs].rearrange("p c m t -> p (c m t)"),
+            )
+
+        def turn_pool(g, a):
+            pool_turned = next_bank(("pool", g, a), [P, 2, P])
+            pool_ps[g, a] = pool_turned
+            turn_words(pool_turned, pool_raw[:, a].bitcast(F32)[:, 256 * g : 256 * (g + 1)])
+
+        def empty_pool(g, a):
+            if a == 0:
+                pool_i = work.tile([P, 2, P, 2], F32, bufs=2, align_bytes=ALIGN)
+                pool_inter[g] = pool_i
+            nc.scalar.copy(out=pool_inter[g][:, a], in_=pool_ps[g, a][:].rearrange("p u m -> p m u"))
+            release(("pool", g, a))
+
+        def quantize_pool(g):
+            nc.vector.quantize_mx(
+                out=pool_codes[:, g].rearrange("p a m -> p (a m)").bitcast(F8X4),
+                scales=pool_scales[:, g].rearrange("p a m -> p (a m)"),
+                in_=pool_inter[g][:].rearrange("p a m u -> p (a m u)").bitcast(BF16),
             )
 
         def place(i, h):
-            placed = next_bank([P, HALF], F32)
+            placed = next_bank(("term", i, h), [P, HALF])
             term_ps[i, h] = placed
             nc.tensor.matmul(
                 out=placed[:],
@@ -235,7 +247,7 @@ def tile_tubelet_embed_pool_s8_kernel(
             )
 
         def scale_term(i, h):
-            term_i = work.tile([P, HALF], F32, bufs=6, align_bytes=ALIGN)
+            term_i = work.tile([P, HALF], F32, bufs=TB, align_bytes=ALIGN)
             term[i, h] = term_i
             nc.scalar.activation(
                 out=term_i[:].rearrange("p (u q e) -> p u q e", u=2, e=2),
@@ -243,11 +255,13 @@ def tile_tubelet_embed_pool_s8_kernel(
                 func=COPY,
                 scale=gain_col[:, i : i + 1],
             )
+            release(("term", i, h))
 
-        def embed(i, h):
-            acc = held_bank() if i < 2 and h == 0 else next_bank([P, HALF], F32)
-            e_ps[i, h] = acc
-            for c in range(PASSES):
+        def embed(i, h, first=0, count=PASSES):
+            if first == 0:
+                e_ps[i, h] = next_bank(("e", i, h), [P, HALF])
+            acc = e_ps[i, h]
+            for c in range(first, first + count):
                 nc.tensor.matmul_mx(
                     out=acc[:],
                     lhsT=x_codes[i][:, c].bitcast(F8X4),
@@ -271,11 +285,12 @@ def tile_tubelet_embed_pool_s8_kernel(
                 op0=MULT,
                 op1=ADD,
             )
+            release(("e", i, h))
 
         def turn_h(i):
             g, t = i // 4, i % 4
             words = h_rows[g][:].rearrange("p t d -> p (t d)").bitcast(F32)
-            turned = next_bank([P, 2, 2, P], F32)
+            turned = next_bank(("h", i), [P, 2, 2, P])
             h_ps[i] = turned
             for b in range(2):
                 for u in range(2):
@@ -287,6 +302,7 @@ def tile_tubelet_embed_pool_s8_kernel(
                 hf_i = work.tile([P, 2, 2, P, 2], F32, bufs=2, align_bytes=ALIGN)
                 hf_inter[i // 2] = hf_i
             nc.scalar.copy(out=hf_inter[i // 2][:, i % 2], in_=h_ps[i][:].rearrange("p b u m -> p b m u"))
+            release(("h", i))
 
         def quantize_features(first, count):
             j = first // 2
@@ -303,7 +319,7 @@ def tile_tubelet_embed_pool_s8_kernel(
             )
 
         def project(i):
-            projected = next_bank([P, R], F32)
+            projected = next_bank(("feats", i), [P, R])
             feats_ps[i] = projected
             for b in range(2):
                 nc.tensor.matmul_mx(
@@ -316,229 +332,228 @@ def tile_tubelet_embed_pool_s8_kernel(
                     stop=(b == 1),
                 )
 
-        def store_features(i):
+        def store_features(i, copy=nc.scalar.copy):
             feats = work.tile([P, R], F32, bufs=6, align_bytes=ALIGN)
-            nc.scalar.copy(out=feats[:], in_=feats_ps[i][:])
+            copy(out=feats[:], in_=feats_ps[i][:])
+            release(("feats", i))
             nc.sync.dma_start(out=out_0.rearrange("(g p t) r -> g t p r", p=P, t=4)[i // 4, i % 4], in_=feats[:])
 
-        def interleave_h(n, copy, first=0, count=QUARTER):
-            g, d0 = n // 4, QUARTER * (n % 4) + first
-            if n // 2 not in ht_inter:
-                ht_i = work.tile([P, 2, QUARTER, 4], BF16, tag="w_i", bufs=4, align_bytes=ALIGN)
-                ht_inter[n // 2] = ht_i
-            copy(
-                out=ht_inter[n // 2][:, n % 2, first : first + count].rearrange("p (n i) t -> p n t i", i=4),
-                in_=h_rows[g][:, :, d0 : d0 + count].rearrange("p t (n i) -> p n t i", i=4),
-            )
+        def interleave_h(n, copy):
+            g, d0 = n // 4, QUARTER * (n % 4)
+            if copy is gpsimd_copy:
+                ht_i = work.tile([P, QUARTER, 4], BF16, tag="gated", bufs=1, align_bytes=ALIGN)
+            else:
+                ht_i = work.tile([P, QUARTER, 4], BF16, tag="plane", bufs=5, align_bytes=ALIGN)
+            ht_inter[n] = ht_i
+            if copy is gpsimd_copy:
+                copy(out=ht_i[:], in_=h_rows[g][:, :, d0 : d0 + QUARTER].rearrange("p t d -> p d t"))
+            else:
+                copy(
+                    out=ht_i[:].rearrange("p (n i) t -> p n t i", i=4),
+                    in_=h_rows[g][:, :, d0 : d0 + QUARTER].rearrange("p t (n i) -> p n t i", i=4),
+                )
 
-        def quantize_tokens(m):
-            g, h = divmod(m, 2)
+        def quantize_tokens(n):
+            g, d0 = n // 4, QUARTER * (n % 4)
             nc.vector.quantize_mx(
-                out=h_codes[g][:, h * HALF : (h + 1) * HALF].bitcast(F8X4),
-                scales=h_scales[g][:, h * HALF : (h + 1) * HALF],
-                in_=ht_inter[m][:].rearrange("p n d t -> p (n d t)"),
+                out=h_codes[g][:, d0 : d0 + QUARTER].bitcast(F8X4),
+                scales=h_scales[g][:, d0 : d0 + QUARTER],
+                in_=ht_inter[n][:].rearrange("p d t -> p (d t)"),
             )
 
         def pool_pass(g, a, h):
-            if g == 0 and h == 0:
-                latents_ps[a, h] = held_bank()
-            elif g == 0:
-                latents_ps[a, h] = next_bank([P, HALF], F32)
+            if g == 0:
+                latents_ps[a, h] = next_bank(("latents", a, h), [P, HALF])
             nc.tensor.matmul_mx(
                 out=latents_ps[a, h][:],
-                lhsT=x_codes[POOL_STEP + 2 * g + a][:, PASSES].bitcast(F8X4),
-                lhsT_scale=x_scales[POOL_STEP + 2 * g + a][:, PASSES],
+                lhsT=pool_codes[:, g, a].bitcast(F8X4),
+                lhsT_scale=pool_scales[:, g, a],
                 rhs=h_codes[g][:, h * HALF : (h + 1) * HALF].bitcast(F8X4),
                 rhs_scale=h_scales[g][:, h * HALF : (h + 1) * HALF],
                 start=(g == 0),
                 stop=(g == GROUPS - 1),
             )
 
-        def store_latents(a, h):
+        def store_latents(a, h, copy):
             lat = work.tile([P, HALF], F32, tag="feats", bufs=6, align_bytes=ALIGN)
-            copy = nc.vector.tensor_copy if (a, h) == (0, 1) else nc.scalar.copy
             copy(
                 out=lat[:].rearrange("p (q u e) -> p q u e", u=2, e=2),
                 in_=latents_ps[a, h][:].rearrange("p (u q e) -> p q u e", u=2, e=2),
             )
+            release(("latents", a, h))
             nc.sync.dma_start(out=out_1[a * P : (a + 1) * P, h * HALF : (h + 1) * HALF], in_=lat[:])
 
         scalar, vector = nc.scalar.copy, nc.vector.tensor_copy
 
-        for c in range(PASSES):
-            spread_scale(c)
-            empty_scale(c, scalar)
-            widen_x(0, c, 1)
-        copy_w(0, 0, scalar)
+        def prepare_x(i):
+            for c in range(PASSES):
+                scale_x(i, c)
+
+        def quantize_all_x(i):
+            quantize_x(i, 0, 2)
+            quantize_x(i, 2, 1)
+
+        copy_w(0, 0, 0, vector)
+        copy_w(0, 0, 1, vector)
+        widen_x(0, 0, 2)
         turn_x(0, 0)
+        widen_x(0, 2, 1)
         turn_x(0, 1)
-        copy_w(1, 0, vector)
-        copy_w(2, 0, vector)
-        empty_x(0, 0)
-        empty_x(0, 1)
-        quantize_w(1, 0)
-        quantize_w(0, 0)
-        copy_w(0, 1, scalar)
-        quantize_x(0, 0)
-        quantize_x(0, 1)
-        quantize_w(2, 0)
+        quantize_w(0, 0, 0)
+        quantize_w(0, 0, 1)
+        copy_w(1, 0, 0, gpsimd_copy)
+        copy_w(1, 0, 1, scalar)
+        prepare_x(0)
+        copy_w(2, 0, 0, scalar)
         widen_x(1)
-        copy_w(1, 1, scalar)
-        embed(0, 0)
+        copy_w(2, 0, 1, vector)
+        quantize_all_x(0)
         turn_x(1, 0)
         turn_x(1, 1)
-        empty_x(1, 0)
-        empty_x(1, 1)
-        nc.vector.tensor_copy(out=gain_col[:], in_=gain_raw[:].rearrange("p g t -> p (g t)"))
+        quantize_w(1, 0, 1)
+        quantize_w(2, 0, 0)
+        quantize_w(2, 0, 1)
+        quantize_w(1, 0, 0)
+        embed(0, 0)
+        copy_w(0, 1, 0, gpsimd_copy)
+        copy_w(0, 1, 1, scalar)
+        prepare_x(1)
+        copy_w(1, 1, 0, scalar)
         widen_x(2)
-        place(0, 0)
-        place(1, 0)
-        place(0, 1)
-        quantize_w(0, 1)
-        quantize_x(1, 0)
-        quantize_x(1, 1)
         turn_x(2, 0)
         turn_x(2, 1)
+        copy_w(1, 1, 1, scalar)
+        nc.vector.tensor_copy(out=gain_col[:], in_=gain_raw[:].rearrange("p g t -> p (g t)"))
+        quantize_all_x(1)
+        quantize_w(0, 1, 1)
+        quantize_w(1, 1, 0)
+        quantize_w(0, 1, 0)
         embed(1, 0)
-        copy_w(2, 1, scalar, slice(0, 64))
-        empty_x(2, 0)
-        empty_x(2, 1)
-        scale_term(0, 0)
-        scale_term(1, 0)
-        scale_term(0, 1)
-        copy_w(2, 1, vector, slice(64, 128))
-        quantize_w(1, 1)
-        quantize_x(2, 0)
-        quantize_x(2, 1)
-        quantize_w(2, 1)
-        finish_h(0, 0)
-        place(2, 0)
-        place(1, 1)
-        embed(2, 0)
-        scale_term(2, 0)
-        scale_term(1, 1)
+        copy_w(2, 1, 1, gpsimd_copy)
+        prepare_x(2)
+        embed(0, 1, 0, 1)
+        embed(1, 1, 0, 1)
+        copy_w(2, 1, 0, scalar)
         widen_x(3)
+        place(0, 0)
+        place(1, 0)
+        scale_term(0, 0)
+        turn_x(3, 0)
+        turn_x(3, 1)
+        scale_term(1, 0)
+        quantize_w(1, 1, 1)
+        quantize_all_x(2)
+        quantize_w(2, 1, 0)
+        quantize_w(2, 1, 1)
+        finish_h(0, 0)
+        place(0, 1)
+        embed(0, 1, 1, 1)
+        embed(1, 1, 1, 1)
+        place(1, 1)
+        scale_term(0, 1)
+        scale_term(1, 1)
+        embed(0, 1, 2, 1)
+        embed(1, 1, 2, 1)
+        prepare_x(3)
+        widen_x(4)
+        place(2, 0)
+        embed(2, 0)
         place(2, 1)
-        place(3, 0)
-        embed(0, 1)
-        scale_term(2, 1)
-        scale_term(3, 0)
-        embed(1, 1)
-        finish_h(2, 0)
-        finish_h(0, 1)
+        scale_term(2, 0)
         finish_h(1, 0)
+        quantize_all_x(3)
+        scale_term(2, 1)
+        finish_h(0, 1)
+        embed(2, 1)
+        place(3, 0)
+        place(3, 1)
         finish_h(1, 1)
+        scale_term(3, 0)
+        scale_term(3, 1)
+        finish_h(2, 0)
 
-        for i in range(3, TILES - 1):
-            last = i == TILES
+        for i in range(3, TILES):
             n = i - 4
-            if not last:
-                place(i, 1)
-                turn_x(i, 0)
-                turn_x(i, 1)
-            turn_h(0 if i == 3 else i - 2)
-            if i > 3:
-                finish_h(i - 1, 0)
-            if i + 1 < TILES:
-                widen_x(i + 1)
-            if last:
-                quantize_tokens(5)
-                interleave_h(12, vector)
-            if not last:
-                scale_term(i, 1)
-                empty_x(i, 0)
-                empty_x(i, 1)
-                quantize_x(i, 0)
-                quantize_x(i, 1)
-            empty_h(0 if i == 3 else i - 2)
-            if i + 1 < TILES:
+            ahead = i + 1 < TILES
+            if ahead:
                 place(i + 1, 0)
+                turn_x(i + 1, 0)
+                turn_x(i + 1, 1)
+            if n >= 0:
+                interleave_h(n, gpsimd_copy)
+            finish_h(i - 1, 1)
+            turn_h(i - 3 if i < 5 else i - 2)
+            if i == 4:
+                turn_h(2)
+            if 5 <= i < 5 + 2 * GROUPS:
+                turn_pool(*divmod(i - 5, 2))
+            if ahead:
                 scale_term(i + 1, 0)
-            if i == 3:
-                turn_h(1)
-                empty_h(1)
-            if i >= 4:
+                place(i + 1, 1)
+                prepare_x(i + 1)
+            empty_h(i - 3 if i < 5 else i - 2)
+            if ahead:
+                scale_term(i + 1, 1)
+            if i == 4:
+                quantize_features(0, 2)
+                empty_h(2)
+            if 5 <= i < 5 + 2 * GROUPS:
+                empty_pool(*divmod(i - 5, 2))
+            if i == 5:
+                project(0)
+                store_features(0)
+            if i >= 5:
                 project(i - 4)
                 store_features(i - 4)
-            if last:
-                interleave_h(13, scalar)
-            elif n == 11:
-                interleave_h(n, scalar)
-            elif 0 <= n < 11:
-                interleave_h(n, scalar, SHARE, QUARTER - SHARE)
-            if i % 4 == 3 and i > 3:
-                pool_pass(i // 4 - 1, 0, 0)
-                pool_pass(i // 4 - 1, 1, 0)
-            embed(i - 1, 1)
-            if last:
-                break
-            if i > 3 and i % 2 == 1:
-                quantize_features(i - 3, 2)
-            if 2 <= n < 8 and n % 2 == 0:
-                quantize_tokens(n // 2 - 1)
-            if 0 <= n < 11:
-                interleave_h(n, vector, 0, SHARE)
-            finish_h(i - 1, 1)
-            if i == 3:
-                quantize_features(0, 2)
+            if i + 2 < TILES:
+                widen_x(i + 2)
             embed(i, 0)
+            embed(i, 1)
+            if ahead:
+                quantize_all_x(i + 1)
+            if i % 2 == 1 and i > 3:
+                quantize_features(i - 3, 2)
+            elif 6 <= i < 6 + 2 * GROUPS:
+                quantize_pool((i - 6) // 2)
+            if n >= 0:
+                quantize_tokens(n)
+            finish_h(i, 0)
 
-        place(15, 1)
-        turn_x(15, 0)
-        turn_x(15, 1)
-        turn_h(13)
-        finish_h(14, 0)
-        quantize_tokens(3)
-        empty_x(15, 0)
-        empty_x(15, 1)
-        quantize_x(15, 0)
-        quantize_x(15, 1)
-        scale_term(15, 1)
-        empty_h(13)
-        project(11)
-        embed(14, 1)
-        quantize_tokens(4)
-        finish_h(14, 1)
-        embed(15, 0)
-        store_features(11)
-        interleave_h(11, scalar)
-        quantize_features(12, 2)
-        embed(15, 1)
-        finish_h(15, 0)
-        finish_h(15, 1)
-        project(12)
-        turn_h(14)
-        turn_h(15)
-        interleave_h(12, vector)
+        interleave_h(12, gpsimd_copy)
         interleave_h(13, scalar)
+        finish_h(15, 1)
+        turn_h(14)
+        project(12)
         project(13)
-        pool_pass(2, 0, 0)
-        pool_pass(2, 1, 0)
-        store_features(12)
+        turn_h(15)
         empty_h(14)
-        empty_h(15)
-        quantize_tokens(5)
-        quantize_tokens(6)
+        store_features(12, vector)
+        for g in range(3):
+            pool_pass(g, 0, 0)
+            pool_pass(g, 1, 0)
         interleave_h(14, vector)
-        for g in range(2):
-            pool_pass(g, 0, 1)
-            pool_pass(g, 1, 1)
+        empty_h(15)
+        quantize_features(14, 1)
+        quantize_tokens(12)
+        quantize_tokens(13)
+        store_features(13)
+        interleave_h(15, vector)
+        quantize_features(15, 1)
+        quantize_tokens(14)
+        quantize_tokens(15)
+        project(14)
         pool_pass(3, 0, 0)
         pool_pass(3, 1, 0)
-        store_features(13)
-        quantize_features(14, 1)
-        interleave_h(15, vector)
-        store_latents(0, 0)
-        store_latents(1, 0)
-        project(14)
-        quantize_features(15, 1)
-        quantize_tokens(7)
-        pool_pass(2, 0, 1)
-        pool_pass(2, 1, 1)
-        project(15)
         store_features(14)
+        for g in range(3):
+            pool_pass(g, 0, 1)
+        project(15)
+        store_latents(0, 0, scalar)
+        store_latents(1, 0, vector)
+        for g in range(3):
+            pool_pass(g, 1, 1)
         pool_pass(3, 0, 1)
         pool_pass(3, 1, 1)
-        store_features(15)
-        store_latents(0, 1)
-        store_latents(1, 1)
+        store_features(15, scalar)
+        store_latents(0, 1, vector)
+        store_latents(1, 1, scalar)

@@ -26,6 +26,7 @@ PAIRS = TILES // 2
 HALF = 512
 QUARTER = 256
 XB = 4
+SORTED = 2
 TB = 8
 BANKS = 8
 ALIGN = 64
@@ -130,9 +131,11 @@ def tile_tubelet_embed_pool_s8_kernel(
             load_x(i, 2)
 
         pool_ps = {}
+        pool_sorted = {}
         pool_inter = {}
         w_inter = {}
         x_wide = {}
+        x_sorted = {}
         x_ps = {}
         x_inter = {}
         x_codes = {}
@@ -179,16 +182,29 @@ def tile_tubelet_embed_pool_s8_kernel(
             ks = slice(512 * first, 512 * (first + count))
             nc.scalar.copy(out=x_wide[i][:, ks], in_=x_raw[i // 2][:, i % 2, ks].bitcast(F8))
 
+        def sort_x(i):
+            words = work.tile([P, SORTED, 2, P], F32, bufs=2, align_bytes=ALIGN)
+            x_sorted[i] = words
+            nc.scalar.copy(
+                out=words[:],
+                in_=x_wide[i][:].bitcast(F32)[:, : 256 * SORTED].rearrange("p (c q u) -> p c u q", u=2, q=P),
+            )
+
         def turn_words(bank, words):
             for u in range(2):
                 nc.tensor.transpose(bank[:, u, :], words[:, u:256:2], ident[:])
 
         def turn_x(i, b):
-            cs = range(0, 2) if b == 0 else range(2, 3)
+            cut = 1 if i == 0 else 2
+            cs = range(0, cut) if b == 0 else range(cut, PASSES)
             x_turned = next_bank(("x", i, b), [P, len(cs), 2, P])
             for c in cs:
                 x_ps[i, c] = x_turned[:, c - cs.start]
-                turn_words(x_ps[i, c], x_wide[i][:].bitcast(F32)[:, 256 * c : 256 * (c + 1)])
+                if i in x_sorted and c < SORTED:
+                    for u in range(2):
+                        nc.tensor.transpose(x_ps[i, c][:, u, :], x_sorted[i][:, c, u], ident[:])
+                else:
+                    turn_words(x_ps[i, c], x_wide[i][:].bitcast(F32)[:, 256 * c : 256 * (c + 1)])
 
         def scale_x(i, c):
             if c == 0:
@@ -200,8 +216,10 @@ def tile_tubelet_embed_pool_s8_kernel(
                 in1=scale_k[:, c].rearrange("p (u e) -> p u e", e=2).unsqueeze(1).to_broadcast([P, P, 2, 2]),
                 op=MULT,
             )
-            if c > 0:
-                release(("x", i, c - 1))
+            if c == PASSES - 1:
+                release(("x", i, 1))
+            elif c == (0 if i == 0 else 1):
+                release(("x", i, 0))
 
         def quantize_x(i, first, count):
             if first == 0:
@@ -216,17 +234,26 @@ def tile_tubelet_embed_pool_s8_kernel(
                 in_=x_inter[i][:, cs].rearrange("p c m t -> p (c m t)"),
             )
 
-        def turn_pool(g, a):
-            pool_turned = next_bank(("pool", g, a), [P, 2, P])
-            pool_ps[g, a] = pool_turned
-            turn_words(pool_turned, pool_raw[:, a].bitcast(F32)[:, 256 * g : 256 * (g + 1)])
+        def sort_pool(g):
+            words = work.tile([P, 2, 2, P], F32, bufs=2, align_bytes=ALIGN)
+            pool_sorted[g] = words
+            nc.scalar.copy(
+                out=words[:],
+                in_=pool_raw[:].bitcast(F32)[:, :, 256 * g : 256 * (g + 1)].rearrange("p a (q u) -> p a u q", u=2),
+            )
 
-        def empty_pool(g, a):
-            if a == 0:
-                pool_i = work.tile([P, 2, P, 2], F32, bufs=2, align_bytes=ALIGN)
-                pool_inter[g] = pool_i
-            nc.scalar.copy(out=pool_inter[g][:, a], in_=pool_ps[g, a][:].rearrange("p u m -> p m u"))
-            release(("pool", g, a))
+        def turn_pool(g):
+            pool_turned = next_bank(("pool", g), [P, 2, 2, P])
+            pool_ps[g] = pool_turned
+            for a in range(2):
+                for u in range(2):
+                    nc.tensor.transpose(pool_turned[:, a, u, :], pool_sorted[g][:, a, u], ident[:])
+
+        def empty_pool(g):
+            pool_i = work.tile([P, 2, P, 2], F32, bufs=2, align_bytes=ALIGN)
+            pool_inter[g] = pool_i
+            nc.scalar.copy(out=pool_i[:], in_=pool_ps[g][:].rearrange("p a u m -> p a m u"))
+            release(("pool", g))
 
         def quantize_pool(g):
             nc.vector.quantize_mx(
@@ -361,15 +388,15 @@ def tile_tubelet_embed_pool_s8_kernel(
                 in_=ht_inter[n][:].rearrange("p d t -> p (d t)"),
             )
 
-        def pool_pass(g, a, h):
+        def pool_pass(g, a, d0, width=HALF):
             if g == 0:
-                latents_ps[a, h] = next_bank(("latents", a, h), [P, HALF])
+                latents_ps[a, d0] = next_bank(("latents", a, d0), [P, width])
             nc.tensor.matmul_mx(
-                out=latents_ps[a, h][:],
+                out=latents_ps[a, d0][:],
                 lhsT=pool_codes[:, g, a].bitcast(F8X4),
                 lhsT_scale=pool_scales[:, g, a],
-                rhs=h_codes[g][:, h * HALF : (h + 1) * HALF].bitcast(F8X4),
-                rhs_scale=h_scales[g][:, h * HALF : (h + 1) * HALF],
+                rhs=h_codes[g][:, d0 : d0 + width].bitcast(F8X4),
+                rhs_scale=h_scales[g][:, d0 : d0 + width],
                 start=(g == 0),
                 stop=(g == GROUPS - 1),
             )
@@ -378,9 +405,9 @@ def tile_tubelet_embed_pool_s8_kernel(
             lat = work.tile([P, HALF], F32, tag="feats", bufs=6, align_bytes=ALIGN)
             copy(
                 out=lat[:].rearrange("p (q u e) -> p q u e", u=2, e=2),
-                in_=latents_ps[a, h][:].rearrange("p (u q e) -> p q u e", u=2, e=2),
+                in_=latents_ps[a, h * HALF][:].rearrange("p (u q e) -> p q u e", u=2, e=2),
             )
-            release(("latents", a, h))
+            release(("latents", a, h * HALF))
             nc.sync.dma_start(out=out_1[a * P : (a + 1) * P, h * HALF : (h + 1) * HALF], in_=lat[:])
 
         scalar, vector = nc.scalar.copy, nc.vector.tensor_copy
@@ -395,9 +422,9 @@ def tile_tubelet_embed_pool_s8_kernel(
 
         copy_w(0, 0, 0, vector)
         copy_w(0, 0, 1, vector)
-        widen_x(0, 0, 2)
+        widen_x(0, 0, 1)
         turn_x(0, 0)
-        widen_x(0, 2, 1)
+        widen_x(0, 1, 2)
         turn_x(0, 1)
         quantize_w(0, 0, 0)
         quantize_w(0, 0, 1)
@@ -470,9 +497,10 @@ def tile_tubelet_embed_pool_s8_kernel(
         finish_h(1, 1)
         scale_term(3, 0)
         scale_term(3, 1)
+        widen_x(5)
         finish_h(2, 0)
 
-        for i in range(3, TILES):
+        for i in range(3, TILES - 2):
             n = i - 4
             ahead = i + 1 < TILES
             if ahead:
@@ -482,78 +510,114 @@ def tile_tubelet_embed_pool_s8_kernel(
             if n >= 0:
                 interleave_h(n, gpsimd_copy)
             finish_h(i - 1, 1)
-            turn_h(i - 3 if i < 5 else i - 2)
-            if i == 4:
-                turn_h(2)
-            if 5 <= i < 5 + 2 * GROUPS:
-                turn_pool(*divmod(i - 5, 2))
+            turn_h(i - 3)
             if ahead:
                 scale_term(i + 1, 0)
                 place(i + 1, 1)
                 prepare_x(i + 1)
-            empty_h(i - 3 if i < 5 else i - 2)
+            if i + 2 < TILES:
+                sort_x(i + 2)
+            empty_h(i - 3)
             if ahead:
                 scale_term(i + 1, 1)
-            if i == 4:
-                quantize_features(0, 2)
-                empty_h(2)
-            if 5 <= i < 5 + 2 * GROUPS:
-                empty_pool(*divmod(i - 5, 2))
-            if i == 5:
-                project(0)
-                store_features(0)
             if i >= 5:
-                project(i - 4)
-                store_features(i - 4)
-            if i + 2 < TILES:
-                widen_x(i + 2)
+                project(i - 5)
+                store_features(i - 5)
+            if i + 3 < TILES:
+                widen_x(i + 3)
+            else:
+                sort_pool(0)
             embed(i, 0)
             embed(i, 1)
             if ahead:
                 quantize_all_x(i + 1)
-            if i % 2 == 1 and i > 3:
-                quantize_features(i - 3, 2)
-            elif 6 <= i < 6 + 2 * GROUPS:
-                quantize_pool((i - 6) // 2)
+            if i % 2 == 0:
+                quantize_features(i - 4, 2)
             if n >= 0:
                 quantize_tokens(n)
             finish_h(i, 0)
 
+        place(15, 0)
+        turn_x(15, 0)
+        turn_x(15, 1)
+        interleave_h(10, gpsimd_copy)
+        finish_h(13, 1)
+        turn_h(11)
+        turn_pool(0)
+        scale_term(15, 0)
+        place(15, 1)
+        prepare_x(15)
+        sort_pool(1)
+        empty_h(11)
+        scale_term(15, 1)
+        empty_pool(0)
+        project(9)
+        sort_pool(2)
+        store_features(9)
+        embed(14, 0)
+        embed(14, 1)
+        quantize_all_x(15)
+        quantize_features(10, 2)
+        quantize_pool(0)
+        quantize_tokens(10)
+        finish_h(14, 0)
+
+        interleave_h(11, gpsimd_copy)
+        turn_h(12)
+        turn_h(13)
+        turn_pool(1)
+        turn_pool(2)
+        finish_h(14, 1)
+        empty_h(12)
+        empty_h(13)
+        project(10)
+        project(11)
+        sort_pool(3)
+        store_features(10, vector)
+        empty_pool(1)
+        empty_pool(2)
+        embed(15, 0)
+        embed(15, 1)
+        store_features(11)
+        quantize_features(12, 2)
+        quantize_pool(1)
+        quantize_tokens(11)
+        finish_h(15, 0)
         interleave_h(12, gpsimd_copy)
+        project(12)
+        project(13)
         interleave_h(13, scalar)
         finish_h(15, 1)
         turn_h(14)
-        project(12)
-        project(13)
+        turn_pool(3)
         turn_h(15)
-        empty_h(14)
         store_features(12, vector)
+        empty_h(14)
+        empty_pool(3)
+        empty_h(15)
+        quantize_pool(2)
         for g in range(3):
             pool_pass(g, 0, 0)
             pool_pass(g, 1, 0)
         interleave_h(14, vector)
-        empty_h(15)
-        quantize_features(14, 1)
         quantize_tokens(12)
+        quantize_pool(3)
         quantize_tokens(13)
+        quantize_features(14, 2)
         store_features(13)
         interleave_h(15, vector)
-        quantize_features(15, 1)
         quantize_tokens(14)
         quantize_tokens(15)
-        project(14)
         pool_pass(3, 0, 0)
         pool_pass(3, 1, 0)
-        store_features(14)
-        for g in range(3):
-            pool_pass(g, 0, 1)
+        project(14)
         project(15)
         store_latents(0, 0, scalar)
-        store_latents(1, 0, vector)
-        for g in range(3):
-            pool_pass(g, 1, 1)
-        pool_pass(3, 0, 1)
-        pool_pass(3, 1, 1)
+        store_latents(1, 0, scalar)
+        store_features(14, vector)
         store_features(15, scalar)
+        for a in range(2):
+            for g in range(4):
+                pool_pass(g, a, HALF)
         store_latents(0, 1, vector)
         store_latents(1, 1, scalar)

@@ -26,7 +26,8 @@ PAIRS = TILES // 2
 HALF = 512
 QUARTER = 256
 XB = 4
-SORTED = 2
+SORT_ALL = 14
+GQ = 96
 TB = 8
 BANKS = 8
 ALIGN = 64
@@ -155,17 +156,19 @@ def tile_tubelet_embed_pool_s8_kernel(
         def gpsimd_copy(out, in_):
             nc.gpsimd.tensor_scalar(out=out, in0=in_, scalar1=1.0, scalar2=0.0, op0=MULT, op1=ADD)
 
-        def copy_w(c, h, u, copy):
-            if copy is gpsimd_copy or (c, h, u) == (0, 0, 0):
+        def copy_w(c, h, u, copy, qs=slice(0, P)):
+            if (c, h, u) in w_inter:
+                plane = w_inter[c, h, u]
+            elif copy is gpsimd_copy or (c, h, u) == (0, 0, 0):
                 plane = work.tile([P, P, 2, 4], BF16, tag="gated", bufs=1, align_bytes=ALIGN)
             else:
                 plane = work.tile([P, P, 2, 4], BF16, tag="plane", bufs=5, align_bytes=ALIGN)
             w_inter[c, h, u] = plane
-            rows = w_raw[c, h][:].rearrange("p j (q u e) -> p u q e j", u=2, e=2)[:, u]
+            rows = w_raw[c, h][:].rearrange("p j (q u e) -> p u q e j", u=2, e=2)[:, u, qs]
             if copy is gpsimd_copy:
-                copy(out=plane[:], in_=rows)
+                copy(out=plane[:, qs], in_=rows)
             else:
-                copy(out=plane[:].rearrange("p q e j -> p q j e"), in_=rows.rearrange("p q e j -> p q j e"))
+                copy(out=plane[:, qs].rearrange("p q e j -> p q j e"), in_=rows.rearrange("p q e j -> p q j e"))
 
         def quantize_w(c, h, u):
             ns = slice(u * QUARTER, (u + 1) * QUARTER)
@@ -182,44 +185,50 @@ def tile_tubelet_embed_pool_s8_kernel(
             ks = slice(512 * first, 512 * (first + count))
             nc.scalar.copy(out=x_wide[i][:, ks], in_=x_raw[i // 2][:, i % 2, ks].bitcast(F8))
 
+        def sorted_passes(i):
+            return 2 if i < SORT_ALL else PASSES
+
         def sort_x(i):
-            words = work.tile([P, SORTED, 2, P], F32, bufs=2, align_bytes=ALIGN)
+            count = sorted_passes(i)
+            words = work.tile([P, count, 2, P], F32, bufs=2, align_bytes=ALIGN)
             x_sorted[i] = words
             nc.scalar.copy(
                 out=words[:],
-                in_=x_wide[i][:].bitcast(F32)[:, : 256 * SORTED].rearrange("p (c q u) -> p c u q", u=2, q=P),
+                in_=x_wide[i][:].bitcast(F32)[:, : 256 * count].rearrange("p (c q u) -> p c u q", u=2, q=P),
             )
 
-        def turn_words(bank, words):
-            for u in range(2):
-                nc.tensor.transpose(bank[:, u, :], words[:, u:256:2], ident[:])
+        def passes_of(i, b):
+            cut = 1 if i == 0 else 2
+            return slice(0, cut) if b == 0 else slice(cut, PASSES)
 
         def turn_x(i, b):
-            cut = 1 if i == 0 else 2
-            cs = range(0, cut) if b == 0 else range(cut, PASSES)
-            x_turned = next_bank(("x", i, b), [P, len(cs), 2, P])
-            for c in cs:
-                x_ps[i, c] = x_turned[:, c - cs.start]
-                if i in x_sorted and c < SORTED:
-                    for u in range(2):
-                        nc.tensor.transpose(x_ps[i, c][:, u, :], x_sorted[i][:, c, u], ident[:])
-                else:
-                    turn_words(x_ps[i, c], x_wide[i][:].bitcast(F32)[:, 256 * c : 256 * (c + 1)])
+            cs = passes_of(i, b)
+            x_turned = next_bank(("x", i, b), [P, 2, cs.stop - cs.start, P])
+            x_ps[i, b] = x_turned
+            for c in range(cs.start, cs.stop):
+                for u in range(2):
+                    if i in x_sorted and c < sorted_passes(i):
+                        words = x_sorted[i][:, c, u]
+                    else:
+                        words = x_wide[i][:].bitcast(F32)[:, 256 * c + u : 256 * (c + 1) : 2]
+                    nc.tensor.transpose(x_turned[:, u, c - cs.start, :], words, ident[:])
 
-        def scale_x(i, c):
-            if c == 0:
+        def scale_x(i, b):
+            if b == 0:
                 x_i = work.tile([P, PASSES, P, 4], BF16, bufs=3, align_bytes=ALIGN)
                 x_inter[i] = x_i
+            cs = passes_of(i, b)
+            count = cs.stop - cs.start
             nc.vector.tensor_tensor(
-                out=x_inter[i][:, c].rearrange("p m (u e) -> p m u e", e=2),
-                in0=x_ps[i, c].bitcast(BF16).rearrange("p u (m e) -> p m u e", e=2),
-                in1=scale_k[:, c].rearrange("p (u e) -> p u e", e=2).unsqueeze(1).to_broadcast([P, P, 2, 2]),
+                out=x_inter[i][:, cs].rearrange("p c m (u e) -> p c m u e", e=2),
+                in0=x_ps[i, b][:].bitcast(BF16).rearrange("p u c (m e) -> p c m u e", e=2),
+                in1=scale_k[:, cs]
+                .rearrange("p c (u e) -> p c u e", e=2)
+                .unsqueeze(2)
+                .to_broadcast([P, count, P, 2, 2]),
                 op=MULT,
             )
-            if c == PASSES - 1:
-                release(("x", i, 1))
-            elif c == (0 if i == 0 else 1):
-                release(("x", i, 0))
+            release(("x", i, b))
 
         def quantize_x(i, first, count):
             if first == 0:
@@ -413,8 +422,8 @@ def tile_tubelet_embed_pool_s8_kernel(
         scalar, vector = nc.scalar.copy, nc.vector.tensor_copy
 
         def prepare_x(i):
-            for c in range(PASSES):
-                scale_x(i, c)
+            for b in range(2):
+                scale_x(i, b)
 
         def quantize_all_x(i):
             quantize_x(i, 0, 2)
@@ -442,7 +451,7 @@ def tile_tubelet_embed_pool_s8_kernel(
         quantize_w(2, 0, 1)
         quantize_w(1, 0, 0)
         embed(0, 0)
-        copy_w(0, 1, 0, gpsimd_copy)
+        copy_w(0, 1, 0, gpsimd_copy, slice(0, GQ))
         copy_w(0, 1, 1, scalar)
         prepare_x(1)
         copy_w(1, 1, 0, scalar)
@@ -451,12 +460,13 @@ def tile_tubelet_embed_pool_s8_kernel(
         turn_x(2, 1)
         copy_w(1, 1, 1, scalar)
         nc.vector.tensor_copy(out=gain_col[:], in_=gain_raw[:].rearrange("p g t -> p (g t)"))
+        copy_w(0, 1, 0, vector, slice(GQ, P))
         quantize_all_x(1)
         quantize_w(0, 1, 1)
         quantize_w(1, 1, 0)
         quantize_w(0, 1, 0)
         embed(1, 0)
-        copy_w(2, 1, 1, gpsimd_copy)
+        copy_w(2, 1, 1, gpsimd_copy, slice(0, GQ))
         prepare_x(2)
         embed(0, 1, 0, 1)
         embed(1, 1, 0, 1)
@@ -468,6 +478,7 @@ def tile_tubelet_embed_pool_s8_kernel(
         turn_x(3, 0)
         turn_x(3, 1)
         scale_term(1, 0)
+        copy_w(2, 1, 1, vector, slice(GQ, P))
         quantize_w(1, 1, 1)
         quantize_all_x(2)
         quantize_w(2, 1, 0)
@@ -582,42 +593,44 @@ def tile_tubelet_embed_pool_s8_kernel(
         quantize_features(12, 2)
         quantize_pool(1)
         quantize_tokens(11)
+        quantize_pool(2)
         finish_h(15, 0)
-        interleave_h(12, gpsimd_copy)
-        project(12)
-        project(13)
-        interleave_h(13, scalar)
         finish_h(15, 1)
         turn_h(14)
         turn_pool(3)
-        turn_h(15)
-        store_features(12, vector)
+        project(12)
+        project(13)
         empty_h(14)
+        interleave_h(13, scalar)
+        interleave_h(12, vector)
+        turn_h(15)
         empty_pool(3)
-        empty_h(15)
-        quantize_pool(2)
+        interleave_h(14, vector)
         for g in range(3):
             pool_pass(g, 0, 0)
             pool_pass(g, 1, 0)
-        interleave_h(14, vector)
+        empty_h(15)
         quantize_tokens(12)
+        store_features(12, vector)
         quantize_pool(3)
         quantize_tokens(13)
-        quantize_features(14, 2)
         store_features(13)
         interleave_h(15, vector)
+        quantize_features(14, 2)
         quantize_tokens(14)
         quantize_tokens(15)
         pool_pass(3, 0, 0)
         pool_pass(3, 1, 0)
+        for g in range(3):
+            pool_pass(g, 0, HALF)
+        store_latents(0, 0, scalar)
         project(14)
         project(15)
-        store_latents(0, 0, scalar)
         store_latents(1, 0, scalar)
         store_features(14, vector)
+        pool_pass(3, 0, HALF)
+        for g in range(4):
+            pool_pass(g, 1, HALF)
         store_features(15, scalar)
-        for a in range(2):
-            for g in range(4):
-                pool_pass(g, a, HALF)
         store_latents(0, 1, vector)
         store_latents(1, 1, scalar)

@@ -27,6 +27,8 @@ HALF = 512
 QUARTER = 256
 XB = 4
 SORT_ALL = 14
+POOL_STEP = 6
+POOL_GAP = 2
 GQ = 96
 TB = 8
 BANKS = 8
@@ -132,7 +134,6 @@ def tile_tubelet_embed_pool_s8_kernel(
             load_x(i, 2)
 
         pool_ps = {}
-        pool_sorted = {}
         pool_inter = {}
         w_inter = {}
         x_wide = {}
@@ -243,20 +244,13 @@ def tile_tubelet_embed_pool_s8_kernel(
                 in_=x_inter[i][:, cs].rearrange("p c m t -> p (c m t)"),
             )
 
-        def sort_pool(g):
-            words = work.tile([P, 2, 2, P], F32, bufs=2, align_bytes=ALIGN)
-            pool_sorted[g] = words
-            nc.scalar.copy(
-                out=words[:],
-                in_=pool_raw[:].bitcast(F32)[:, :, 256 * g : 256 * (g + 1)].rearrange("p a (q u) -> p a u q", u=2),
-            )
-
         def turn_pool(g):
             pool_turned = next_bank(("pool", g), [P, 2, 2, P])
             pool_ps[g] = pool_turned
             for a in range(2):
                 for u in range(2):
-                    nc.tensor.transpose(pool_turned[:, a, u, :], pool_sorted[g][:, a, u], ident[:])
+                    words = pool_raw[:, a].bitcast(F32)[:, 256 * g + u : 256 * (g + 1) : 2]
+                    nc.tensor.transpose(pool_turned[:, a, u, :], words, ident[:])
 
         def empty_pool(g):
             pool_i = work.tile([P, 2, P, 2], F32, bufs=2, align_bytes=ALIGN)
@@ -511,126 +505,90 @@ def tile_tubelet_embed_pool_s8_kernel(
         widen_x(5)
         finish_h(2, 0)
 
-        for i in range(3, TILES - 2):
+        for i in range(3, TILES - 1):
             n = i - 4
-            ahead = i + 1 < TILES
-            if ahead:
-                place(i + 1, 0)
-                turn_x(i + 1, 0)
-                turn_x(i + 1, 1)
+            g, phase = divmod(i - POOL_STEP, POOL_GAP)
+            place(i + 1, 0)
+            turn_x(i + 1, 0)
+            turn_x(i + 1, 1)
             if n >= 0:
                 interleave_h(n, gpsimd_copy)
             finish_h(i - 1, 1)
             turn_h(i - 3)
-            if ahead:
-                scale_term(i + 1, 0)
-                place(i + 1, 1)
-                prepare_x(i + 1)
+            if 0 <= g < GROUPS and phase == 0:
+                turn_pool(g)
+            scale_term(i + 1, 0)
+            place(i + 1, 1)
+            prepare_x(i + 1)
             if i + 2 < TILES:
                 sort_x(i + 2)
             empty_h(i - 3)
-            if ahead:
-                scale_term(i + 1, 1)
+            scale_term(i + 1, 1)
+            if 0 <= g < GROUPS and phase == 0:
+                empty_pool(g)
             if i >= 5:
                 project(i - 5)
                 store_features(i - 5)
             if i + 3 < TILES:
                 widen_x(i + 3)
-            else:
-                sort_pool(0)
             embed(i, 0)
             embed(i, 1)
-            if ahead:
-                quantize_all_x(i + 1)
+            quantize_all_x(i + 1)
             if i % 2 == 0:
                 quantize_features(i - 4, 2)
+            if 0 <= g < GROUPS and phase == 1:
+                quantize_pool(g)
             if n >= 0:
                 quantize_tokens(n)
             finish_h(i, 0)
 
-        place(15, 0)
-        turn_x(15, 0)
-        turn_x(15, 1)
-        interleave_h(10, gpsimd_copy)
-        finish_h(13, 1)
-        turn_h(11)
-        turn_pool(0)
-        scale_term(15, 0)
-        place(15, 1)
-        prepare_x(15)
-        sort_pool(1)
-        empty_h(11)
-        scale_term(15, 1)
-        empty_pool(0)
-        project(9)
-        sort_pool(2)
-        store_features(9)
-        embed(14, 0)
-        embed(14, 1)
-        quantize_all_x(15)
-        quantize_features(10, 2)
-        quantize_pool(0)
-        quantize_tokens(10)
-        finish_h(14, 0)
-
         interleave_h(11, gpsimd_copy)
         turn_h(12)
         turn_h(13)
-        turn_pool(1)
-        turn_pool(2)
         finish_h(14, 1)
         empty_h(12)
         empty_h(13)
-        project(10)
-        project(11)
-        sort_pool(3)
-        store_features(10, vector)
-        empty_pool(1)
-        empty_pool(2)
         embed(15, 0)
         embed(15, 1)
-        store_features(11)
-        quantize_features(12, 2)
-        quantize_pool(1)
-        quantize_tokens(11)
-        quantize_pool(2)
+        project(10)
+        project(11)
+        store_features(10)
         finish_h(15, 0)
         finish_h(15, 1)
+        store_features(11)
+        quantize_features(12, 2)
+        quantize_tokens(11)
+        for g in range(3):
+            pool_pass(g, 0, 0)
         turn_h(14)
-        turn_pool(3)
+        turn_h(15)
+        interleave_h(13, scalar)
+        interleave_h(12, vector)
         project(12)
         project(13)
         empty_h(14)
-        interleave_h(13, scalar)
-        interleave_h(12, vector)
-        turn_h(15)
-        empty_pool(3)
+        empty_h(15)
         interleave_h(14, vector)
         for g in range(3):
-            pool_pass(g, 0, 0)
             pool_pass(g, 1, 0)
-        empty_h(15)
         quantize_tokens(12)
-        store_features(12, vector)
-        quantize_pool(3)
         quantize_tokens(13)
-        store_features(13)
-        interleave_h(15, vector)
+        store_features(12)
         quantize_features(14, 2)
-        quantize_tokens(14)
-        quantize_tokens(15)
+        interleave_h(15, vector)
+        store_features(13)
         pool_pass(3, 0, 0)
         pool_pass(3, 1, 0)
-        for g in range(3):
-            pool_pass(g, 0, HALF)
-        store_latents(0, 0, scalar)
+        quantize_tokens(14)
+        quantize_tokens(15)
         project(14)
         project(15)
-        store_latents(1, 0, scalar)
-        store_features(14, vector)
-        pool_pass(3, 0, HALF)
-        for g in range(4):
-            pool_pass(g, 1, HALF)
-        store_features(15, scalar)
-        store_latents(0, 1, vector)
-        store_latents(1, 1, scalar)
+        store_latents(0, 0, scalar)
+        store_latents(1, 0, vector)
+        store_features(14, scalar)
+        for a in range(2):
+            for g in range(4):
+                pool_pass(g, a, HALF)
+        store_features(15, vector)
+        store_latents(0, 1, scalar)
+        store_latents(1, 1, vector)

@@ -82,9 +82,13 @@ def tile_tubelet_embed_pool_s8_kernel(
         w_raw = {}
         w_codes = {}
         w_scales = {}
+        w_first = []
+        for s in range(2):
+            w_first.append(keep.tile([P, 4, QUARTER], BF16, name="w_first%d" % s, align_bytes=ALIGN))
         for h in range(2):
             for c in range(PASSES):
-                w_raw[c, h] = keep.tile([P, 4, HALF], BF16, name="w_raw%d%d" % (c, h), align_bytes=ALIGN)
+                if (c, h) != (0, 0):
+                    w_raw[c, h] = keep.tile([P, 4, HALF], BF16, name="w_raw%d%d" % (c, h), align_bytes=ALIGN)
                 w_codes[c, h] = keep.tile([P, HALF], U32, name="w_codes%d%d" % (c, h), align_bytes=ALIGN)
                 w_scales[c, h] = keep.tile([P, HALF], U8, name="w_scales%d%d" % (c, h), align_bytes=ALIGN)
         pool_codes = keep.tile([P, GROUPS, 2, P], U32, align_bytes=ALIGN)
@@ -105,12 +109,17 @@ def tile_tubelet_embed_pool_s8_kernel(
             slot = first % 2
             nc.sync.dma_start(out=x_raw[first // 2][:, slot : slot + count, :], in_=rows[:, t : t + count, :])
 
-        def load_sites(t):
+        def load_positions(t):
+            nc.sync.dma_start(out=pos[64:72, t : t + 2], in_=time_pos.unsqueeze(1).to_broadcast([T, 2, N]))
             nc.sync.dma_start(out=pos[0:64, t : t + 2], in_=space_pos.rearrange("(k t) d -> k t d", t=4)[:, t : t + 2])
 
         nc.scalar.dma_start(out=scale_k[:], in_=x_scale.rearrange("o (c p t) -> p (o c) t", p=P, t=4))
-        load_w(0, 0)
-        load_x(0, 1)
+        for s, ks in enumerate((slice(0, 512), slice(512, K))):
+            nc.sync.dma_start(
+                out=w_first[s][:],
+                in_=w.rearrange("(c p j) n -> c p j n", p=P, j=4)[0][:, :, s * QUARTER : (s + 1) * QUARTER],
+            )
+            nc.sync.dma_start(out=x_raw[0][:, 0, ks], in_=x_bytes.rearrange("(p t) k -> p t k", t=4)[:P, 0, ks])
         load_w(1, 0)
         load_w(2, 0)
         load_x(1, 1)
@@ -119,9 +128,8 @@ def tile_tubelet_embed_pool_s8_kernel(
         load_w(1, 1)
         load_x(2, 2)
         load_w(2, 1)
-        load_sites(0)
-        nc.sync.dma_start(out=pos[64:72], in_=time_pos.unsqueeze(1).to_broadcast([T, 4, N]))
-        load_sites(2)
+        load_positions(0)
+        load_positions(2)
         load_x(4, 2)
         for q in range(4):
             nc.sync.dma_start(
@@ -165,7 +173,10 @@ def tile_tubelet_embed_pool_s8_kernel(
             else:
                 plane = work.tile([P, P, 2, 4], BF16, tag="plane", bufs=5, align_bytes=ALIGN)
             w_inter[c, h, u] = plane
-            rows = w_raw[c, h][:].rearrange("p j (q u e) -> p u q e j", u=2, e=2)[:, u, qs]
+            if (c, h) == (0, 0):
+                rows = w_first[qs.start // 64][:].rearrange("p j (q u e) -> p u q e j", u=2, e=2)[:, u]
+            else:
+                rows = w_raw[c, h][:].rearrange("p j (q u e) -> p u q e j", u=2, e=2)[:, u, qs]
             if copy is gpsimd_copy:
                 copy(out=plane[:, qs], in_=rows)
             else:
@@ -404,6 +415,30 @@ def tile_tubelet_embed_pool_s8_kernel(
                 stop=(g == GROUPS - 1),
             )
 
+        def pool_last(s):
+            bank = next_bank(("last", s), [P, 2, P])
+            latents_ps[s] = bank
+            for u in range(2):
+                ds = slice(HALF + QUARTER * u + P * s, HALF + QUARTER * u + P * (s + 1))
+                for g in range(GROUPS):
+                    nc.tensor.matmul_mx(
+                        out=bank[:, u],
+                        lhsT=pool_codes[:, g, 1].bitcast(F8X4),
+                        lhsT_scale=pool_scales[:, g, 1],
+                        rhs=h_codes[g][:, ds].bitcast(F8X4),
+                        rhs_scale=h_scales[g][:, ds],
+                        start=(g == 0),
+                        stop=(g == GROUPS - 1),
+                    )
+
+        def store_last(s, copy):
+            lat = work.tile([P, QUARTER], F32, tag="feats", bufs=6, align_bytes=ALIGN)
+            copy(
+                out=lat[:].rearrange("p (q u e) -> p q u e", u=2, e=2),
+                in_=latents_ps[s][:].rearrange("p u (q e) -> p q u e", e=2),
+            )
+            nc.sync.dma_start(out=out_1[P:, HALF + QUARTER * s : HALF + QUARTER * (s + 1)], in_=lat[:])
+
         def store_latents(a, h, copy):
             lat = work.tile([P, HALF], F32, tag="feats", bufs=6, align_bytes=ALIGN)
             copy(
@@ -423,8 +458,9 @@ def tile_tubelet_embed_pool_s8_kernel(
             quantize_x(i, 0, 2)
             quantize_x(i, 2, 1)
 
-        copy_w(0, 0, 0, vector)
-        copy_w(0, 0, 1, vector)
+        for s in range(2):
+            for u in range(2):
+                copy_w(0, 0, u, vector, slice(64 * s, 64 * (s + 1)))
         widen_x(0, 0, 1)
         turn_x(0, 0)
         widen_x(0, 1, 2)
@@ -461,16 +497,16 @@ def tile_tubelet_embed_pool_s8_kernel(
         quantize_w(0, 1, 0)
         embed(1, 0)
         copy_w(2, 1, 1, gpsimd_copy, slice(0, GQ))
-        prepare_x(2)
         embed(0, 1, 0, 1)
         embed(1, 1, 0, 1)
-        copy_w(2, 1, 0, scalar)
         widen_x(3)
+        copy_w(2, 1, 0, scalar)
         place(0, 0)
+        turn_x(3, 0)
+        prepare_x(2)
+        turn_x(3, 1)
         place(1, 0)
         scale_term(0, 0)
-        turn_x(3, 0)
-        turn_x(3, 1)
         scale_term(1, 0)
         copy_w(2, 1, 1, vector, slice(GQ, P))
         quantize_w(1, 1, 1)
@@ -478,24 +514,24 @@ def tile_tubelet_embed_pool_s8_kernel(
         quantize_w(2, 1, 0)
         quantize_w(2, 1, 1)
         finish_h(0, 0)
-        place(0, 1)
+        finish_h(1, 0)
         embed(0, 1, 1, 1)
         embed(1, 1, 1, 1)
+        place(0, 1)
         place(1, 1)
         scale_term(0, 1)
         scale_term(1, 1)
         embed(0, 1, 2, 1)
         embed(1, 1, 2, 1)
-        prepare_x(3)
         widen_x(4)
-        place(2, 0)
         embed(2, 0)
+        place(2, 0)
+        prepare_x(3)
         place(2, 1)
         scale_term(2, 0)
-        finish_h(1, 0)
+        finish_h(0, 1)
         quantize_all_x(3)
         scale_term(2, 1)
-        finish_h(0, 1)
         embed(2, 1)
         place(3, 0)
         place(3, 1)
@@ -586,9 +622,11 @@ def tile_tubelet_embed_pool_s8_kernel(
         store_latents(0, 0, scalar)
         store_latents(1, 0, vector)
         store_features(14, scalar)
-        for a in range(2):
-            for g in range(4):
-                pool_pass(g, a, HALF)
+        for g in range(GROUPS):
+            pool_pass(g, 0, HALF)
+        pool_last(0)
+        pool_last(1)
         store_features(15, vector)
         store_latents(0, 1, scalar)
-        store_latents(1, 1, vector)
+        store_last(0, vector)
+        store_last(1, scalar)

@@ -82,13 +82,9 @@ def tile_tubelet_embed_pool_s8_kernel(
         w_raw = {}
         w_codes = {}
         w_scales = {}
-        w_first = []
-        for s in range(2):
-            w_first.append(keep.tile([P, 4, QUARTER], BF16, name="w_first%d" % s, align_bytes=ALIGN))
         for h in range(2):
             for c in range(PASSES):
-                if (c, h) != (0, 0):
-                    w_raw[c, h] = keep.tile([P, 4, HALF], BF16, name="w_raw%d%d" % (c, h), align_bytes=ALIGN)
+                w_raw[c, h] = keep.tile([P, 4, HALF], BF16, name="w_raw%d%d" % (c, h), align_bytes=ALIGN)
                 w_codes[c, h] = keep.tile([P, HALF], U32, name="w_codes%d%d" % (c, h), align_bytes=ALIGN)
                 w_scales[c, h] = keep.tile([P, HALF], U8, name="w_scales%d%d" % (c, h), align_bytes=ALIGN)
         pool_codes = keep.tile([P, GROUPS, 2, P], U32, align_bytes=ALIGN)
@@ -114,19 +110,15 @@ def tile_tubelet_embed_pool_s8_kernel(
             nc.sync.dma_start(out=pos[0:64, t : t + 2], in_=space_pos.rearrange("(k t) d -> k t d", t=4)[:, t : t + 2])
 
         nc.scalar.dma_start(out=scale_k[:], in_=x_scale.rearrange("o (c p t) -> p (o c) t", p=P, t=4))
-        for s, ks in enumerate((slice(0, 512), slice(512, K))):
-            nc.sync.dma_start(
-                out=w_first[s][:],
-                in_=w.rearrange("(c p j) n -> c p j n", p=P, j=4)[0][:, :, s * QUARTER : (s + 1) * QUARTER],
-            )
-            nc.sync.dma_start(out=x_raw[0][:, 0, ks], in_=x_bytes.rearrange("(p t) k -> p t k", t=4)[:P, 0, ks])
+        load_w(0, 0)
+        load_x(0, 1)
         load_w(1, 0)
-        load_w(2, 0)
         load_x(1, 1)
+        load_w(2, 0)
         nc.scalar.dma_start(out=gain_raw[:], in_=gain.rearrange("(g p t) -> p g t", p=P, t=4))
         load_w(0, 1)
-        load_w(1, 1)
         load_x(2, 2)
+        load_w(1, 1)
         load_w(2, 1)
         load_positions(0)
         load_positions(2)
@@ -173,10 +165,7 @@ def tile_tubelet_embed_pool_s8_kernel(
             else:
                 plane = work.tile([P, P, 2, 4], BF16, tag="plane", bufs=5, align_bytes=ALIGN)
             w_inter[c, h, u] = plane
-            if (c, h) == (0, 0):
-                rows = w_first[qs.start // 64][:].rearrange("p j (q u e) -> p u q e j", u=2, e=2)[:, u]
-            else:
-                rows = w_raw[c, h][:].rearrange("p j (q u e) -> p u q e j", u=2, e=2)[:, u, qs]
+            rows = w_raw[c, h][:].rearrange("p j (q u e) -> p u q e j", u=2, e=2)[:, u, qs]
             if copy is gpsimd_copy:
                 copy(out=plane[:, qs], in_=rows)
             else:
@@ -415,30 +404,6 @@ def tile_tubelet_embed_pool_s8_kernel(
                 stop=(g == GROUPS - 1),
             )
 
-        def pool_last(s):
-            bank = next_bank(("last", s), [P, 2, P])
-            latents_ps[s] = bank
-            for u in range(2):
-                ds = slice(HALF + QUARTER * u + P * s, HALF + QUARTER * u + P * (s + 1))
-                for g in range(GROUPS):
-                    nc.tensor.matmul_mx(
-                        out=bank[:, u],
-                        lhsT=pool_codes[:, g, 1].bitcast(F8X4),
-                        lhsT_scale=pool_scales[:, g, 1],
-                        rhs=h_codes[g][:, ds].bitcast(F8X4),
-                        rhs_scale=h_scales[g][:, ds],
-                        start=(g == 0),
-                        stop=(g == GROUPS - 1),
-                    )
-
-        def store_last(s, copy):
-            lat = work.tile([P, QUARTER], F32, tag="feats", bufs=6, align_bytes=ALIGN)
-            copy(
-                out=lat[:].rearrange("p (q u e) -> p q u e", u=2, e=2),
-                in_=latents_ps[s][:].rearrange("p u (q e) -> p q u e", e=2),
-            )
-            nc.sync.dma_start(out=out_1[P:, HALF + QUARTER * s : HALF + QUARTER * (s + 1)], in_=lat[:])
-
         def store_latents(a, h, copy):
             lat = work.tile([P, HALF], F32, tag="feats", bufs=6, align_bytes=ALIGN)
             copy(
@@ -458,9 +423,8 @@ def tile_tubelet_embed_pool_s8_kernel(
             quantize_x(i, 0, 2)
             quantize_x(i, 2, 1)
 
-        for s in range(2):
-            for u in range(2):
-                copy_w(0, 0, u, vector, slice(64 * s, 64 * (s + 1)))
+        copy_w(0, 0, 0, vector)
+        copy_w(0, 0, 1, vector)
         widen_x(0, 0, 1)
         turn_x(0, 0)
         widen_x(0, 1, 2)
@@ -470,12 +434,12 @@ def tile_tubelet_embed_pool_s8_kernel(
         copy_w(1, 0, 0, gpsimd_copy)
         copy_w(1, 0, 1, scalar)
         prepare_x(0)
-        copy_w(2, 0, 0, scalar)
         widen_x(1)
-        copy_w(2, 0, 1, vector)
-        quantize_all_x(0)
         turn_x(1, 0)
         turn_x(1, 1)
+        copy_w(2, 0, 0, scalar)
+        copy_w(2, 0, 1, vector)
+        quantize_all_x(0)
         quantize_w(1, 0, 1)
         quantize_w(2, 0, 0)
         quantize_w(2, 0, 1)
@@ -484,10 +448,11 @@ def tile_tubelet_embed_pool_s8_kernel(
         copy_w(0, 1, 0, gpsimd_copy, slice(0, GQ))
         copy_w(0, 1, 1, scalar)
         prepare_x(1)
-        copy_w(1, 1, 0, scalar)
         widen_x(2)
         turn_x(2, 0)
         turn_x(2, 1)
+        copy_w(1, 1, 0, scalar)
+        widen_x(3)
         copy_w(1, 1, 1, scalar)
         nc.vector.tensor_copy(out=gain_col[:], in_=gain_raw[:].rearrange("p g t -> p (g t)"))
         copy_w(0, 1, 0, vector, slice(GQ, P))
@@ -496,15 +461,14 @@ def tile_tubelet_embed_pool_s8_kernel(
         quantize_w(1, 1, 0)
         quantize_w(0, 1, 0)
         embed(1, 0)
+        turn_x(3, 0)
+        turn_x(3, 1)
         copy_w(2, 1, 1, gpsimd_copy, slice(0, GQ))
         embed(0, 1, 0, 1)
         embed(1, 1, 0, 1)
-        widen_x(3)
         copy_w(2, 1, 0, scalar)
-        place(0, 0)
-        turn_x(3, 0)
         prepare_x(2)
-        turn_x(3, 1)
+        place(0, 0)
         place(1, 0)
         scale_term(0, 0)
         scale_term(1, 0)
@@ -518,11 +482,11 @@ def tile_tubelet_embed_pool_s8_kernel(
         embed(0, 1, 1, 1)
         embed(1, 1, 1, 1)
         place(0, 1)
+        embed(0, 1, 2, 1)
+        embed(1, 1, 2, 1)
         place(1, 1)
         scale_term(0, 1)
         scale_term(1, 1)
-        embed(0, 1, 2, 1)
-        embed(1, 1, 2, 1)
         widen_x(4)
         embed(2, 0)
         place(2, 0)
@@ -622,11 +586,9 @@ def tile_tubelet_embed_pool_s8_kernel(
         store_latents(0, 0, scalar)
         store_latents(1, 0, vector)
         store_features(14, scalar)
-        for g in range(GROUPS):
-            pool_pass(g, 0, HALF)
-        pool_last(0)
-        pool_last(1)
+        for a in range(2):
+            for g in range(4):
+                pool_pass(g, a, HALF)
         store_features(15, vector)
         store_latents(0, 1, scalar)
-        store_last(0, vector)
-        store_last(1, scalar)
+        store_latents(1, 1, vector)

@@ -509,8 +509,8 @@ def tile_tubelet_embed_pool_s8_kernel(
             n = i - 4
             g, phase = divmod(i - POOL_STEP, POOL_GAP)
             place(i + 1, 0)
-            turn_x(i + 1, 0)
             turn_x(i + 1, 1)
+            turn_x(i + 1, 0)
             if n >= 0:
                 interleave_h(n, gpsimd_copy)
             finish_h(i - 1, 1)

@@ -27,7 +27,7 @@ HALF = 512
 QUARTER = 256
 XB = 4
 SORT_ALL = 14
-POOL_STEP = 6
+POOL_STEP = 4
 POOL_GAP = 2
 GQ = 96
 TB = 8
@@ -87,8 +87,6 @@ def tile_tubelet_embed_pool_s8_kernel(
                 w_raw[c, h] = keep.tile([P, 4, HALF], BF16, name="w_raw%d%d" % (c, h), align_bytes=ALIGN)
                 w_codes[c, h] = keep.tile([P, HALF], U32, name="w_codes%d%d" % (c, h), align_bytes=ALIGN)
                 w_scales[c, h] = keep.tile([P, HALF], U8, name="w_scales%d%d" % (c, h), align_bytes=ALIGN)
-        pool_codes = keep.tile([P, GROUPS, 2, P], U32, align_bytes=ALIGN)
-        pool_scales = keep.tile([P, GROUPS, 2, P], U8, align_bytes=ALIGN)
         h_codes = []
         h_scales = []
         for g in range(GROUPS):
@@ -134,7 +132,6 @@ def tile_tubelet_embed_pool_s8_kernel(
             load_x(i, 2)
 
         pool_ps = {}
-        pool_inter = {}
         w_inter = {}
         x_wide = {}
         x_sorted = {}
@@ -215,8 +212,8 @@ def tile_tubelet_embed_pool_s8_kernel(
                     nc.tensor.transpose(x_turned[:, u, c - cs.start, :], words, ident[:])
 
         def scale_x(i, b):
-            if b == 0:
-                x_i = work.tile([P, PASSES, P, 4], BF16, bufs=3, align_bytes=ALIGN)
+            if i not in x_inter:
+                x_i = work.tile([P, PASSES + 1, P, 4], BF16, bufs=3, align_bytes=ALIGN)
                 x_inter[i] = x_i
             cs = passes_of(i, b)
             count = cs.stop - cs.start
@@ -232,7 +229,10 @@ def tile_tubelet_embed_pool_s8_kernel(
             release(("x", i, b))
 
         def quantize_x(i, first, count):
-            if first == 0:
+            if count > PASSES:
+                x_codes[i] = keep.tile([P, count, P], U32, name="ride_codes%d" % i, align_bytes=ALIGN)
+                x_scales[i] = keep.tile([P, count, P], U8, name="ride_scales%d" % i, align_bytes=ALIGN)
+            elif first == 0:
                 codes = work.tile([P, PASSES, P], U32, bufs=XB, align_bytes=ALIGN)
                 scales = work.tile([P, PASSES, P], U8, bufs=XB, align_bytes=ALIGN)
                 x_codes[i] = codes
@@ -244,26 +244,24 @@ def tile_tubelet_embed_pool_s8_kernel(
                 in_=x_inter[i][:, cs].rearrange("p c m t -> p (c m t)"),
             )
 
-        def turn_pool(g):
-            pool_turned = next_bank(("pool", g), [P, 2, 2, P])
-            pool_ps[g] = pool_turned
-            for a in range(2):
-                for u in range(2):
-                    words = pool_raw[:, a].bitcast(F32)[:, 256 * g + u : 256 * (g + 1) : 2]
-                    nc.tensor.transpose(pool_turned[:, a, u, :], words, ident[:])
+        def turn_pool(g, a):
+            pool_turned = next_bank(("pool", g, a), [P, 2, P])
+            pool_ps[g, a] = pool_turned
+            for u in range(2):
+                words = pool_raw[:, a].bitcast(F32)[:, 256 * g + u : 256 * (g + 1) : 2]
+                nc.tensor.transpose(pool_turned[:, u, :], words, ident[:])
 
-        def empty_pool(g):
-            pool_i = work.tile([P, 2, P, 2], F32, bufs=2, align_bytes=ALIGN)
-            pool_inter[g] = pool_i
-            nc.scalar.copy(out=pool_i[:], in_=pool_ps[g][:].rearrange("p a u m -> p a m u"))
-            release(("pool", g))
+        def carrier(g, a):
+            return POOL_STEP + 2 + 2 * g + a
 
-        def quantize_pool(g):
-            nc.vector.quantize_mx(
-                out=pool_codes[:, g].rearrange("p a m -> p (a m)").bitcast(F8X4),
-                scales=pool_scales[:, g].rearrange("p a m -> p (a m)"),
-                in_=pool_inter[g][:].rearrange("p a m u -> p (a m u)").bitcast(BF16),
+        def empty_pool(g, a):
+            x_i = work.tile([P, PASSES + 1, P, 4], BF16, bufs=3, align_bytes=ALIGN)
+            x_inter[carrier(g, a)] = x_i
+            nc.scalar.copy(
+                out=x_i[:, PASSES].rearrange("p m t -> p (m t)").bitcast(F32).rearrange("p (m u) -> p m u", u=2),
+                in_=pool_ps[g, a][:].rearrange("p u m -> p m u"),
             )
+            release(("pool", g, a))
 
         def place(i, h):
             placed = next_bank(("term", i, h), [P, HALF])
@@ -396,8 +394,8 @@ def tile_tubelet_embed_pool_s8_kernel(
                 latents_ps[a, d0] = next_bank(("latents", a, d0), [P, width])
             nc.tensor.matmul_mx(
                 out=latents_ps[a, d0][:],
-                lhsT=pool_codes[:, g, a].bitcast(F8X4),
-                lhsT_scale=pool_scales[:, g, a],
+                lhsT=x_codes[carrier(g, a)][:, PASSES].bitcast(F8X4),
+                lhsT_scale=x_scales[carrier(g, a)][:, PASSES],
                 rhs=h_codes[g][:, d0 : d0 + width].bitcast(F8X4),
                 rhs_scale=h_scales[g][:, d0 : d0 + width],
                 start=(g == 0),
@@ -515,8 +513,8 @@ def tile_tubelet_embed_pool_s8_kernel(
                 interleave_h(n, gpsimd_copy)
             finish_h(i - 1, 1)
             turn_h(i - 3)
-            if 0 <= g < GROUPS and phase == 0:
-                turn_pool(g)
+            if 0 <= g < GROUPS:
+                turn_pool(g, phase)
             scale_term(i + 1, 0)
             place(i + 1, 1)
             prepare_x(i + 1)
@@ -524,8 +522,8 @@ def tile_tubelet_embed_pool_s8_kernel(
                 sort_x(i + 2)
             empty_h(i - 3)
             scale_term(i + 1, 1)
-            if 0 <= g < GROUPS and phase == 0:
-                empty_pool(g)
+            if 0 <= g < GROUPS:
+                empty_pool(g, phase)
             if i >= 5:
                 project(i - 5)
                 store_features(i - 5)
@@ -533,14 +531,20 @@ def tile_tubelet_embed_pool_s8_kernel(
                 widen_x(i + 3)
             embed(i, 0)
             embed(i, 1)
-            quantize_all_x(i + 1)
-            if i % 2 == 0:
-                quantize_features(i - 4, 2)
-            if 0 <= g < GROUPS and phase == 1:
-                quantize_pool(g)
+            if carrier(0, 0) <= i + 1 <= carrier(GROUPS - 1, 1):
+                if i % 2 == 0:
+                    quantize_features(i - 4, 2)
+                else:
+                    finish_h(i, 0)
+                quantize_x(i + 1, 0, PASSES + 1)
+            else:
+                quantize_all_x(i + 1)
+                if i % 2 == 0:
+                    quantize_features(i - 4, 2)
             if n >= 0:
                 quantize_tokens(n)
-            finish_h(i, 0)
+            if i % 2 == 0 or not carrier(0, 0) <= i + 1 <= carrier(GROUPS - 1, 1):
+                finish_h(i, 0)
 
         interleave_h(11, gpsimd_copy)
         turn_h(12)

@@ -184,7 +184,7 @@ def tile_tubelet_embed_pool_s8_kernel(
             nc.scalar.copy(out=x_wide[i][:, ks], in_=x_raw[i // 2][:, i % 2, ks].bitcast(F8))
 
         def sorted_passes(i):
-            return 2 if i < SORT_ALL else PASSES
+            return 1 + i % 2 if i < SORT_ALL else PASSES
 
         def sort_x(i):
             count = sorted_passes(i)

@@ -30,6 +30,13 @@ SORT_ALL = 14
 POOL_STEP = 4
 POOL_GAP = 2
 GQ = 96
+GW = 256
+SUM_FROM = 6
+LT = 3
+LQ = 4
+LP = 5
+HELD_FROM = 12
+HELD = 0
 TB = 8
 BANKS = 8
 ALIGN = 64
@@ -48,10 +55,10 @@ def tile_tubelet_embed_pool_s8_kernel(
         free_banks = list(range(BANKS))
         bank_of = {}
 
-        def next_bank(key, shape):
+        def next_bank(key, shape, dtype=F32):
             bank_of[key] = free_banks[0]
             free_banks.remove(bank_of[key])
-            return psum.tile(shape, F32, name="bank%d" % bank_of[key])
+            return psum.tile(shape, dtype, name="bank%d" % bank_of[key])
 
         def release(key):
             free_banks.append(bank_of[key])
@@ -87,6 +94,10 @@ def tile_tubelet_embed_pool_s8_kernel(
                 w_raw[c, h] = keep.tile([P, 4, HALF], BF16, name="w_raw%d%d" % (c, h), align_bytes=ALIGN)
                 w_codes[c, h] = keep.tile([P, HALF], U32, name="w_codes%d%d" % (c, h), align_bytes=ALIGN)
                 w_scales[c, h] = keep.tile([P, HALF], U8, name="w_scales%d%d" % (c, h), align_bytes=ALIGN)
+        pool_codes = keep.tile([P, GROUPS, 2, P], U32, align_bytes=ALIGN)
+        pool_scales = keep.tile([P, GROUPS, 2, P], U8, align_bytes=ALIGN)
+        space_rep = keep.tile([P, 4, GW], BF16, align_bytes=ALIGN)
+        time_rep = keep.tile([P, GROUPS, GW], BF16, align_bytes=ALIGN)
         h_codes = []
         h_scales = []
         for g in range(GROUPS):
@@ -121,6 +132,11 @@ def tile_tubelet_embed_pool_s8_kernel(
         load_positions(0)
         load_positions(2)
         load_x(4, 2)
+        for f in range(2):
+            half = slice(64 * f, 64 * (f + 1))
+            nc.sync.dma_start(out=space_rep[half], in_=space_pos.rearrange("(k t) d -> k t d", t=4)[:, :, N - GW :])
+            rows = time_pos.rearrange("(g f) d -> f g d", f=2)[f : f + 1, :, N - GW :]
+            nc.sync.dma_start(out=time_rep[half], in_=rows.to_broadcast([64, GROUPS, GW]))
         for q in range(4):
             nc.sync.dma_start(
                 out=proj_s[32 * q : 32 * q + 4].bitcast(I32),
@@ -132,7 +148,10 @@ def tile_tubelet_embed_pool_s8_kernel(
             load_x(i, 2)
 
         pool_ps = {}
+        pool_inter = {}
+        sums = {}
         w_inter = {}
+        w_ps = {}
         x_wide = {}
         x_sorted = {}
         x_ps = {}
@@ -184,7 +203,7 @@ def tile_tubelet_embed_pool_s8_kernel(
             nc.scalar.copy(out=x_wide[i][:, ks], in_=x_raw[i // 2][:, i % 2, ks].bitcast(F8))
 
         def sorted_passes(i):
-            return 1 + i % 2 if i < SORT_ALL else PASSES
+            return 1 + 0 * (i % 2) if i < SORT_ALL else PASSES
 
         def sort_x(i):
             count = sorted_passes(i)
@@ -199,12 +218,13 @@ def tile_tubelet_embed_pool_s8_kernel(
             cut = 1 if i == 0 else 2
             return slice(0, cut) if b == 0 else slice(cut, PASSES)
 
-        def turn_x(i, b):
+        def turn_x(i, b, planes=range(2)):
             cs = passes_of(i, b)
-            x_turned = next_bank(("x", i, b), [P, 2, cs.stop - cs.start, P])
-            x_ps[i, b] = x_turned
-            for c in range(cs.start, cs.stop):
-                for u in range(2):
+            if 0 in planes:
+                x_ps[i, b] = next_bank(("x", i, b), [P, 2, cs.stop - cs.start, P])
+            x_turned = x_ps[i, b]
+            for c in range(cs.stop - 1, cs.start - 1, -1):
+                for u in planes:
                     if i in x_sorted and c < sorted_passes(i):
                         words = x_sorted[i][:, c, u]
                     else:
@@ -213,7 +233,7 @@ def tile_tubelet_embed_pool_s8_kernel(
 
         def scale_x(i, b):
             if i not in x_inter:
-                x_i = work.tile([P, PASSES + 1, P, 4], BF16, bufs=3, align_bytes=ALIGN)
+                x_i = work.tile([P, PASSES, P, 4], BF16, bufs=3, align_bytes=ALIGN)
                 x_inter[i] = x_i
             cs = passes_of(i, b)
             count = cs.stop - cs.start
@@ -229,10 +249,7 @@ def tile_tubelet_embed_pool_s8_kernel(
             release(("x", i, b))
 
         def quantize_x(i, first, count):
-            if count > PASSES:
-                x_codes[i] = keep.tile([P, count, P], U32, name="ride_codes%d" % i, align_bytes=ALIGN)
-                x_scales[i] = keep.tile([P, count, P], U8, name="ride_scales%d" % i, align_bytes=ALIGN)
-            elif first == 0:
+            if first == 0:
                 codes = work.tile([P, PASSES, P], U32, bufs=XB, align_bytes=ALIGN)
                 scales = work.tile([P, PASSES, P], U8, bufs=XB, align_bytes=ALIGN)
                 x_codes[i] = codes
@@ -251,25 +268,35 @@ def tile_tubelet_embed_pool_s8_kernel(
                 words = pool_raw[:, a].bitcast(F32)[:, 256 * g + u : 256 * (g + 1) : 2]
                 nc.tensor.transpose(pool_turned[:, u, :], words, ident[:])
 
-        def carrier(g, a):
-            return POOL_STEP + 2 + 2 * g + a
-
         def empty_pool(g, a):
-            x_i = work.tile([P, PASSES + 1, P, 4], BF16, bufs=3, align_bytes=ALIGN)
-            x_inter[carrier(g, a)] = x_i
-            nc.scalar.copy(
-                out=x_i[:, PASSES].rearrange("p m t -> p (m t)").bitcast(F32).rearrange("p (m u) -> p m u", u=2),
-                in_=pool_ps[g, a][:].rearrange("p u m -> p m u"),
-            )
+            if a == 0:
+                pool_i = work.tile([P, 2, P, 2], F32, bufs=2, align_bytes=ALIGN)
+                pool_inter[g] = pool_i
+            nc.scalar.copy(out=pool_inter[g][:, a], in_=pool_ps[g, a][:].rearrange("p u m -> p m u"))
             release(("pool", g, a))
 
+        def quantize_pool(g):
+            nc.vector.quantize_mx(
+                out=pool_codes[:, g].rearrange("p a m -> p (a m)").bitcast(F8X4),
+                scales=pool_scales[:, g].rearrange("p a m -> p (a m)"),
+                in_=pool_inter[g][:].rearrange("p a m u -> p (a m u)").bitcast(BF16),
+            )
+
+        def placed_width(i, h):
+            return HALF - GW if h == 1 and i >= SUM_FROM and i % 4 != 2 else HALF
+
+        def add_positions(i):
+            added = work.tile([P, GW], F32, bufs=3, align_bytes=ALIGN)
+            sums[i] = added
+            nc.gpsimd.tensor_tensor(out=added[:], in0=space_rep[:, i % 4], in1=time_rep[:, i // 4], op=ADD)
+
         def place(i, h):
-            placed = next_bank(("term", i, h), [P, HALF])
-            term_ps[i, h] = placed
+            width = placed_width(i, h)
+            term_ps[i, h] = next_bank(("term", i, h), [P, width])
             nc.tensor.matmul(
-                out=placed[:],
+                out=term_ps[i, h][:],
                 lhsT=select[:, i // 4].rearrange("p a b -> p (a b)"),
-                rhs=pos[:, i % 4, h * HALF : (h + 1) * HALF],
+                rhs=pos[:, i % 4, h * HALF : h * HALF + width],
                 start=True,
                 stop=True,
             )
@@ -277,13 +304,21 @@ def tile_tubelet_embed_pool_s8_kernel(
         def scale_term(i, h):
             term_i = work.tile([P, HALF], F32, bufs=TB, align_bytes=ALIGN)
             term[i, h] = term_i
+            cut = placed_width(i, h) // 4
             nc.scalar.activation(
-                out=term_i[:].rearrange("p (u q e) -> p u q e", u=2, e=2),
+                out=term_i[:].rearrange("p (u q e) -> p u q e", u=2, e=2)[:, :, :cut],
                 in_=term_ps[i, h][:].rearrange("p (q u e) -> p u q e", u=2, e=2),
                 func=COPY,
                 scale=gain_col[:, i : i + 1],
             )
             release(("term", i, h))
+            if cut < P:
+                nc.scalar.activation(
+                    out=term_i[:].rearrange("p (u q e) -> p u q e", u=2, e=2)[:, :, cut:],
+                    in_=sums[i][:].rearrange("p (q u e) -> p u q e", u=2, e=2),
+                    func=COPY,
+                    scale=gain_col[:, i : i + 1],
+                )
 
         def embed(i, h, first=0, count=PASSES):
             if first == 0:
@@ -325,25 +360,21 @@ def tile_tubelet_embed_pool_s8_kernel(
                     d0 = t * HALF + 256 * b + 128 * u
                     nc.tensor.transpose(turned[:, b, u, :], words[:, d0 : d0 + 128], ident[:])
 
-        def empty_h(i):
-            if i % 2 == 0:
-                hf_i = work.tile([P, 2, 2, P, 2], F32, bufs=2, align_bytes=ALIGN)
-                hf_inter[i // 2] = hf_i
-            nc.scalar.copy(out=hf_inter[i // 2][:, i % 2], in_=h_ps[i][:].rearrange("p b u m -> p b m u"))
+        def empty_h(i, copy=nc.scalar.copy):
+            hf_i = work.tile([P, 2, P, 2], F32, bufs=3, align_bytes=ALIGN)
+            hf_inter[i] = hf_i
+            copy(out=hf_i[:], in_=h_ps[i][:].rearrange("p b u m -> p b m u"))
             release(("h", i))
 
-        def quantize_features(first, count):
-            j = first // 2
-            if first % 2 == 0:
-                codes_f = work.tile([P, 2, 2, P], U32, bufs=2, align_bytes=ALIGN)
-                scales_f = work.tile([P, 2, 2, P], U8, bufs=2, align_bytes=ALIGN)
-                hf_codes[j] = codes_f
-                hf_scales[j] = scales_f
-            ss = slice(first % 2, first % 2 + count)
+        def quantize_features(i):
+            codes_f = work.tile([P, 2, P], U32, bufs=3, align_bytes=ALIGN)
+            scales_f = work.tile([P, 2, P], U8, bufs=3, align_bytes=ALIGN)
+            hf_codes[i] = codes_f
+            hf_scales[i] = scales_f
             nc.vector.quantize_mx(
-                out=hf_codes[j][:, ss].rearrange("p s b m -> p (s b m)").bitcast(F8X4),
-                scales=hf_scales[j][:, ss].rearrange("p s b m -> p (s b m)"),
-                in_=hf_inter[j][:, ss].rearrange("p s b m u -> p (s b m u)").bitcast(BF16),
+                out=codes_f[:].rearrange("p b m -> p (b m)").bitcast(F8X4),
+                scales=scales_f[:].rearrange("p b m -> p (b m)"),
+                in_=hf_inter[i][:].rearrange("p b m u -> p (b m u)").bitcast(BF16),
             )
 
         def project(i):
@@ -352,8 +383,8 @@ def tile_tubelet_embed_pool_s8_kernel(
             for b in range(2):
                 nc.tensor.matmul_mx(
                     out=projected[:],
-                    lhsT=hf_codes[i // 2][:, i % 2, b].bitcast(F8X4),
-                    lhsT_scale=hf_scales[i // 2][:, i % 2, b],
+                    lhsT=hf_codes[i][:, b].bitcast(F8X4),
+                    lhsT_scale=hf_scales[i][:, b],
                     rhs=proj_w[:, b].bitcast(F4X4),
                     rhs_scale=proj_s[:, b],
                     start=(b == 0),
@@ -394,8 +425,8 @@ def tile_tubelet_embed_pool_s8_kernel(
                 latents_ps[a, d0] = next_bank(("latents", a, d0), [P, width])
             nc.tensor.matmul_mx(
                 out=latents_ps[a, d0][:],
-                lhsT=x_codes[carrier(g, a)][:, PASSES].bitcast(F8X4),
-                lhsT_scale=x_scales[carrier(g, a)][:, PASSES],
+                lhsT=pool_codes[:, g, a].bitcast(F8X4),
+                lhsT_scale=pool_scales[:, g, a],
                 rhs=h_codes[g][:, d0 : d0 + width].bitcast(F8X4),
                 rhs_scale=h_scales[g][:, d0 : d0 + width],
                 start=(g == 0),
@@ -511,40 +542,44 @@ def tile_tubelet_embed_pool_s8_kernel(
             turn_x(i + 1, 0)
             if n >= 0:
                 interleave_h(n, gpsimd_copy)
+            if i + 2 < TILES and placed_width(i + 2, 1) < HALF:
+                add_positions(i + 2)
             finish_h(i - 1, 1)
-            turn_h(i - 3)
+            turn_h(i - LT)
             if 0 <= g < GROUPS:
                 turn_pool(g, phase)
             scale_term(i + 1, 0)
             place(i + 1, 1)
             prepare_x(i + 1)
-            if i + 2 < TILES:
+            if i + 2 < TILES and sorted_passes(i + 2):
                 sort_x(i + 2)
-            empty_h(i - 3)
+            empty_h(i - LT)
             scale_term(i + 1, 1)
             if 0 <= g < GROUPS:
                 empty_pool(g, phase)
-            if i >= 5:
-                project(i - 5)
-                store_features(i - 5)
+            if i >= LP:
+                project(i - LP)
+                store_features(i - LP)
             if i + 3 < TILES:
                 widen_x(i + 3)
             embed(i, 0)
             embed(i, 1)
-            if carrier(0, 0) <= i + 1 <= carrier(GROUPS - 1, 1):
-                if i % 2 == 0:
-                    quantize_features(i - 4, 2)
-                else:
-                    finish_h(i, 0)
-                quantize_x(i + 1, 0, PASSES + 1)
-            else:
+            if HELD_FROM <= i < HELD_FROM + 3:
+                for a in range(HELD):
+                    pool_pass(i - HELD_FROM, a, 0)
+            if i < LQ or i == TILES - 2:
                 quantize_all_x(i + 1)
-                if i % 2 == 0:
-                    quantize_features(i - 4, 2)
+            if i >= LQ:
+                quantize_features(i - LQ)
+            if 1 <= g <= GROUPS and phase == 0:
+                quantize_pool(g - 1)
             if n >= 0:
                 quantize_tokens(n)
-            if i % 2 == 0 or not carrier(0, 0) <= i + 1 <= carrier(GROUPS - 1, 1):
-                finish_h(i, 0)
+            if i == TILES - 2:
+                quantize_features(i - LQ + 1)
+            elif i >= LQ:
+                quantize_x(i + 1, 0, PASSES)
+            finish_h(i, 0)
 
         interleave_h(11, gpsimd_copy)
         turn_h(12)
@@ -560,7 +595,8 @@ def tile_tubelet_embed_pool_s8_kernel(
         finish_h(15, 0)
         finish_h(15, 1)
         store_features(11)
-        quantize_features(12, 2)
+        quantize_features(12)
+        quantize_features(13)
         quantize_tokens(11)
         for g in range(3):
             pool_pass(g, 0, 0)
@@ -578,7 +614,8 @@ def tile_tubelet_embed_pool_s8_kernel(
         quantize_tokens(12)
         quantize_tokens(13)
         store_features(12)
-        quantize_features(14, 2)
+        quantize_features(14)
+        quantize_features(15)
         interleave_h(15, vector)
         store_features(13)
         pool_pass(3, 0, 0)

@@ -30,13 +30,9 @@ SORT_ALL = 14
 POOL_STEP = 4
 POOL_GAP = 2
 GQ = 96
-GW = 256
-SUM_FROM = 6
 LT = 3
 LQ = 4
 LP = 5
-HELD_FROM = 12
-HELD = 0
 TB = 8
 BANKS = 8
 ALIGN = 64
@@ -96,8 +92,6 @@ def tile_tubelet_embed_pool_s8_kernel(
                 w_scales[c, h] = keep.tile([P, HALF], U8, name="w_scales%d%d" % (c, h), align_bytes=ALIGN)
         pool_codes = keep.tile([P, GROUPS, 2, P], U32, align_bytes=ALIGN)
         pool_scales = keep.tile([P, GROUPS, 2, P], U8, align_bytes=ALIGN)
-        space_rep = keep.tile([P, 4, GW], BF16, align_bytes=ALIGN)
-        time_rep = keep.tile([P, GROUPS, GW], BF16, align_bytes=ALIGN)
         h_codes = []
         h_scales = []
         for g in range(GROUPS):
@@ -132,11 +126,6 @@ def tile_tubelet_embed_pool_s8_kernel(
         load_positions(0)
         load_positions(2)
         load_x(4, 2)
-        for f in range(2):
-            half = slice(64 * f, 64 * (f + 1))
-            nc.sync.dma_start(out=space_rep[half], in_=space_pos.rearrange("(k t) d -> k t d", t=4)[:, :, N - GW :])
-            rows = time_pos.rearrange("(g f) d -> f g d", f=2)[f : f + 1, :, N - GW :]
-            nc.sync.dma_start(out=time_rep[half], in_=rows.to_broadcast([64, GROUPS, GW]))
         for q in range(4):
             nc.sync.dma_start(
                 out=proj_s[32 * q : 32 * q + 4].bitcast(I32),
@@ -149,7 +138,6 @@ def tile_tubelet_embed_pool_s8_kernel(
 
         pool_ps = {}
         pool_inter = {}
-        sums = {}
         w_inter = {}
         w_ps = {}
         x_wide = {}
@@ -203,7 +191,7 @@ def tile_tubelet_embed_pool_s8_kernel(
             nc.scalar.copy(out=x_wide[i][:, ks], in_=x_raw[i // 2][:, i % 2, ks].bitcast(F8))
 
         def sorted_passes(i):
-            return 1 + 0 * (i % 2) if i < SORT_ALL else PASSES
+            return 1 + 1 * (i % 2) if i < SORT_ALL else PASSES
 
         def sort_x(i):
             count = sorted_passes(i)
@@ -282,21 +270,12 @@ def tile_tubelet_embed_pool_s8_kernel(
                 in_=pool_inter[g][:].rearrange("p a m u -> p (a m u)").bitcast(BF16),
             )
 
-        def placed_width(i, h):
-            return HALF - GW if h == 1 and i >= SUM_FROM and i % 4 != 2 else HALF
-
-        def add_positions(i):
-            added = work.tile([P, GW], F32, bufs=3, align_bytes=ALIGN)
-            sums[i] = added
-            nc.gpsimd.tensor_tensor(out=added[:], in0=space_rep[:, i % 4], in1=time_rep[:, i // 4], op=ADD)
-
         def place(i, h):
-            width = placed_width(i, h)
-            term_ps[i, h] = next_bank(("term", i, h), [P, width])
+            term_ps[i, h] = next_bank(("term", i, h), [P, HALF])
             nc.tensor.matmul(
                 out=term_ps[i, h][:],
                 lhsT=select[:, i // 4].rearrange("p a b -> p (a b)"),
-                rhs=pos[:, i % 4, h * HALF : h * HALF + width],
+                rhs=pos[:, i % 4, h * HALF : (h + 1) * HALF],
                 start=True,
                 stop=True,
             )
@@ -304,21 +283,13 @@ def tile_tubelet_embed_pool_s8_kernel(
         def scale_term(i, h):
             term_i = work.tile([P, HALF], F32, bufs=TB, align_bytes=ALIGN)
             term[i, h] = term_i
-            cut = placed_width(i, h) // 4
             nc.scalar.activation(
-                out=term_i[:].rearrange("p (u q e) -> p u q e", u=2, e=2)[:, :, :cut],
+                out=term_i[:].rearrange("p (u q e) -> p u q e", u=2, e=2),
                 in_=term_ps[i, h][:].rearrange("p (q u e) -> p u q e", u=2, e=2),
                 func=COPY,
                 scale=gain_col[:, i : i + 1],
             )
             release(("term", i, h))
-            if cut < P:
-                nc.scalar.activation(
-                    out=term_i[:].rearrange("p (u q e) -> p u q e", u=2, e=2)[:, :, cut:],
-                    in_=sums[i][:].rearrange("p (q u e) -> p u q e", u=2, e=2),
-                    func=COPY,
-                    scale=gain_col[:, i : i + 1],
-                )
 
         def embed(i, h, first=0, count=PASSES):
             if first == 0:
@@ -542,8 +513,6 @@ def tile_tubelet_embed_pool_s8_kernel(
             turn_x(i + 1, 0)
             if n >= 0:
                 interleave_h(n, gpsimd_copy)
-            if i + 2 < TILES and placed_width(i + 2, 1) < HALF:
-                add_positions(i + 2)
             finish_h(i - 1, 1)
             turn_h(i - LT)
             if 0 <= g < GROUPS:
@@ -564,9 +533,6 @@ def tile_tubelet_embed_pool_s8_kernel(
                 widen_x(i + 3)
             embed(i, 0)
             embed(i, 1)
-            if HELD_FROM <= i < HELD_FROM + 3:
-                for a in range(HELD):
-                    pool_pass(i - HELD_FROM, a, 0)
             if i < LQ or i == TILES - 2:
                 quantize_all_x(i + 1)
             if i >= LQ:

@@ -62,7 +62,9 @@ def tile_tubelet_embed_pool_s8_kernel(
         ident = keep.tile([P, P], F32, align_bytes=ALIGN)
         make_identity(nc, ident[:])
         pos = keep.tile([P, 4, N], BF16, align_bytes=ALIGN)
-        nc.vector.memset(pos[64:128].rearrange("p t d -> p (t d)").bitcast(F32), 0.0)
+        unused_rows = pos[64:128].rearrange("p t d -> p (t d)").bitcast(F32)
+        nc.vector.memset(unused_rows[:, : N - 1], 0.0)
+        nc.vector.memset(unused_rows[:, N - 1 :], 0.0)
         proj_s = keep.tile([P, 2, R], U8, align_bytes=ALIGN)
         nc.vector.memset(proj_s[:].rearrange("p b n -> p (b n)").bitcast(I32), 0)
         select = keep.tile([P, GROUPS, 2, 64], BF16, align_bytes=ALIGN)

@@ -539,7 +539,7 @@ def tile_tubelet_embed_pool_s8_kernel(
                 quantize_all_x(i + 1)
             if i >= LQ:
                 quantize_features(i - LQ)
-            if 1 <= g <= GROUPS and phase == 0:
+            if 1 <= g <= 2 and phase == 0:
                 quantize_pool(g - 1)
             if n >= 0:
                 quantize_tokens(n)
@@ -563,9 +563,9 @@ def tile_tubelet_embed_pool_s8_kernel(
         finish_h(15, 0)
         finish_h(15, 1)
         store_features(11)
+        quantize_pool(2)
         quantize_features(12)
         quantize_features(13)
-        quantize_tokens(11)
         for g in range(3):
             pool_pass(g, 0, 0)
         turn_h(14)
@@ -580,6 +580,7 @@ def tile_tubelet_embed_pool_s8_kernel(
         for g in range(3):
             pool_pass(g, 1, 0)
         quantize_tokens(12)
+        quantize_pool(3)
         quantize_tokens(13)
         store_features(12)
         quantize_features(14)
@@ -588,6 +589,7 @@ def tile_tubelet_embed_pool_s8_kernel(
         store_features(13)
         pool_pass(3, 0, 0)
         pool_pass(3, 1, 0)
+        quantize_tokens(11)
         quantize_tokens(14)
         quantize_tokens(15)
         project(14)

from contextlib import ExitStack

import concourse.mybir as mybir
from concourse.masks import make_identity

M, T, K, N, R, L = 2048, 8, 1536, 1024, 512, 256
FLOPS = 2 * (M * K * N + M * N * R + L * M * N)

F32 = mybir.dt.float32
BF16 = mybir.dt.bfloat16
I32 = mybir.dt.int32
U32 = mybir.dt.uint32
U8 = mybir.dt.uint8
F8 = mybir.dt.float8_e4m3fn
F8X4 = mybir.dt.float8_e4m3fn_x4
F4X4 = mybir.dt.float4_e2m1fn_x4
COPY = mybir.ActivationFunctionType.Copy
ADD = mybir.AluOpType.add
MULT = mybir.AluOpType.mult

P = 128
PASSES = K // 512
GROUPS = M // 512
TILES = M // P
PAIRS = TILES // 2
HALF = 512
QUARTER = 256
XB = 4
SORT_ALL = 14
POOL_STEP = 4
POOL_GAP = 2
GQ = 96
LT = 3
LQ = 4
LP = 5
TB = 8
BANKS = 8
ALIGN = 64


def tile_tubelet_embed_pool_s8_kernel(
    tc, x_bytes, x_scale, w, time_pos, space_pos, gain, proj_words, proj_scales, pool, out_0, out_1
):
    nc = tc.nc
    with ExitStack() as ctx:
        keep = ctx.enter_context(tc.tile_pool(name="keep", bufs=1))
        work = ctx.enter_context(tc.tile_pool(name="work", bufs=2))
        psum = ctx.enter_context(tc.psum_pool(name="psum", bufs=1))
        ctx.enter_context(tc.manual_schedule())

        free_banks = list(range(BANKS))
        bank_of = {}

        def next_bank(key, shape, dtype=F32):
            bank_of[key] = free_banks[0]
            free_banks.remove(bank_of[key])
            return psum.tile(shape, dtype, name="bank%d" % bank_of[key])

        def release(key):
            free_banks.append(bank_of[key])

        ident = keep.tile([P, P], F32, align_bytes=ALIGN)
        make_identity(nc, ident[:])
        pos = keep.tile([P, 4, N], BF16, align_bytes=ALIGN)
        unused_rows = pos[64:128].rearrange("p t d -> p (t d)").bitcast(F32)
        nc.vector.memset(unused_rows[:, : N - 1], 0.0)
        nc.vector.memset(unused_rows[:, N - 1 :], 0.0)
        proj_s = keep.tile([P, 2, R], U8, align_bytes=ALIGN)
        nc.vector.memset(proj_s[:].rearrange("p b n -> p (b n)").bitcast(I32), 0)
        select = keep.tile([P, GROUPS, 2, 64], BF16, align_bytes=ALIGN)
        for g in range(GROUPS):
            nc.vector.tensor_tensor(
                out=select[:, g],
                in0=ident[:, 0:64].unsqueeze(1).to_broadcast([P, 2, 64]),
                in1=ident[:, 64 + 2 * g : 66 + 2 * g].unsqueeze(2).to_broadcast([P, 2, 64]),
                op=ADD,
            )

        x_raw = []
        for s in range(PAIRS):
            x_raw.append(keep.tile([P, 2, K], U8, name="x_raw%d" % s, align_bytes=ALIGN))
        scale_k = keep.tile([P, PASSES, 4], F32, align_bytes=ALIGN)
        gain_raw = keep.tile([P, GROUPS, 4], BF16)
        gain_col = keep.tile([P, TILES], F32, align_bytes=ALIGN)
        pool_raw = keep.tile([P, 2, M], BF16, align_bytes=ALIGN)
        proj_w = keep.tile([P, 2, 2 * R], U8, align_bytes=ALIGN)
        w_raw = {}
        w_codes = {}
        w_scales = {}
        for h in range(2):
            for c in range(PASSES):
                w_raw[c, h] = keep.tile([P, 4, HALF], BF16, name="w_raw%d%d" % (c, h), align_bytes=ALIGN)
                w_codes[c, h] = keep.tile([P, HALF], U32, name="w_codes%d%d" % (c, h), align_bytes=ALIGN)
                w_scales[c, h] = keep.tile([P, HALF], U8, name="w_scales%d%d" % (c, h), align_bytes=ALIGN)
        pool_codes = keep.tile([P, GROUPS, 2, P], U32, align_bytes=ALIGN)
        pool_scales = keep.tile([P, GROUPS, 2, P], U8, align_bytes=ALIGN)
        h_codes = []
        h_scales = []
        for g in range(GROUPS):
            h_codes.append(keep.tile([P, N], U32, name="h_codes%d" % g, align_bytes=ALIGN))
            h_scales.append(keep.tile([P, N], U8, name="h_scales%d" % g, align_bytes=ALIGN))

        def load_w(c, h):
            rows = w.rearrange("(c p j) n -> c p j n", p=P, j=4)[c]
            nc.sync.dma_start(out=w_raw[c, h][:], in_=rows[:, :, h * HALF : (h + 1) * HALF])

        def load_x(first, count):
            g, t = first // 4, first % 4
            rows = x_bytes.rearrange("(g p t) k -> g p t k", p=P, t=4)[g]
            slot = first % 2
            nc.sync.dma_start(out=x_raw[first // 2][:, slot : slot + count, :], in_=rows[:, t : t + count, :])

        def load_positions(t):
            nc.sync.dma_start(out=pos[64:72, t : t + 2], in_=time_pos.unsqueeze(1).to_broadcast([T, 2, N]))
            nc.sync.dma_start(out=pos[0:64, t : t + 2], in_=space_pos.rearrange("(k t) d -> k t d", t=4)[:, t : t + 2])

        nc.scalar.dma_start(out=scale_k[:], in_=x_scale.rearrange("o (c p t) -> p (o c) t", p=P, t=4))
        load_w(0, 0)
        load_x(0, 1)
        load_w(1, 0)
        load_x(1, 1)
        load_w(2, 0)
        nc.scalar.dma_start(out=gain_raw[:], in_=gain.rearrange("(g p t) -> p g t", p=P, t=4))
        load_w(0, 1)
        load_x(2, 2)
        load_w(1, 1)
        load_w(2, 1)
        load_positions(0)
        load_positions(2)
        load_x(4, 2)
        for q in range(4):
            nc.sync.dma_start(
                out=proj_s[32 * q : 32 * q + 4].bitcast(I32),
                in_=proj_scales[:, 4 * q : 4 * q + 4, :].rearrange("b r n -> r b n").bitcast(I32),
            )
        nc.sync.dma_start(out=proj_w[:].bitcast(I32), in_=proj_words.rearrange("b p n -> p b n").bitcast(I32))
        nc.sync.dma_start(out=pool_raw[:], in_=pool.rearrange("(a p) m -> p a m", p=P))
        for i in range(6, TILES, 2):
            load_x(i, 2)

        pool_ps = {}
        pool_inter = {}
        w_inter = {}
        w_ps = {}
        x_wide = {}
        x_sorted = {}
        x_ps = {}
        x_inter = {}
        x_codes = {}
        x_scales = {}
        term_ps = {}
        term = {}
        e_ps = {}
        h_rows = {}
        h_ps = {}
        hf_inter = {}
        hf_codes = {}
        hf_scales = {}
        feats_ps = {}
        ht_inter = {}
        latents_ps = {}

        def gpsimd_copy(out, in_):
            nc.gpsimd.tensor_scalar(out=out, in0=in_, scalar1=1.0, scalar2=0.0, op0=MULT, op1=ADD)

        def copy_w(c, h, u, copy, qs=slice(0, P)):
            if (c, h, u) in w_inter:
                plane = w_inter[c, h, u]
            elif copy is gpsimd_copy or (c, h, u) == (0, 0, 0):
                plane = work.tile([P, P, 2, 4], BF16, tag="gated", bufs=1, align_bytes=ALIGN)
            else:
                plane = work.tile([P, P, 2, 4], BF16, tag="plane", bufs=5, align_bytes=ALIGN)
            w_inter[c, h, u] = plane
            rows = w_raw[c, h][:].rearrange("p j (q u e) -> p u q e j", u=2, e=2)[:, u, qs]
            if copy is gpsimd_copy:
                copy(out=plane[:, qs], in_=rows)
            else:
                copy(out=plane[:, qs].rearrange("p q e j -> p q j e"), in_=rows.rearrange("p q e j -> p q j e"))

        def quantize_w(c, h, u):
            ns = slice(u * QUARTER, (u + 1) * QUARTER)
            nc.vector.quantize_mx(
                out=w_codes[c, h][:, ns].bitcast(F8X4),
                scales=w_scales[c, h][:, ns],
                in_=w_inter[c, h, u][:].rearrange("p q e j -> p (q e j)"),
            )

        def widen_x(i, first=0, count=PASSES):
            if first == 0:
                wide = work.tile([P, K], BF16, bufs=3, align_bytes=ALIGN)
                x_wide[i] = wide
            ks = slice(512 * first, 512 * (first + count))
            nc.scalar.copy(out=x_wide[i][:, ks], in_=x_raw[i // 2][:, i % 2, ks].bitcast(F8))

        def sorted_passes(i):
            return 1 + 1 * (i % 2) if i < SORT_ALL else PASSES

        def sort_x(i):
            count = sorted_passes(i)
            words = work.tile([P, count, 2, P], F32, bufs=2, align_bytes=ALIGN)
            x_sorted[i] = words
            nc.scalar.copy(
                out=words[:],
                in_=x_wide[i][:].bitcast(F32)[:, : 256 * count].rearrange("p (c q u) -> p c u q", u=2, q=P),
            )

        def passes_of(i, b):
            cut = 1 if i == 0 else 2
            return slice(0, cut) if b == 0 else slice(cut, PASSES)

        def turn_x(i, b, planes=range(2)):
            cs = passes_of(i, b)
            if 0 in planes:
                x_ps[i, b] = next_bank(("x", i, b), [P, 2, cs.stop - cs.start, P])
            x_turned = x_ps[i, b]
            for c in range(cs.stop - 1, cs.start - 1, -1):
                for u in planes:
                    if i in x_sorted and c < sorted_passes(i):
                        words = x_sorted[i][:, c, u]
                    else:
                        words = x_wide[i][:].bitcast(F32)[:, 256 * c + u : 256 * (c + 1) : 2]
                    nc.tensor.transpose(x_turned[:, u, c - cs.start, :], words, ident[:])

        def scale_x(i, b):
            if i not in x_inter:
                x_i = work.tile([P, PASSES, P, 4], BF16, bufs=3, align_bytes=ALIGN)
                x_inter[i] = x_i
            cs = passes_of(i, b)
            count = cs.stop - cs.start
            nc.vector.tensor_tensor(
                out=x_inter[i][:, cs].rearrange("p c m (u e) -> p c m u e", e=2),
                in0=x_ps[i, b][:].bitcast(BF16).rearrange("p u c (m e) -> p c m u e", e=2),
                in1=scale_k[:, cs]
                .rearrange("p c (u e) -> p c u e", e=2)
                .unsqueeze(2)
                .to_broadcast([P, count, P, 2, 2]),
                op=MULT,
            )
            release(("x", i, b))

        def quantize_x(i, first, count):
            if first == 0:
                codes = work.tile([P, PASSES, P], U32, bufs=XB, align_bytes=ALIGN)
                scales = work.tile([P, PASSES, P], U8, bufs=XB, align_bytes=ALIGN)
                x_codes[i] = codes
                x_scales[i] = scales
            cs = slice(first, first + count)
            nc.vector.quantize_mx(
                out=x_codes[i][:, cs].rearrange("p c m -> p (c m)").bitcast(F8X4),
                scales=x_scales[i][:, cs].rearrange("p c m -> p (c m)"),
                in_=x_inter[i][:, cs].rearrange("p c m t -> p (c m t)"),
            )

        def turn_pool(g, a):
            pool_turned = next_bank(("pool", g, a), [P, 2, P])
            pool_ps[g, a] = pool_turned
            for u in range(2):
                words = pool_raw[:, a].bitcast(F32)[:, 256 * g + u : 256 * (g + 1) : 2]
                nc.tensor.transpose(pool_turned[:, u, :], words, ident[:])

        def empty_pool(g, a):
            if a == 0:
                pool_i = work.tile([P, 2, P, 2], F32, bufs=2, align_bytes=ALIGN)
                pool_inter[g] = pool_i
            nc.scalar.copy(out=pool_inter[g][:, a], in_=pool_ps[g, a][:].rearrange("p u m -> p m u"))
            release(("pool", g, a))

        def quantize_pool(g):
            nc.vector.quantize_mx(
                out=pool_codes[:, g].rearrange("p a m -> p (a m)").bitcast(F8X4),
                scales=pool_scales[:, g].rearrange("p a m -> p (a m)"),
                in_=pool_inter[g][:].rearrange("p a m u -> p (a m u)").bitcast(BF16),
            )

        def place(i, h):
            term_ps[i, h] = next_bank(("term", i, h), [P, HALF])
            nc.tensor.matmul(
                out=term_ps[i, h][:],
                lhsT=select[:, i // 4].rearrange("p a b -> p (a b)"),
                rhs=pos[:, i % 4, h * HALF : (h + 1) * HALF],
                start=True,
                stop=True,
            )

        def scale_term(i, h):
            term_i = work.tile([P, HALF], F32, bufs=TB, align_bytes=ALIGN)
            term[i, h] = term_i
            nc.scalar.activation(
                out=term_i[:].rearrange("p (u q e) -> p u q e", u=2, e=2),
                in_=term_ps[i, h][:].rearrange("p (q u e) -> p u q e", u=2, e=2),
                func=COPY,
                scale=gain_col[:, i : i + 1],
            )
            release(("term", i, h))

        def embed(i, h, first=0, count=PASSES):
            if first == 0:
                e_ps[i, h] = next_bank(("e", i, h), [P, HALF])
            acc = e_ps[i, h]
            for c in range(first, first + count):
                nc.tensor.matmul_mx(
                    out=acc[:],
                    lhsT=x_codes[i][:, c].bitcast(F8X4),
                    lhsT_scale=x_scales[i][:, c],
                    rhs=w_codes[c, h][:].bitcast(F8X4),
                    rhs_scale=w_scales[c, h][:],
                    start=(c == 0),
                    stop=(c == PASSES - 1),
                )

        def finish_h(i, h):
            g, t = i // 4, i % 4
            if t == 0 and h == 0:
                rows = work.tile([P, 4, N], BF16, bufs=2, align_bytes=ALIGN)
                h_rows[g] = rows
            nc.vector.scalar_tensor_tensor(
                out=h_rows[g][:, t, h * HALF : (h + 1) * HALF],
                in0=e_ps[i, h][:],
                scalar=gain_col[:, i : i + 1],
                in1=term[i, h][:],
                op0=MULT,
                op1=ADD,
            )
            release(("e", i, h))

        def turn_h(i):
            g, t = i // 4, i % 4
            words = h_rows[g][:].rearrange("p t d -> p (t d)").bitcast(F32)
            turned = next_bank(("h", i), [P, 2, 2, P])
            h_ps[i] = turned
            for b in range(2):
                for u in range(2):
                    d0 = t * HALF + 256 * b + 128 * u
                    nc.tensor.transpose(turned[:, b, u, :], words[:, d0 : d0 + 128], ident[:])

        def empty_h(i, copy=nc.scalar.copy):
            hf_i = work.tile([P, 2, P, 2], F32, bufs=3, align_bytes=ALIGN)
            hf_inter[i] = hf_i
            copy(out=hf_i[:], in_=h_ps[i][:].rearrange("p b u m -> p b m u"))
            release(("h", i))

        def quantize_features(i):
            codes_f = work.tile([P, 2, P], U32, bufs=3, align_bytes=ALIGN)
            scales_f = work.tile([P, 2, P], U8, bufs=3, align_bytes=ALIGN)
            hf_codes[i] = codes_f
            hf_scales[i] = scales_f
            nc.vector.quantize_mx(
                out=codes_f[:].rearrange("p b m -> p (b m)").bitcast(F8X4),
                scales=scales_f[:].rearrange("p b m -> p (b m)"),
                in_=hf_inter[i][:].rearrange("p b m u -> p (b m u)").bitcast(BF16),
            )

        def project(i):
            projected = next_bank(("feats", i), [P, R])
            feats_ps[i] = projected
            for b in range(2):
                nc.tensor.matmul_mx(
                    out=projected[:],
                    lhsT=hf_codes[i][:, b].bitcast(F8X4),
                    lhsT_scale=hf_scales[i][:, b],
                    rhs=proj_w[:, b].bitcast(F4X4),
                    rhs_scale=proj_s[:, b],
                    start=(b == 0),
                    stop=(b == 1),
                )

        def store_features(i, copy=nc.scalar.copy):
            feats = work.tile([P, R], F32, bufs=6, align_bytes=ALIGN)
            copy(out=feats[:], in_=feats_ps[i][:])
            release(("feats", i))
            nc.sync.dma_start(out=out_0.rearrange("(g p t) r -> g t p r", p=P, t=4)[i // 4, i % 4], in_=feats[:])

        def interleave_h(n, copy):
            g, d0 = n // 4, QUARTER * (n % 4)
            if copy is gpsimd_copy:
                ht_i = work.tile([P, QUARTER, 4], BF16, tag="gated", bufs=1, align_bytes=ALIGN)
            else:
                ht_i = work.tile([P, QUARTER, 4], BF16, tag="plane", bufs=5, align_bytes=ALIGN)
            ht_inter[n] = ht_i
            if copy is gpsimd_copy:
                copy(out=ht_i[:], in_=h_rows[g][:, :, d0 : d0 + QUARTER].rearrange("p t d -> p d t"))
            else:
                copy(
                    out=ht_i[:].rearrange("p (n i) t -> p n t i", i=4),
                    in_=h_rows[g][:, :, d0 : d0 + QUARTER].rearrange("p t (n i) -> p n t i", i=4),
                )

        def quantize_tokens(n):
            g, d0 = n // 4, QUARTER * (n % 4)
            nc.vector.quantize_mx(
                out=h_codes[g][:, d0 : d0 + QUARTER].bitcast(F8X4),
                scales=h_scales[g][:, d0 : d0 + QUARTER],
                in_=ht_inter[n][:].rearrange("p d t -> p (d t)"),
            )

        def pool_pass(g, a, d0, width=HALF):
            if g == 0:
                latents_ps[a, d0] = next_bank(("latents", a, d0), [P, width])
            nc.tensor.matmul_mx(
                out=latents_ps[a, d0][:],
                lhsT=pool_codes[:, g, a].bitcast(F8X4),
                lhsT_scale=pool_scales[:, g, a],
                rhs=h_codes[g][:, d0 : d0 + width].bitcast(F8X4),
                rhs_scale=h_scales[g][:, d0 : d0 + width],
                start=(g == 0),
                stop=(g == GROUPS - 1),
            )

        def store_latents(a, h, copy):
            lat = work.tile([P, HALF], F32, tag="feats", bufs=6, align_bytes=ALIGN)
            copy(
                out=lat[:].rearrange("p (q u e) -> p q u e", u=2, e=2),
                in_=latents_ps[a, h * HALF][:].rearrange("p (u q e) -> p q u e", u=2, e=2),
            )
            release(("latents", a, h * HALF))
            nc.sync.dma_start(out=out_1[a * P : (a + 1) * P, h * HALF : (h + 1) * HALF], in_=lat[:])

        scalar, vector = nc.scalar.copy, nc.vector.tensor_copy

        def prepare_x(i):
            for b in range(2):
                scale_x(i, b)

        def quantize_all_x(i):
            quantize_x(i, 0, 2)
            quantize_x(i, 2, 1)

        copy_w(0, 0, 0, vector)
        copy_w(0, 0, 1, vector)
        widen_x(0, 0, 1)
        turn_x(0, 0)
        widen_x(0, 1, 2)
        turn_x(0, 1)
        quantize_w(0, 0, 0)
        quantize_w(0, 0, 1)
        copy_w(1, 0, 0, gpsimd_copy)
        copy_w(1, 0, 1, scalar)
        prepare_x(0)
        widen_x(1)
        turn_x(1, 0)
        turn_x(1, 1)
        copy_w(2, 0, 0, scalar)
        copy_w(2, 0, 1, vector)
        quantize_all_x(0)
        quantize_w(1, 0, 1)
        quantize_w(2, 0, 0)
        quantize_w(2, 0, 1)
        quantize_w(1, 0, 0)
        embed(0, 0)
        copy_w(0, 1, 0, gpsimd_copy, slice(0, GQ))
        copy_w(0, 1, 1, scalar)
        prepare_x(1)
        widen_x(2)
        turn_x(2, 0)
        turn_x(2, 1)
        copy_w(1, 1, 0, scalar)
        widen_x(3)
        copy_w(1, 1, 1, scalar)
        nc.vector.tensor_copy(out=gain_col[:], in_=gain_raw[:].rearrange("p g t -> p (g t)"))
        copy_w(0, 1, 0, vector, slice(GQ, P))
        quantize_all_x(1)
        quantize_w(0, 1, 1)
        quantize_w(1, 1, 0)
        quantize_w(0, 1, 0)
        embed(1, 0)
        turn_x(3, 0)
        turn_x(3, 1)
        copy_w(2, 1, 1, gpsimd_copy, slice(0, GQ))
        embed(0, 1, 0, 1)
        embed(1, 1, 0, 1)
        copy_w(2, 1, 0, scalar)
        prepare_x(2)
        place(0, 0)
        place(1, 0)
        scale_term(0, 0)
        scale_term(1, 0)
        copy_w(2, 1, 1, vector, slice(GQ, P))
        quantize_w(1, 1, 1)
        quantize_all_x(2)
        quantize_w(2, 1, 0)
        quantize_w(2, 1, 1)
        finish_h(0, 0)
        finish_h(1, 0)
        embed(0, 1, 1, 1)
        embed(1, 1, 1, 1)
        place(0, 1)
        embed(0, 1, 2, 1)
        embed(1, 1, 2, 1)
        place(1, 1)
        scale_term(0, 1)
        scale_term(1, 1)
        widen_x(4)
        embed(2, 0)
        place(2, 0)
        prepare_x(3)
        place(2, 1)
        scale_term(2, 0)
        finish_h(0, 1)
        quantize_all_x(3)
        scale_term(2, 1)
        embed(2, 1)
        place(3, 0)
        place(3, 1)
        finish_h(1, 1)
        scale_term(3, 0)
        scale_term(3, 1)
        widen_x(5)
        finish_h(2, 0)

        for i in range(3, TILES - 1):
            n = i - 4
            g, phase = divmod(i - POOL_STEP, POOL_GAP)
            place(i + 1, 0)
            turn_x(i + 1, 1)
            turn_x(i + 1, 0)
            if n >= 0:
                interleave_h(n, gpsimd_copy)
            finish_h(i - 1, 1)
            turn_h(i - LT)
            if 0 <= g < GROUPS:
                turn_pool(g, phase)
            scale_term(i + 1, 0)
            place(i + 1, 1)
            prepare_x(i + 1)
            if i + 2 < TILES and sorted_passes(i + 2):
                sort_x(i + 2)
            empty_h(i - LT)
            scale_term(i + 1, 1)
            if 0 <= g < GROUPS:
                empty_pool(g, phase)
            if i >= LP:
                project(i - LP)
                store_features(i - LP)
            if i + 3 < TILES:
                widen_x(i + 3)
            embed(i, 0)
            embed(i, 1)
            if i < LQ or i == TILES - 2:
                quantize_all_x(i + 1)
            if i >= LQ:
                quantize_features(i - LQ)
            if 1 <= g <= 2 and phase == 0:
                quantize_pool(g - 1)
            if n >= 0:
                quantize_tokens(n)
            if i == TILES - 2:
                quantize_features(i - LQ + 1)
            elif i >= LQ:
                quantize_x(i + 1, 0, PASSES)
            finish_h(i, 0)

        interleave_h(11, gpsimd_copy)
        turn_h(12)
        turn_h(13)
        finish_h(14, 1)
        empty_h(12)
        empty_h(13)
        embed(15, 0)
        embed(15, 1)
        project(10)
        project(11)
        store_features(10)
        finish_h(15, 0)
        finish_h(15, 1)
        store_features(11)
        quantize_pool(2)
        quantize_features(12)
        quantize_features(13)
        for g in range(3):
            pool_pass(g, 0, 0)
        turn_h(14)
        turn_h(15)
        interleave_h(13, scalar)
        interleave_h(12, vector)
        project(12)
        project(13)
        empty_h(14)
        empty_h(15)
        interleave_h(14, vector)
        for g in range(3):
            pool_pass(g, 1, 0)
        quantize_tokens(12)
        quantize_pool(3)
        quantize_tokens(13)
        store_features(12)
        quantize_features(14)
        quantize_features(15)
        interleave_h(15, vector)
        store_features(13)
        pool_pass(3, 0, 0)
        pool_pass(3, 1, 0)
        quantize_tokens(11)
        quantize_tokens(14)
        quantize_tokens(15)
        project(14)
        project(15)
        store_latents(0, 0, scalar)
        store_latents(1, 0, vector)
        store_features(14, scalar)
        for a in range(2):
            for g in range(4):
                pool_pass(g, a, HALF)
        store_features(15, vector)
        store_latents(0, 1, scalar)
        store_latents(1, 1, vector)
